import numpy as np
import ml_dtypes


def mxq(x, axis, fmt="e4m3"):
    dtype, down = {"e4m3": (ml_dtypes.float8_e4m3fn, 7), "e5m2": (ml_dtypes.float8_e5m2, 14)}[fmt]
    v = np.moveaxis(np.asarray(x, np.float32).astype(ml_dtypes.bfloat16).astype(np.float64), axis, -1)
    blocks = v.reshape(v.shape[:-1] + (-1, 32))
    amax = np.abs(blocks).max(-1, keepdims=True)
    byte = np.maximum(np.where(amax > 0, np.frexp(amax)[1] - 1 + 127, 0) - down, 1)
    scale = np.exp2(byte - 127.0)
    codes = (blocks / scale).astype(np.float32).astype(dtype).astype(np.float64)
    return np.moveaxis((codes * scale).reshape(v.shape), -1, axis)


WIDE = False


def mx_kscale(k):
    if not WIDE:
        return np.ones(k)
    levels = np.array([10, -10, 5, -5, 0])
    if k % 512:
        return np.exp2(np.random.permutation(np.resize(levels, k // 32))).repeat(32)
    a = np.empty((k // 512, 16))
    for p in range(k // 512):
        a[p, :8] = np.random.permutation(np.resize(levels, 8))
        for g in range(8):
            far = levels[np.abs(levels - a[p, g]) >= 10]
            a[p, g + 8] = far[np.random.randint(len(far))]
    return np.exp2(a.ravel()).repeat(32)


def f64(x):
    return np.asarray(x).astype(np.float64)


def striped(idx):
    return np.tile(idx.reshape(-1, 16).T, (8, 1)).astype(np.uint16)


def unstriped(offs):
    return offs[:16].T.reshape(-1).astype(np.int64)


E2M1 = np.array([0.0, 0.5, 1.0, 1.5, 2.0, 3.0, 4.0, 6.0, -0.0, -0.5, -1.0, -1.5, -2.0, -3.0, -4.0, -6.0])


def pack_weight(w, fmt):
    k, n = w.shape
    w = f64(np.asarray(w, np.float32).astype(ml_dtypes.bfloat16)).reshape(k // 32, 32, n)
    amax = np.abs(w).max(1)
    if fmt == "e4m3":
        byte = np.frexp(amax)[1] - 1 + 127 - 7
    else:
        mant, ex = np.frexp(amax / 6.0)
        byte = np.where(mant > 0.5, ex, ex - 1) + 127
    byte = np.clip(np.where(amax > 0, byte, 1), 1, 254)
    scaled = (w * np.exp2(127.0 - byte)[:, None, :]).reshape(k, n).astype(np.float32)
    by_word = np.ascontiguousarray(scaled.reshape(k // 512, 128, 4, n).transpose(0, 1, 3, 2))
    if fmt == "e4m3":
        words = by_word.astype(ml_dtypes.float8_e4m3fn).view(np.uint8)
    else:
        c = by_word.astype(ml_dtypes.float4_e2m1fn).view(np.uint8) & 0xF
        words = (c[..., 0::2] | (c[..., 1::2] << 4)).reshape(k // 512, 128, 2 * n)
    return np.ascontiguousarray(words), np.ascontiguousarray(byte.astype(np.uint8).reshape(k // 512, 16, n))


def unpack_weight(words, scales, fmt):
    g, _, n = scales.shape
    words = np.ascontiguousarray(words).reshape(g, 128, n, -1)
    if fmt == "e4m3":
        vals = words.view(ml_dtypes.float8_e4m3fn).astype(np.float64)
    else:
        nib = np.empty((g, 128, n, 4), np.uint8)
        nib[..., 0::2] = words & 0xF
        nib[..., 1::2] = words >> 4
        vals = E2M1[nib]
    vals = vals * np.repeat(np.exp2(scales.astype(np.float64) - 127.0), 8, axis=1)[..., None]
    return vals.transpose(0, 1, 3, 2).reshape(g * 512, n)


def gelu(v):
    return 0.5 * v * (1.0 + np.tanh(np.sqrt(2.0 / np.pi) * (v + 0.044715 * v**3)))


K, H, N, T, S = 1024, 1024, 384, 2048, 1024


def setup_inputs():
    n = np.random.standard_normal
    s = mx_kscale(K)[:, None]
    u = mx_kscale(H)[:, None]
    tab_words, tab_scales = pack_weight(n((K, T)) * s, "e4m3")
    w4_words, w4_scales = pack_weight(n((K, H)) / np.sqrt(K) / s, "e2m1")
    return {
        "tab_words": tab_words, "tab_scales": tab_scales,
        "offs": striped(np.random.permutation(T)[:S]),
        "w1": (n((K, H)) / np.sqrt(K) / s * u.T).astype(np.float32),
        "ba": (0.7 * n(H) * u[:, 0]).astype(np.float32),
        "w4_words": w4_words, "w4_scales": w4_scales,
        "w3": (n((H, N)) / np.sqrt(H) / u).astype(np.float32),
        "offs2": striped(np.random.permutation(S)),
        "wgo": np.exp(0.3 * n((128, S))).astype(np.float32),
        "gn": np.exp(0.3 * n(N)).astype(np.float32),
        "x0": n((N, S)).astype(np.float32),
    }


def reference(tab_words, tab_scales, offs, w1, ba, w4_words, w4_scales, w3, offs2, wgo, gn, x0):
    v = unpack_weight(tab_words, tab_scales, "e4m3")[:, unstriped(offs)]
    w4 = unpack_weight(w4_words, w4_scales, "e2m1")
    a = (mxq(f64(w1), 0, "e4m3").T @ v) + f64(ba)[:, None]
    b = w4.T @ v
    h = a * b
    y = mxq(f64(w3), 0, "e4m3").T @ mxq(h, 0, "e4m3")
    page = np.zeros((N, S))
    page[:, unstriped(offs2)] = np.tile(f64(wgo), (N // 128, 1)) * y
    return f64(gn)[:, None] * page + f64(x0)

@@ -1,0 +1,392 @@
+from contextlib import ExitStack
+
+import concourse.mybir as mybir
+from concourse.masks import make_identity
+
+K, H, N, T, S = 1024, 1024, 384, 2048, 1024
+FLOPS = 2 * K * H * S * 2 + 2 * H * N * S
+
+F32 = mybir.dt.float32
+BF16 = mybir.dt.bfloat16
+I32 = mybir.dt.int32
+U32 = mybir.dt.uint32
+U16 = mybir.dt.uint16
+U8 = mybir.dt.uint8
+FP8X4 = mybir.dt.float8_e4m3fn_x4
+FP4X4 = mybir.dt.float4_e2m1fn_x4
+MULT = mybir.AluOpType.mult
+ADD = mybir.AluOpType.add
+IDENT = mybir.ActivationFunctionType.Identity
+COPY = mybir.ActivationFunctionType.Copy
+
+P = 128
+PASS = 512
+HALF = 512
+CHUNK = 128
+
+
+def tile_list_bridge_order_forces_kernel(
+    tc, tab_words, tab_scales, offs, w1, ba, w4_words, w4_scales, w3, offs2, wgo, gn, x0, out
+):
+    nc = tc.nc
+    with ExitStack() as ctx:
+        keep = ctx.enter_context(tc.tile_pool(name="keep", bufs=1))
+        ring = ctx.enter_context(tc.tile_pool(name="ring", bufs=2))
+        psum = ctx.enter_context(tc.psum_pool(name="psum", bufs=1))
+
+        def held(shape, dtype, name):
+            return keep.tile(shape, dtype, name=name, align_bytes=64)
+
+        def slot(shape, dtype, tag):
+            return keep.tile(shape, dtype, name=tag, align_bytes=64)
+
+        idx = keep.tile([P, S // 16], U16, name="idx")
+        nc.sync.dma_start(idx[:], offs)
+
+        tab_s_rows = slot([P, T // 4], I32, "slot_a")
+        for q in range(4):
+            nc.sync.dma_start(
+                out=tab_s_rows[32 * q : 32 * q + 8, :],
+                in_=tab_scales[:, 4 * q : 4 * q + 4, :].bitcast(I32),
+            )
+        tab_s = slot([P, T], U8, "slot_b")
+        nc.vector.memset(tab_s[:].bitcast(I32), 0)
+        w4s_raw = held([P, 2, H], U8, "w4s_raw")
+        nc.vector.memset(w4s_raw[:].rearrange("p a c -> p (a c)").bitcast(I32), 0)
+        ba_rows = slot([2, PASS], F32, "slot_e")
+        nc.sync.dma_start(out=ba_rows[:], in_=ba.rearrange("(b c) -> b c", b=2))
+        gn_rows = slot([3, P], F32, "slot_f")
+        nc.sync.dma_start(out=gn_rows[:], in_=gn.rearrange("(c p) -> c p", p=P))
+        ident = held([P, P], F32, "ident")
+        make_identity(nc, ident[:])
+        rows = held([P, 5, P], F32, "rows")
+        nc.gpsimd.memset(rows[:], 0.0)
+        nc.scalar.copy(
+            out=rows[0:2, 0:4, :].rearrange("b t (g i) -> b t g i", i=4),
+            in_=ba_rows[:].rearrange("b (g t i) -> b t g i", t=4, i=4),
+        )
+        nc.scalar.copy(out=rows[0:3, 4, :], in_=gn_rows[:])
+
+        w1_raw = {}
+        w4_raw = {}
+        tab_w = {}
+        w3_raw = {}
+        x0_sb = {}
+
+        def load_w1(a, b, tag):
+            w1_raw[a, b] = slot([P, 4, PASS], F32, tag)
+            nc.sync.dma_start(
+                out=w1_raw[a, b][:],
+                in_=w1[PASS * a : PASS * (a + 1), PASS * b : PASS * (b + 1)].rearrange("(p j) c -> p j c", j=4),
+            )
+
+        def load_w4(b, tag):
+            w4_raw[b] = slot([P, 2, 256], I32, tag)
+            nc.sync.dma_start(
+                out=w4_raw[b][:],
+                in_=w4_words[:, :, 1024 * b : 1024 * (b + 1)].rearrange("a p c -> p a c").bitcast(I32),
+            )
+
+        def load_tab(a, tag):
+            tab_w[a] = slot([P, T], U32, tag)
+            nc.sync.dma_start(
+                out=tab_w[a][:].bitcast(I32),
+                in_=tab_words[a].rearrange("p t i -> p (t i)").bitcast(I32),
+            )
+
+        def load_w3(b, tag):
+            w3_raw[b] = slot([P, 4, N], F32, tag)
+            for t in range(4):
+                nc.sync.dma_start(
+                    out=w3_raw[b][:, t, :],
+                    in_=w3[PASS * b : PASS * (b + 1), :].rearrange("(g t i) n -> t g i n", t=4, i=4)[t],
+                )
+
+        def load_x0(n, tag):
+            x0_sb[n] = slot([P, S], F32, tag)
+            nc.sync.dma_start(out=x0_sb[n][:], in_=x0[P * n : P * (n + 1), :])
+
+        load_tab(0, "slot_c")
+        load_tab(1, "slot_d")
+        load_w4(0, "slot_g")
+        idx2 = keep.tile([P, S // 16], U16, name="idx2")
+        nc.sync.dma_start(idx2[:], offs2)
+        for q in range(4):
+            nc.sync.dma_start(
+                out=w4s_raw[32 * q : 32 * q + 4, :, :].bitcast(I32),
+                in_=w4_scales[:, 4 * q : 4 * q + 4, :].rearrange("a r c -> r a c").bitcast(I32),
+            )
+        load_w1(0, 0, "slot_e")
+        load_w1(1, 0, "slot_f")
+
+        w1_bf = {}
+        w1_c = {}
+        w1_s = {}
+
+        def cast_w1(copy, a, b, t0, t1):
+            if (a, b) not in w1_bf:
+                w1_bf[a, b] = ring.tile([P, 4 * PASS], BF16, name="w1_bf", align_bytes=64)
+            copy(
+                out=w1_bf[a, b][:, PASS * t0 : PASS * t1].rearrange("p (t g i j) -> p t g j i", t=t1 - t0, i=4, j=4),
+                in_=w1_raw[a, b][:].rearrange("p j (g t i) -> p t g j i", t=4, i=4)[:, t0:t1],
+            )
+
+        def quant_w1(a, b, t0, t1):
+            if (a, b) not in w1_c:
+                w1_c[a, b] = held([P, PASS], U32, "w1_c%d%d" % (a, b))
+                w1_s[a, b] = held([P, PASS], U8, "w1_s%d%d" % (a, b))
+            nc.vector.quantize_mx(
+                out=w1_c[a, b][:, P * t0 : P * t1].bitcast(FP8X4),
+                scales=w1_s[a, b][:, P * t0 : P * t1],
+                in_=w1_bf[a, b][:, PASS * t0 : PASS * t1],
+            )
+
+        w4_c = {}
+
+        def order_w4(b):
+            w4_c[b] = held([P, 2, 1024], U8, "w4_c%d" % b)
+            nc.vector.tensor_copy(
+                out=w4_c[b][:].bitcast(I32).rearrange("p a (t g e) -> p a g t e", t=4, e=2),
+                in_=w4_raw[b][:].rearrange("p a (g t e) -> p a g t e", t=4, e=2),
+            )
+
+        v_w = {}
+
+        def gather_words(a, h):
+            v_w[a, h] = held([P, HALF], U32, "v_w%d%d" % (a, h))
+            nc.vector.tensor_copy(v_w[a, h][:], tab_w[a][:].indirect(idx[:, 32 * h : 32 * (h + 1)]))
+
+        a_sb = {}
+
+        def product_a(b, h, c0, c1, tag):
+            width = CHUNK * (c1 - c0)
+            tile = slot([P, 4, width], F32, tag)
+            for c in range(c0, c1):
+                a_sb[b, h, c] = tile[:, :, CHUNK * (c - c0) : CHUNK * (c - c0 + 1)]
+            local = slice(CHUNK * c0, CHUNK * c1)
+            cols = slice(HALF * h + CHUNK * c0, HALF * h + CHUNK * c1)
+            for t in range(4):
+                acc = psum.tile([P, width], F32, name="acc_a", bufs=3)
+                for a in range(2):
+                    nc.tensor.matmul_mx(
+                        out=acc[:],
+                        lhsT=w1_c[a, b][:, P * t : P * (t + 1)].bitcast(FP8X4),
+                        lhsT_scale=w1_s[a, b][:, P * t : P * (t + 1)],
+                        rhs=v_w[a, h][:, local].bitcast(FP8X4),
+                        rhs_scale=v_s[4 * a : P, cols],
+                        start=(a == 0),
+                        stop=(a == 1),
+                    )
+                nc.scalar.activation(out=tile[:, t, :], in_=acc[:], func=IDENT, bias=bias[:, t, b : b + 1])
+
+        h_bf = {}
+        b_acc = {}
+
+        def product_b(b, h, c):
+            acc = psum.tile([P, 4, CHUNK], F32, name="acc_b", bufs=4)
+            b_acc[b, h, c] = acc
+            local = slice(CHUNK * c, CHUNK * (c + 1))
+            cols = slice(HALF * h + CHUNK * c, HALF * h + CHUNK * (c + 1))
+            for t in range(4):
+                for a in range(2):
+                    nc.tensor.matmul_mx(
+                        out=acc[:, t, :],
+                        lhsT=w4_c[b][:, a, 256 * t : 256 * (t + 1)].bitcast(FP4X4),
+                        lhsT_scale=w4_s[:, a, PASS * b + P * t : PASS * b + P * (t + 1)],
+                        rhs=v_w[a, h][:, local].bitcast(FP8X4),
+                        rhs_scale=(v_s, v_s1)[a][:, cols],
+                        start=(a == 0),
+                        stop=(a == 1),
+                    )
+
+        def product_h(b, h, c):
+            nc.vector.tensor_tensor(
+                out=h_bf[b, h][:, 4 * CHUNK * c : 4 * CHUNK * (c + 1)].rearrange("p (c i t) -> p c t i", i=4, t=4),
+                in0=b_acc[b, h, c][:].rearrange("p t (c i) -> p c t i", i=4),
+                in1=a_sb[b, h, c].rearrange("p t (c i) -> p c t i", i=4),
+                op=MULT,
+            )
+
+        def step(b, h, c):
+            product_h(b, h, c)
+            nxt = 2 * h + b + 1
+            if nxt < 4:
+                product_b(nxt % 2, nxt // 2, c)
+
+        h_c = {}
+        h_s = {}
+
+        def quant_h(b, h):
+            h_c[b, h] = held([P, HALF], U32, "h_c%d%d" % (b, h))
+            h_s[b, h] = held([P, HALF], U8, "h_s%d%d" % (b, h))
+            nc.vector.quantize_mx(out=h_c[b, h][:].bitcast(FP8X4), scales=h_s[b, h][:], in_=h_bf[b, h][:])
+
+        w3_bf = {}
+        w3_c = {}
+        w3_s = {}
+
+        def cast_w3(copy, n):
+            w3_bf[n] = held([P, 2 * 4 * P], BF16, "w3_bf%d" % n)
+            for b in range(2):
+                copy(
+                    out=w3_bf[n][:, 4 * P * b : 4 * P * (b + 1)].rearrange("p (c i t) -> p c t i", i=4, t=4),
+                    in_=w3_raw[b][:, :, P * n : P * (n + 1)].rearrange("p t (c i) -> p c t i", i=4),
+                )
+
+        def quant_w3(n):
+            w3_c[n] = held([P, 2 * P], U32, "w3_c%d" % n)
+            w3_s[n] = held([P, 2 * P], U8, "w3_s%d" % n)
+            nc.vector.quantize_mx(out=w3_c[n][:].bitcast(FP8X4), scales=w3_s[n][:], in_=w3_bf[n][:])
+
+        y_sb = {}
+
+        def product_y(n, h, tag):
+            acc = psum.tile([P, HALF], F32, name="acc_y", bufs=1)
+            for b in range(2):
+                nc.tensor.matmul_mx(
+                    out=acc[:],
+                    lhsT=w3_c[n][:, P * b : P * (b + 1)].bitcast(FP8X4),
+                    lhsT_scale=w3_s[n][:, P * b : P * (b + 1)],
+                    rhs=h_c[b, h][:].bitcast(FP8X4),
+                    rhs_scale=h_s[b, h][:],
+                    start=(b == 0),
+                    stop=(b == 1),
+                )
+            y_sb[n, h] = slot([P, HALF], F32, tag)
+            nc.scalar.activation(out=y_sb[n, h][:], in_=acc[:], func=COPY, scale=gain[:, n : n + 1])
+
+        page = {}
+
+        def scatter(n, h):
+            if n not in page:
+                page[n] = slot([P, S], F32, ("page0", "page1", "y_3")[n])
+            nc.vector.tensor_tensor(
+                page[n][:].indirect(idx2[:, 32 * h : 32 * (h + 1)]),
+                y_sb[n, h][:],
+                wgo_sb[:, HALF * h : HALF * (h + 1)],
+                MULT,
+            )
+
+        def finish(n, pieces):
+            width = S // pieces
+            for k in range(pieces):
+                cols = slice(width * k, width * (k + 1))
+                nc.vector.tensor_tensor(out=x0_sb[n][:, cols], in0=page[n][:, cols], in1=x0_sb[n][:, cols], op=ADD)
+                nc.sync.dma_start(out=out[P * n : P * (n + 1), cols], in_=x0_sb[n][:, cols])
+
+        def finish_on_tensor(n):
+            for k in range(2):
+                total = psum.tile([P, 4, P], F32, name="acc_b", bufs=4)
+                for c in range(4):
+                    cols = slice(HALF * k + P * c, HALF * k + P * (c + 1))
+                    nc.tensor.matmul(total[:, c, :], x0_sb[n][:, cols], ident[:], start=True, stop=False, is_transpose=True)
+                    nc.tensor.matmul(total[:, c, :], page[n][:, cols], ident[:], start=False, stop=True, is_transpose=True)
+                total_sb = ring.tile([P, 4, P], F32, name="total_sb", bufs=4, align_bytes=64)
+                nc.scalar.copy(out=total_sb[:], in_=total[:])
+                back = psum.tile([P, 4, P], F32, name="acc_b", bufs=4)
+                for c in range(4):
+                    nc.tensor.transpose(back[:, c, :], total_sb[:, c, :], ident[:])
+                back_sb = ring.tile([P, HALF], F32, name="back_sb", bufs=4, align_bytes=64)
+                nc.scalar.copy(out=back_sb[:], in_=back[:].rearrange("p c m -> p (c m)"))
+                nc.scalar.dma_start(out=out[P * n : P * (n + 1), HALF * k : HALF * (k + 1)], in_=back_sb[:])
+
+        v_s1 = held([P, S], U8, "v_s1")
+        nc.vector.memset(v_s1[:].bitcast(I32), 0)
+        for q in range(4):
+            nc.vector.tensor_copy(out=tab_s[32 * q : 32 * q + 8, :].bitcast(I32), in_=tab_s_rows[32 * q : 32 * q + 8, :])
+        load_w1(0, 1, "slot_a")
+        v_s = held([P, S], U8, "v_s")
+        nc.vector.tensor_copy(v_s[:], tab_s[:].indirect(idx[:]))
+        load_w4(1, "slot_b")
+        nc.gpsimd.dma_start(out=v_s1[0:100, :].bitcast(I32), in_=v_s[4:104, :].bitcast(I32))
+
+        turned = psum.tile([P, 4, P], F32, name="acc_a", bufs=3)
+        for t in range(4):
+            nc.tensor.transpose(turned[:, t, :], rows[:, t, :], ident[:])
+        turned_gn = psum.tile([P, 4, P], F32, name="acc_y", bufs=1)
+        nc.tensor.transpose(turned_gn[:, 0, :], rows[:, 4, :], ident[:])
+        bias = held([P, 4, 2], F32, "bias")
+        nc.scalar.copy(out=bias[:], in_=turned[:, :, 0:2])
+        gain = held([P, 3], F32, "gain")
+        nc.scalar.copy(out=gain[:], in_=turned_gn[:, 0, 0:3])
+
+        gather_words(0, 0)
+        gather_words(1, 0)
+        gather_words(0, 1)
+        load_w1(1, 1, "slot_c")
+        gather_words(1, 1)
+        load_w3(0, "slot_d")
+        order_w4(0)
+        load_w3(1, "slot_g")
+        w4_s = held([P, 2, H], U8, "w4_s")
+        nc.vector.tensor_copy(
+            out=w4_s[:].bitcast(I32).rearrange("p a (b t g) -> p (a b) g t", b=2, t=4),
+            in_=w4s_raw[:].bitcast(I32).rearrange("p a (b g t) -> p (a b) g t", b=2, t=4),
+        )
+        for c in range(4):
+            product_b(0, 0, c)
+        cast_w1(nc.scalar.copy, 0, 0, 0, 4)
+        wgo_sb = slot([P, S], F32, "slot_e")
+        nc.sync.dma_start(out=wgo_sb[:], in_=wgo)
+        quant_w1(0, 0, 0, 4)
+        cast_w1(nc.vector.tensor_copy, 1, 0, 0, 1)
+        cast_w1(nc.vector.tensor_copy, 1, 0, 1, 2)
+        cast_w1(nc.scalar.copy, 1, 0, 2, 3)
+        cast_w1(nc.scalar.copy, 1, 0, 3, 4)
+        load_x0(0, "slot_f")
+        for t in range(4):
+            quant_w1(1, 0, t, t + 1)
+        product_a(0, 0, 0, 4, "a_0")
+        cast_w1(nc.vector.tensor_copy, 0, 1, 0, 4)
+        order_w4(1)
+        quant_w1(0, 1, 0, 4)
+        cast_w1(nc.scalar.copy, 1, 1, 0, 4)
+        h_bf[0, 0] = slot([P, 4 * HALF], BF16, "slot_a")
+        for c in range(4):
+            step(0, 0, c)
+        quant_w1(1, 1, 0, 4)
+        product_a(1, 0, 0, 2, "a_1")
+        product_a(1, 0, 2, 4, "a_2")
+        quant_h(0, 0)
+        load_x0(1, "slot_a")
+        cast_w3(nc.vector.tensor_copy, 0)
+        h_bf[1, 0] = held([P, 4 * HALF], BF16, "h_bf1")
+        step(1, 0, 0)
+        step(1, 0, 1)
+        quant_w3(0)
+        product_a(0, 1, 0, 4, "a_3")
+        step(1, 0, 2)
+        step(1, 0, 3)
+        quant_h(1, 0)
+        product_y(0, 0, "y_0")
+        cast_w3(nc.scalar.copy, 1)
+        h_bf[0, 1] = held([P, 4 * HALF], BF16, "h_bf2")
+        step(0, 1, 0)
+        step(0, 1, 1)
+        product_a(1, 1, 0, 4, "a_0")
+        scatter(0, 0)
+        quant_w3(1)
+        product_y(1, 0, "y_1")
+        cast_w3(nc.scalar.copy, 2)
+        load_x0(2, "slot_d")
+        step(0, 1, 2)
+        step(0, 1, 3)
+        h_bf[1, 1] = held([P, 4 * HALF], BF16, "h_bf1")
+        step(1, 1, 0)
+        quant_h(0, 1)
+        for c in range(1, 4):
+            step(1, 1, c)
+        quant_w3(2)
+        quant_h(1, 1)
+        product_y(0, 1, "y_2")
+        product_y(1, 1, "y_3")
+        product_y(2, 0, "y_4")
+        product_y(2, 1, "y_5")
+        scatter(1, 0)
+        scatter(0, 1)
+        finish_on_tensor(0)
+        scatter(1, 1)
+        finish_on_tensor(1)
+        scatter(2, 0)
+        scatter(2, 1)
+        finish(2, 2)

@@ -37,6 +37,12 @@ def tile_list_bridge_order_forces_kernel(
         def held(shape, dtype, name):
             return keep.tile(shape, dtype, name=name, align_bytes=64)
 
+        turn = {"a": 0, "b": 0}
+
+        def bank(kind, shape):
+            turn[kind] = turn[kind] + 1
+            return psum.tile(shape, F32, name="bank_%s%d" % (kind, turn[kind] % {"a": 3, "b": 4}[kind]))
+
         def slot(shape, dtype, tag):
             return keep.tile(shape, dtype, name=tag, align_bytes=64)
 
@@ -51,21 +57,21 @@ def tile_list_bridge_order_forces_kernel(
             )
         tab_s = slot([P, T], U8, "slot_b")
         nc.vector.memset(tab_s[:].bitcast(I32), 0)
-        w4s_raw = held([P, 2, H], U8, "w4s_raw")
+        w4s_raw = slot([P, 2, H], U8, "slot_h")
         nc.vector.memset(w4s_raw[:].rearrange("p a c -> p (a c)").bitcast(I32), 0)
-        ba_rows = slot([2, PASS], F32, "slot_e")
+        ba_rows = held([2, PASS], F32, "ba_rows")
         nc.sync.dma_start(out=ba_rows[:], in_=ba.rearrange("(b c) -> b c", b=2))
-        gn_rows = slot([3, P], F32, "slot_f")
-        nc.sync.dma_start(out=gn_rows[:], in_=gn.rearrange("(c p) -> c p", p=P))
+        gn_row = slot([1, N], F32, "slot_f")
+        nc.sync.dma_start(out=gn_row[:], in_=gn.rearrange("(o n) -> o n", o=1))
         ident = held([P, P], F32, "ident")
         make_identity(nc, ident[:])
-        rows = held([P, 5, P], F32, "rows")
+        rows = held([P, 7, P], F32, "rows")
         nc.gpsimd.memset(rows[:], 0.0)
         nc.scalar.copy(
             out=rows[0:2, 0:4, :].rearrange("b t (g i) -> b t g i", i=4),
             in_=ba_rows[:].rearrange("b (g t i) -> b t g i", t=4, i=4),
         )
-        nc.scalar.copy(out=rows[0:3, 4, :], in_=gn_rows[:])
+        nc.scalar.copy(out=rows[0:1, 4:7, :].rearrange("o c p -> o (c p)"), in_=gn_row[:])
 
         w1_raw = {}
         w4_raw = {}
@@ -109,6 +115,7 @@ def tile_list_bridge_order_forces_kernel(
         load_tab(0, "slot_c")
         load_tab(1, "slot_d")
         load_w4(0, "slot_g")
+        load_w1(0, 0, "slot_e")
         idx2 = keep.tile([P, S // 16], U16, name="idx2")
         nc.sync.dma_start(idx2[:], offs2)
         for q in range(4):
@@ -116,7 +123,6 @@ def tile_list_bridge_order_forces_kernel(
                 out=w4s_raw[32 * q : 32 * q + 4, :, :].bitcast(I32),
                 in_=w4_scales[:, 4 * q : 4 * q + 4, :].rearrange("a r c -> r a c").bitcast(I32),
             )
-        load_w1(0, 0, "slot_e")
         load_w1(1, 0, "slot_f")
 
         w1_bf = {}
@@ -125,7 +131,7 @@ def tile_list_bridge_order_forces_kernel(
 
         def cast_w1(copy, a, b, t0, t1):
             if (a, b) not in w1_bf:
-                w1_bf[a, b] = ring.tile([P, 4 * PASS], BF16, name="w1_bf", align_bytes=64)
+                w1_bf[a, b] = slot([P, 4 * PASS], BF16, "w1_bf%d" % a)
             copy(
                 out=w1_bf[a, b][:, PASS * t0 : PASS * t1].rearrange("p (t g i j) -> p t g j i", t=t1 - t0, i=4, j=4),
                 in_=w1_raw[a, b][:].rearrange("p j (g t i) -> p t g j i", t=4, i=4)[:, t0:t1],
@@ -166,7 +172,7 @@ def tile_list_bridge_order_forces_kernel(
             local = slice(CHUNK * c0, CHUNK * c1)
             cols = slice(HALF * h + CHUNK * c0, HALF * h + CHUNK * c1)
             for t in range(4):
-                acc = psum.tile([P, width], F32, name="acc_a", bufs=3)
+                acc = bank("a", [P, width])
                 for a in range(2):
                     nc.tensor.matmul_mx(
                         out=acc[:],
@@ -183,7 +189,7 @@ def tile_list_bridge_order_forces_kernel(
         b_acc = {}
 
         def product_b(b, h, c):
-            acc = psum.tile([P, 4, CHUNK], F32, name="acc_b", bufs=4)
+            acc = bank("b", [P, 4, CHUNK])
             b_acc[b, h, c] = acc
             local = slice(CHUNK * c, CHUNK * (c + 1))
             cols = slice(HALF * h + CHUNK * c, HALF * h + CHUNK * (c + 1))
@@ -259,7 +265,7 @@ def tile_list_bridge_order_forces_kernel(
 
         def scatter(n, h):
             if n not in page:
-                page[n] = slot([P, S], F32, ("page0", "page1", "y_3")[n])
+                page[n] = slot([P, S], F32, ("page0", "slot_a", "y_3")[n])
             nc.vector.tensor_tensor(
                 page[n][:].indirect(idx2[:, 32 * h : 32 * (h + 1)]),
                 y_sb[n, h][:],
@@ -275,17 +281,19 @@ def tile_list_bridge_order_forces_kernel(
                 nc.sync.dma_start(out=out[P * n : P * (n + 1), cols], in_=x0_sb[n][:, cols])
 
         def finish_on_tensor(n):
+            total_sb = {}
             for k in range(2):
-                total = psum.tile([P, 4, P], F32, name="acc_b", bufs=4)
+                total = bank("b", [P, 4, P])
                 for c in range(4):
                     cols = slice(HALF * k + P * c, HALF * k + P * (c + 1))
                     nc.tensor.matmul(total[:, c, :], x0_sb[n][:, cols], ident[:], start=True, stop=False, is_transpose=True)
                     nc.tensor.matmul(total[:, c, :], page[n][:, cols], ident[:], start=False, stop=True, is_transpose=True)
-                total_sb = ring.tile([P, 4, P], F32, name="total_sb", bufs=4, align_bytes=64)
-                nc.scalar.copy(out=total_sb[:], in_=total[:])
-                back = psum.tile([P, 4, P], F32, name="acc_b", bufs=4)
+                total_sb[k] = ring.tile([P, 4, P], F32, name="total_sb", align_bytes=64)
+                nc.scalar.copy(out=total_sb[k][:], in_=total[:])
+            for k in range(2):
+                back = bank("a", [P, 4, P])
                 for c in range(4):
-                    nc.tensor.transpose(back[:, c, :], total_sb[:, c, :], ident[:])
+                    nc.tensor.transpose(back[:, c, :], total_sb[k][:, c, :], ident[:])
                 back_sb = ring.tile([P, HALF], F32, name="back_sb", bufs=4, align_bytes=64)
                 nc.scalar.copy(out=back_sb[:], in_=back[:].rearrange("p c m -> p (c m)"))
                 nc.scalar.dma_start(out=out[P * n : P * (n + 1), HALF * k : HALF * (k + 1)], in_=back_sb[:])
@@ -297,25 +305,27 @@ def tile_list_bridge_order_forces_kernel(
         load_w1(0, 1, "slot_a")
         v_s = held([P, S], U8, "v_s")
         nc.vector.tensor_copy(v_s[:], tab_s[:].indirect(idx[:]))
-        load_w4(1, "slot_b")
-        nc.gpsimd.dma_start(out=v_s1[0:100, :].bitcast(I32), in_=v_s[4:104, :].bitcast(I32))
+        load_w1(1, 1, "slot_b")
+        nc.scalar.dma_start(out=v_s1[0:100, :].bitcast(I32), in_=v_s[4:104, :].bitcast(I32))
 
-        turned = psum.tile([P, 4, P], F32, name="acc_a", bufs=3)
+        turned = bank("a", [P, 4, P])
         for t in range(4):
             nc.tensor.transpose(turned[:, t, :], rows[:, t, :], ident[:])
         turned_gn = psum.tile([P, 4, P], F32, name="acc_y", bufs=1)
-        nc.tensor.transpose(turned_gn[:, 0, :], rows[:, 4, :], ident[:])
+        for n in range(3):
+            nc.tensor.transpose(turned_gn[:, n, :], rows[:, 4 + n, :], ident[:])
         bias = held([P, 4, 2], F32, "bias")
-        nc.scalar.copy(out=bias[:], in_=turned[:, :, 0:2])
+        nc.scalar.activation(out=bias[:], in_=turned[:, :, 0:2], func=IDENT)
         gain = held([P, 3], F32, "gain")
-        nc.scalar.copy(out=gain[:], in_=turned_gn[:, 0, 0:3])
+        nc.scalar.copy(out=gain[:], in_=turned_gn[:, 0:3, 0])
 
         gather_words(0, 0)
         gather_words(1, 0)
         gather_words(0, 1)
-        load_w1(1, 1, "slot_c")
+        load_w4(1, "slot_c")
         gather_words(1, 1)
         load_w3(0, "slot_d")
+        cast_w1(nc.scalar.copy, 0, 0, 0, 4)
         order_w4(0)
         load_w3(1, "slot_g")
         w4_s = held([P, 2, H], U8, "w4_s")
@@ -325,53 +335,52 @@ def tile_list_bridge_order_forces_kernel(
         )
         for c in range(4):
             product_b(0, 0, c)
-        cast_w1(nc.scalar.copy, 0, 0, 0, 4)
-        wgo_sb = slot([P, S], F32, "slot_e")
+        wgo_sb = slot([P, S], F32, "slot_h")
         nc.sync.dma_start(out=wgo_sb[:], in_=wgo)
+        cast_w1(nc.vector.tensor_copy, 1, 0, 0, 2)
         quant_w1(0, 0, 0, 4)
-        cast_w1(nc.vector.tensor_copy, 1, 0, 0, 1)
-        cast_w1(nc.vector.tensor_copy, 1, 0, 1, 2)
         cast_w1(nc.scalar.copy, 1, 0, 2, 3)
         cast_w1(nc.scalar.copy, 1, 0, 3, 4)
-        load_x0(0, "slot_f")
+        load_x0(0, "slot_e")
+        load_x0(1, "slot_f")
         for t in range(4):
             quant_w1(1, 0, t, t + 1)
-        product_a(0, 0, 0, 4, "a_0")
+        product_a(0, 0, 0, 2, "a_0")
+        product_a(0, 0, 2, 4, "a_1")
         cast_w1(nc.vector.tensor_copy, 0, 1, 0, 4)
         order_w4(1)
         quant_w1(0, 1, 0, 4)
-        cast_w1(nc.scalar.copy, 1, 1, 0, 4)
+        cast_w1(nc.scalar.copy, 1, 1, 2, 4)
         h_bf[0, 0] = slot([P, 4 * HALF], BF16, "slot_a")
-        for c in range(4):
-            step(0, 0, c)
-        quant_w1(1, 1, 0, 4)
-        product_a(1, 0, 0, 2, "a_1")
-        product_a(1, 0, 2, 4, "a_2")
+        step(0, 0, 0)
+        step(0, 0, 1)
+        cast_w1(nc.vector.tensor_copy, 1, 1, 0, 2)
+        step(0, 0, 2)
+        quant_w1(1, 1, 0, 2)
+        step(0, 0, 3)
+        quant_w1(1, 1, 2, 4)
+        product_a(1, 0, 0, 2, "a_2")
+        product_a(1, 0, 2, 4, "a_3")
         quant_h(0, 0)
-        load_x0(1, "slot_a")
-        cast_w3(nc.vector.tensor_copy, 0)
+        cast_w3(nc.scalar.copy, 0)
         h_bf[1, 0] = held([P, 4 * HALF], BF16, "h_bf1")
-        step(1, 0, 0)
-        step(1, 0, 1)
-        quant_w3(0)
-        product_a(0, 1, 0, 4, "a_3")
-        step(1, 0, 2)
-        step(1, 0, 3)
+        for c in range(4):
+            step(1, 0, c)
         quant_h(1, 0)
+        quant_w3(0)
         product_y(0, 0, "y_0")
+        product_a(0, 1, 0, 4, "a_4")
         cast_w3(nc.scalar.copy, 1)
-        h_bf[0, 1] = held([P, 4 * HALF], BF16, "h_bf2")
-        step(0, 1, 0)
-        step(0, 1, 1)
-        product_a(1, 1, 0, 4, "a_0")
         scatter(0, 0)
+        product_a(1, 1, 0, 4, "a_5")
         quant_w3(1)
         product_y(1, 0, "y_1")
         cast_w3(nc.scalar.copy, 2)
         load_x0(2, "slot_d")
-        step(0, 1, 2)
-        step(0, 1, 3)
-        h_bf[1, 1] = held([P, 4 * HALF], BF16, "h_bf1")
+        h_bf[0, 1] = held([P, 4 * HALF], BF16, "h_bf2")
+        for c in range(4):
+            step(0, 1, c)
+        h_bf[1, 1] = slot([P, 4 * HALF], BF16, "slot_a")
         step(1, 1, 0)
         quant_h(0, 1)
         for c in range(1, 4):

@@ -61,7 +61,7 @@ def tile_list_bridge_order_forces_kernel(
         nc.vector.memset(w4s_raw[:].rearrange("p a c -> p (a c)").bitcast(I32), 0)
         ba_rows = held([2, PASS], F32, "ba_rows")
         nc.sync.dma_start(out=ba_rows[:], in_=ba.rearrange("(b c) -> b c", b=2))
-        gn_row = slot([1, N], F32, "slot_f")
+        gn_row = held([1, N], F32, "gn_row")
         nc.sync.dma_start(out=gn_row[:], in_=gn.rearrange("(o n) -> o n", o=1))
         ident = held([P, P], F32, "ident")
         make_identity(nc, ident[:])
@@ -123,7 +123,6 @@ def tile_list_bridge_order_forces_kernel(
                 out=w4s_raw[32 * q : 32 * q + 4, :, :].bitcast(I32),
                 in_=w4_scales[:, 4 * q : 4 * q + 4, :].rearrange("a r c -> r a c").bitcast(I32),
             )
-        load_w1(1, 0, "slot_f")
 
         w1_bf = {}
         w1_c = {}
@@ -131,7 +130,7 @@ def tile_list_bridge_order_forces_kernel(
 
         def cast_w1(copy, a, b, t0, t1):
             if (a, b) not in w1_bf:
-                w1_bf[a, b] = slot([P, 4 * PASS], BF16, "w1_bf%d" % a)
+                w1_bf[a, b] = slot([P, 4 * PASS], BF16, "w1_bf%d%d" % (a, b))
             copy(
                 out=w1_bf[a, b][:, PASS * t0 : PASS * t1].rearrange("p (t g i j) -> p t g j i", t=t1 - t0, i=4, j=4),
                 in_=w1_raw[a, b][:].rearrange("p j (g t i) -> p t g j i", t=4, i=4)[:, t0:t1],
@@ -158,8 +157,8 @@ def tile_list_bridge_order_forces_kernel(
 
         v_w = {}
 
-        def gather_words(a, h):
-            v_w[a, h] = held([P, HALF], U32, "v_w%d%d" % (a, h))
+        def gather_words(a, h, tag):
+            v_w[a, h] = slot([P, HALF], U32, tag)
             nc.vector.tensor_copy(v_w[a, h][:], tab_w[a][:].indirect(idx[:, 32 * h : 32 * (h + 1)]))
 
         a_sb = {}
@@ -213,26 +212,33 @@ def tile_list_bridge_order_forces_kernel(
                 op=MULT,
             )
 
+        chunks = [(0, 0, 0), (0, 0, 1), (0, 0, 2), (0, 0, 3), (0, 1, 0), (0, 1, 1), (1, 0, 0), (1, 0, 1), (1, 0, 2), (1, 0, 3), (0, 1, 2), (0, 1, 3), (1, 1, 0), (1, 1, 1), (1, 1, 2), (1, 1, 3)]
+
         def step(b, h, c):
             product_h(b, h, c)
-            nxt = 2 * h + b + 1
-            if nxt < 4:
-                product_b(nxt % 2, nxt // 2, c)
+            nxt = chunks.index((b, h, c)) + 4
+            if nxt < 16:
+                product_b(*chunks[nxt])
 
         h_c = {}
         h_s = {}
 
-        def quant_h(b, h):
-            h_c[b, h] = held([P, HALF], U32, "h_c%d%d" % (b, h))
-            h_s[b, h] = held([P, HALF], U8, "h_s%d%d" % (b, h))
-            nc.vector.quantize_mx(out=h_c[b, h][:].bitcast(FP8X4), scales=h_s[b, h][:], in_=h_bf[b, h][:])
+        def quant_h(b, h, c0, c1):
+            if (b, h) not in h_c:
+                h_c[b, h] = held([P, HALF], U32, "h_c%d%d" % (b, h))
+                h_s[b, h] = held([P, HALF], U8, "h_s%d%d" % (b, h))
+            nc.vector.quantize_mx(
+                out=h_c[b, h][:, CHUNK * c0 : CHUNK * c1].bitcast(FP8X4),
+                scales=h_s[b, h][:, CHUNK * c0 : CHUNK * c1],
+                in_=h_bf[b, h][:, 4 * CHUNK * c0 : 4 * CHUNK * c1],
+            )
 
         w3_bf = {}
         w3_c = {}
         w3_s = {}
 
-        def cast_w3(copy, n):
-            w3_bf[n] = held([P, 2 * 4 * P], BF16, "w3_bf%d" % n)
+        def cast_w3(copy, n, tag):
+            w3_bf[n] = slot([P, 2 * 4 * P], BF16, tag)
             for b in range(2):
                 copy(
                     out=w3_bf[n][:, 4 * P * b : 4 * P * (b + 1)].rearrange("p (c i t) -> p c t i", i=4, t=4),
@@ -246,30 +252,31 @@ def tile_list_bridge_order_forces_kernel(
 
         y_sb = {}
 
-        def product_y(n, h, tag):
-            acc = psum.tile([P, HALF], F32, name="acc_y", bufs=1)
+        def product_y(n, h, c0, c1, tag):
+            local = slice(CHUNK * c0, CHUNK * c1)
+            acc = psum.tile([P, CHUNK * (c1 - c0)], F32, name="acc_y", bufs=1)
             for b in range(2):
                 nc.tensor.matmul_mx(
                     out=acc[:],
                     lhsT=w3_c[n][:, P * b : P * (b + 1)].bitcast(FP8X4),
                     lhsT_scale=w3_s[n][:, P * b : P * (b + 1)],
-                    rhs=h_c[b, h][:].bitcast(FP8X4),
-                    rhs_scale=h_s[b, h][:],
+                    rhs=h_c[b, h][:, local].bitcast(FP8X4),
+                    rhs_scale=h_s[b, h][:, local],
                     start=(b == 0),
                     stop=(b == 1),
                 )
-            y_sb[n, h] = slot([P, HALF], F32, tag)
-            nc.scalar.activation(out=y_sb[n, h][:], in_=acc[:], func=COPY, scale=gain[:, n : n + 1])
+            y_sb[n, h, c0] = slot([P, CHUNK * (c1 - c0)], F32, tag)
+            nc.scalar.activation(out=y_sb[n, h, c0][:], in_=acc[:], func=COPY, scale=gain[:, n : n + 1])
 
         page = {}
 
-        def scatter(n, h):
+        def scatter(n, h, c0, c1):
             if n not in page:
-                page[n] = slot([P, S], F32, ("page0", "slot_a", "y_3")[n])
+                page[n] = slot([P, S], F32, ("page0", "h_bf1", "y_3")[n])
             nc.vector.tensor_tensor(
-                page[n][:].indirect(idx2[:, 32 * h : 32 * (h + 1)]),
-                y_sb[n, h][:],
-                wgo_sb[:, HALF * h : HALF * (h + 1)],
+                page[n][:].indirect(idx2[:, 32 * h + 8 * c0 : 32 * h + 8 * c1]),
+                y_sb[n, h, c0][:],
+                wgo_sb[:, HALF * h + CHUNK * c0 : HALF * h + CHUNK * c1],
                 MULT,
             )
 
@@ -302,11 +309,10 @@ def tile_list_bridge_order_forces_kernel(
         nc.vector.memset(v_s1[:].bitcast(I32), 0)
         for q in range(4):
             nc.vector.tensor_copy(out=tab_s[32 * q : 32 * q + 8, :].bitcast(I32), in_=tab_s_rows[32 * q : 32 * q + 8, :])
-        load_w1(0, 1, "slot_a")
         v_s = held([P, S], U8, "v_s")
         nc.vector.tensor_copy(v_s[:], tab_s[:].indirect(idx[:]))
-        load_w1(1, 1, "slot_b")
-        nc.scalar.dma_start(out=v_s1[0:100, :].bitcast(I32), in_=v_s[4:104, :].bitcast(I32))
+        nc.sync.dma_start(out=v_s1[0:100, :].bitcast(I32), in_=v_s[4:104, :].bitcast(I32))
+        load_w1(1, 0, "slot_b")
 
         turned = bank("a", [P, 4, P])
         for t in range(4):
@@ -319,15 +325,12 @@ def tile_list_bridge_order_forces_kernel(
         gain = held([P, 3], F32, "gain")
         nc.scalar.copy(out=gain[:], in_=turned_gn[:, 0:3, 0])
 
-        gather_words(0, 0)
-        gather_words(1, 0)
-        gather_words(0, 1)
-        load_w4(1, "slot_c")
-        gather_words(1, 1)
-        load_w3(0, "slot_d")
-        cast_w1(nc.scalar.copy, 0, 0, 0, 4)
+        gather_words(0, 0, "v_w00")
+        gather_words(0, 1, "v_w01")
+        load_w1(0, 1, "slot_c")
+        gather_words(1, 0, "v_w10")
         order_w4(0)
-        load_w3(1, "slot_g")
+        load_w1(1, 1, "slot_g")
         w4_s = held([P, 2, H], U8, "w4_s")
         nc.vector.tensor_copy(
             out=w4_s[:].bitcast(I32).rearrange("p a (b t g) -> p (a b) g t", b=2, t=4),
@@ -335,14 +338,18 @@ def tile_list_bridge_order_forces_kernel(
         )
         for c in range(4):
             product_b(0, 0, c)
-        wgo_sb = slot([P, S], F32, "slot_h")
-        nc.sync.dma_start(out=wgo_sb[:], in_=wgo)
-        cast_w1(nc.vector.tensor_copy, 1, 0, 0, 2)
+        gather_words(1, 1, "slot_h")
+        load_w4(1, "slot_d")
+        cast_w1(nc.scalar.copy, 0, 0, 0, 4)
+        load_w3(0, "slot_e")
         quant_w1(0, 0, 0, 4)
+        load_w3(1, "w1_bf00")
+        cast_w1(nc.vector.tensor_copy, 1, 0, 0, 1)
+        cast_w1(nc.vector.tensor_copy, 1, 0, 1, 2)
         cast_w1(nc.scalar.copy, 1, 0, 2, 3)
         cast_w1(nc.scalar.copy, 1, 0, 3, 4)
-        load_x0(0, "slot_e")
-        load_x0(1, "slot_f")
+        wgo_sb = slot([P, S], F32, "slot_b")
+        nc.sync.dma_start(out=wgo_sb[:], in_=wgo)
         for t in range(4):
             quant_w1(1, 0, t, t + 1)
         product_a(0, 0, 0, 2, "a_0")
@@ -350,52 +357,61 @@ def tile_list_bridge_order_forces_kernel(
         cast_w1(nc.vector.tensor_copy, 0, 1, 0, 4)
         order_w4(1)
         quant_w1(0, 1, 0, 4)
+        product_a(0, 1, 0, 2, "a_4")
         cast_w1(nc.scalar.copy, 1, 1, 2, 4)
-        h_bf[0, 0] = slot([P, 4 * HALF], BF16, "slot_a")
+        h_bf[0, 0] = slot([P, 4 * HALF], BF16, "slot_c")
         step(0, 0, 0)
         step(0, 0, 1)
         cast_w1(nc.vector.tensor_copy, 1, 1, 0, 2)
         step(0, 0, 2)
-        quant_w1(1, 1, 0, 2)
         step(0, 0, 3)
+        load_x0(0, "slot_g")
+        quant_w1(1, 1, 0, 2)
         quant_w1(1, 1, 2, 4)
         product_a(1, 0, 0, 2, "a_2")
         product_a(1, 0, 2, 4, "a_3")
-        quant_h(0, 0)
-        cast_w3(nc.scalar.copy, 0)
-        h_bf[1, 0] = held([P, 4 * HALF], BF16, "h_bf1")
-        for c in range(4):
-            step(1, 0, c)
-        quant_h(1, 0)
-        quant_w3(0)
-        product_y(0, 0, "y_0")
-        product_a(0, 1, 0, 4, "a_4")
-        cast_w3(nc.scalar.copy, 1)
-        scatter(0, 0)
-        product_a(1, 1, 0, 4, "a_5")
-        quant_w3(1)
-        product_y(1, 0, "y_1")
-        cast_w3(nc.scalar.copy, 2)
-        load_x0(2, "slot_d")
         h_bf[0, 1] = held([P, 4 * HALF], BF16, "h_bf2")
+        step(0, 1, 0)
+        quant_h(0, 0, 0, 4)
+        step(0, 1, 1)
+        load_x0(1, "slot_c")
+        cast_w3(nc.scalar.copy, 0, "w3_bf0")
+        quant_w3(0)
+        h_bf[1, 0] = held([P, 4 * HALF], BF16, "h_bf1")
+        product_a(0, 1, 2, 4, "a_0")
+        step(1, 0, 0)
+        step(1, 0, 1)
+        step(1, 0, 2)
+        quant_h(1, 0, 0, 2)
+        product_y(0, 0, 0, 2, "y_0")
+        product_a(1, 1, 0, 4, "a_5")
+        step(1, 0, 3)
+        scatter(0, 0, 0, 2)
+        quant_h(1, 0, 2, 4)
+        product_y(0, 0, 2, 4, "y_6")
+        step(0, 1, 2)
+        step(0, 1, 3)
+        cast_w3(nc.scalar.copy, 1, "a_3")
+        scatter(0, 0, 2, 4)
+        quant_h(0, 1, 0, 4)
+        quant_w3(1)
+        product_y(1, 0, 0, 4, "y_1")
+        cast_w3(nc.scalar.copy, 2, "y_6")
+        load_x0(2, "slot_e")
+        h_bf[1, 1] = slot([P, 4 * HALF], BF16, "h_bf1")
         for c in range(4):
-            step(0, 1, c)
-        h_bf[1, 1] = slot([P, 4 * HALF], BF16, "slot_a")
-        step(1, 1, 0)
-        quant_h(0, 1)
-        for c in range(1, 4):
             step(1, 1, c)
+        quant_h(1, 1, 0, 4)
         quant_w3(2)
-        quant_h(1, 1)
-        product_y(0, 1, "y_2")
-        product_y(1, 1, "y_3")
-        product_y(2, 0, "y_4")
-        product_y(2, 1, "y_5")
-        scatter(1, 0)
-        scatter(0, 1)
+        product_y(2, 0, 0, 4, "y_4")
+        product_y(0, 1, 0, 4, "y_2")
+        product_y(1, 1, 0, 4, "y_3")
+        product_y(2, 1, 0, 4, "y_5")
+        scatter(1, 0, 0, 4)
+        scatter(0, 1, 0, 4)
         finish_on_tensor(0)
-        scatter(1, 1)
+        scatter(1, 1, 0, 4)
         finish_on_tensor(1)
-        scatter(2, 0)
-        scatter(2, 1)
+        scatter(2, 0, 0, 4)
+        scatter(2, 1, 0, 4)
         finish(2, 2)

@@ -23,6 +23,9 @@ P = 128
 PASS = 512
 HALF = 512
 CHUNK = 128
+PER_COLUMN = 16
+BANKS = {"a": 3, "b": 4, "y": 1}
+LAST_PIECES = 4
 
 
 def tile_list_bridge_order_forces_kernel(
@@ -34,44 +37,41 @@ def tile_list_bridge_order_forces_kernel(
         ring = ctx.enter_context(tc.tile_pool(name="ring", bufs=2))
         psum = ctx.enter_context(tc.psum_pool(name="psum", bufs=1))
 
-        def held(shape, dtype, name):
-            return keep.tile(shape, dtype, name=name, align_bytes=64)
+        def sbuf(shape, dtype, buffer):
+            return keep.tile(shape, dtype, name=buffer, align_bytes=64)
 
-        turn = {"a": 0, "b": 0}
+        turn = {kind: 0 for kind in BANKS}
 
         def bank(kind, shape):
             turn[kind] = turn[kind] + 1
-            return psum.tile(shape, F32, name="bank_%s%d" % (kind, turn[kind] % {"a": 3, "b": 4}[kind]))
+            return psum.tile(shape, F32, name="bank_%s%d" % (kind, turn[kind] % BANKS[kind]))
 
-        def slot(shape, dtype, tag):
-            return keep.tile(shape, dtype, name=tag, align_bytes=64)
-
-        idx = keep.tile([P, S // 16], U16, name="idx")
+        idx = keep.tile([P, S // PER_COLUMN], U16, name="idx")
         nc.sync.dma_start(idx[:], offs)
 
-        tab_s_rows = slot([P, T // 4], I32, "slot_a")
+        tab_s_rows = sbuf([P, T // 4], I32, "tab_s_rows")
         for q in range(4):
             nc.sync.dma_start(
                 out=tab_s_rows[32 * q : 32 * q + 8, :],
                 in_=tab_scales[:, 4 * q : 4 * q + 4, :].bitcast(I32),
             )
-        tab_s = slot([P, T], U8, "slot_b")
+        tab_s = sbuf([P, T], U8, "tab_s")
         nc.vector.memset(tab_s[:].bitcast(I32), 0)
-        w4s_raw = slot([P, 2, H], U8, "slot_h")
-        nc.vector.memset(w4s_raw[:].rearrange("p a c -> p (a c)").bitcast(I32), 0)
-        ba_rows = held([2, PASS], F32, "ba_rows")
+        w4_s_raw = sbuf([P, 2, H], U8, "w4_s_raw")
+        nc.vector.memset(w4_s_raw[:].rearrange("p a c -> p (a c)").bitcast(I32), 0)
+        ba_rows = sbuf([2, PASS], F32, "ba_rows")
         nc.sync.dma_start(out=ba_rows[:], in_=ba.rearrange("(b c) -> b c", b=2))
-        gn_row = held([1, N], F32, "gn_row")
+        gn_row = sbuf([1, N], F32, "gn_row")
         nc.sync.dma_start(out=gn_row[:], in_=gn.rearrange("(o n) -> o n", o=1))
-        ident = held([P, P], F32, "ident")
+        ident = sbuf([P, P], F32, "ident")
         make_identity(nc, ident[:])
-        rows = held([P, 7, P], F32, "rows")
-        nc.gpsimd.memset(rows[:], 0.0)
+        vectors = sbuf([P, 7, P], F32, "vectors")
+        nc.gpsimd.memset(vectors[:], 0.0)
         nc.scalar.copy(
-            out=rows[0:2, 0:4, :].rearrange("b t (g i) -> b t g i", i=4),
+            out=vectors[0:2, 0:4, :].rearrange("b t (g i) -> b t g i", i=4),
             in_=ba_rows[:].rearrange("b (g t i) -> b t g i", t=4, i=4),
         )
-        nc.scalar.copy(out=rows[0:1, 4:7, :].rearrange("o c p -> o (c p)"), in_=gn_row[:])
+        nc.scalar.copy(out=vectors[0:1, 4:7, :].rearrange("o n p -> o (n p)"), in_=gn_row[:])
 
         w1_raw = {}
         w4_raw = {}
@@ -79,48 +79,48 @@ def tile_list_bridge_order_forces_kernel(
         w3_raw = {}
         x0_sb = {}
 
-        def load_w1(a, b, tag):
-            w1_raw[a, b] = slot([P, 4, PASS], F32, tag)
+        def load_w1(a, b, buffer):
+            w1_raw[a, b] = sbuf([P, 4, PASS], F32, buffer)
             nc.sync.dma_start(
                 out=w1_raw[a, b][:],
                 in_=w1[PASS * a : PASS * (a + 1), PASS * b : PASS * (b + 1)].rearrange("(p j) c -> p j c", j=4),
             )
 
-        def load_w4(b, tag):
-            w4_raw[b] = slot([P, 2, 256], I32, tag)
+        def load_w4(b, buffer):
+            w4_raw[b] = sbuf([P, 2, PASS // 2], I32, buffer)
             nc.sync.dma_start(
                 out=w4_raw[b][:],
-                in_=w4_words[:, :, 1024 * b : 1024 * (b + 1)].rearrange("a p c -> p a c").bitcast(I32),
+                in_=w4_words[:, :, 2 * PASS * b : 2 * PASS * (b + 1)].rearrange("a p c -> p a c").bitcast(I32),
             )
 
-        def load_tab(a, tag):
-            tab_w[a] = slot([P, T], U32, tag)
+        def load_tab(a):
+            tab_w[a] = sbuf([P, T], U32, "tab_w%d" % a)
             nc.sync.dma_start(
                 out=tab_w[a][:].bitcast(I32),
                 in_=tab_words[a].rearrange("p t i -> p (t i)").bitcast(I32),
             )
 
-        def load_w3(b, tag):
-            w3_raw[b] = slot([P, 4, N], F32, tag)
+        def load_w3(b, buffer):
+            w3_raw[b] = sbuf([P, 4, N], F32, buffer)
             for t in range(4):
                 nc.sync.dma_start(
                     out=w3_raw[b][:, t, :],
                     in_=w3[PASS * b : PASS * (b + 1), :].rearrange("(g t i) n -> t g i n", t=4, i=4)[t],
                 )
 
-        def load_x0(n, tag):
-            x0_sb[n] = slot([P, S], F32, tag)
+        def load_x0(n, buffer):
+            x0_sb[n] = sbuf([P, S], F32, buffer)
             nc.sync.dma_start(out=x0_sb[n][:], in_=x0[P * n : P * (n + 1), :])
 
-        load_tab(0, "slot_c")
-        load_tab(1, "slot_d")
-        load_w4(0, "slot_g")
-        load_w1(0, 0, "slot_e")
-        idx2 = keep.tile([P, S // 16], U16, name="idx2")
+        load_tab(0)
+        load_tab(1)
+        load_w4(0, "w4_raw0")
+        load_w1(0, 0, "w1_raw00")
+        idx2 = keep.tile([P, S // PER_COLUMN], U16, name="idx2")
         nc.sync.dma_start(idx2[:], offs2)
         for q in range(4):
             nc.sync.dma_start(
-                out=w4s_raw[32 * q : 32 * q + 4, :, :].bitcast(I32),
+                out=w4_s_raw[32 * q : 32 * q + 4, :, :].bitcast(I32),
                 in_=w4_scales[:, 4 * q : 4 * q + 4, :].rearrange("a r c -> r a c").bitcast(I32),
             )
 
@@ -130,7 +130,7 @@ def tile_list_bridge_order_forces_kernel(
 
         def cast_w1(copy, a, b, t0, t1):
             if (a, b) not in w1_bf:
-                w1_bf[a, b] = slot([P, 4 * PASS], BF16, "w1_bf%d%d" % (a, b))
+                w1_bf[a, b] = sbuf([P, 4 * PASS], BF16, "w1_bf%d%d" % (a, b))
             copy(
                 out=w1_bf[a, b][:, PASS * t0 : PASS * t1].rearrange("p (t g i j) -> p t g j i", t=t1 - t0, i=4, j=4),
                 in_=w1_raw[a, b][:].rearrange("p j (g t i) -> p t g j i", t=4, i=4)[:, t0:t1],
@@ -138,8 +138,8 @@ def tile_list_bridge_order_forces_kernel(
 
         def quant_w1(a, b, t0, t1):
             if (a, b) not in w1_c:
-                w1_c[a, b] = held([P, PASS], U32, "w1_c%d%d" % (a, b))
-                w1_s[a, b] = held([P, PASS], U8, "w1_s%d%d" % (a, b))
+                w1_c[a, b] = sbuf([P, PASS], U32, "w1_c%d%d" % (a, b))
+                w1_s[a, b] = sbuf([P, PASS], U8, "w1_s%d%d" % (a, b))
             nc.vector.quantize_mx(
                 out=w1_c[a, b][:, P * t0 : P * t1].bitcast(FP8X4),
                 scales=w1_s[a, b][:, P * t0 : P * t1],
@@ -149,7 +149,7 @@ def tile_list_bridge_order_forces_kernel(
         w4_c = {}
 
         def order_w4(b):
-            w4_c[b] = held([P, 2, 1024], U8, "w4_c%d" % b)
+            w4_c[b] = sbuf([P, 2, 2 * PASS], U8, "w4_c%d" % b)
             nc.vector.tensor_copy(
                 out=w4_c[b][:].bitcast(I32).rearrange("p a (t g e) -> p a g t e", t=4, e=2),
                 in_=w4_raw[b][:].rearrange("p a (g t e) -> p a g t e", t=4, e=2),
@@ -157,19 +157,20 @@ def tile_list_bridge_order_forces_kernel(
 
         v_w = {}
 
-        def gather_words(a, h, tag):
-            v_w[a, h] = slot([P, HALF], U32, tag)
-            nc.vector.tensor_copy(v_w[a, h][:], tab_w[a][:].indirect(idx[:, 32 * h : 32 * (h + 1)]))
+        def gather_words(a, h, buffer):
+            v_w[a, h] = sbuf([P, HALF], U32, buffer)
+            entries = slice(HALF * h // PER_COLUMN, HALF * (h + 1) // PER_COLUMN)
+            nc.vector.tensor_copy(v_w[a, h][:], tab_w[a][:].indirect(idx[:, entries]))
 
         a_sb = {}
 
-        def product_a(b, h, c0, c1, tag):
+        def product_a(b, h, c0, c1, buffer):
             width = CHUNK * (c1 - c0)
-            tile = slot([P, 4, width], F32, tag)
+            a_tile = sbuf([P, 4, width], F32, buffer)
             for c in range(c0, c1):
-                a_sb[b, h, c] = tile[:, :, CHUNK * (c - c0) : CHUNK * (c - c0 + 1)]
-            local = slice(CHUNK * c0, CHUNK * c1)
-            cols = slice(HALF * h + CHUNK * c0, HALF * h + CHUNK * c1)
+                a_sb[b, h, c] = a_tile[:, :, CHUNK * (c - c0) : CHUNK * (c - c0 + 1)]
+            in_half = slice(CHUNK * c0, CHUNK * c1)
+            in_list = slice(HALF * h + CHUNK * c0, HALF * h + CHUNK * c1)
             for t in range(4):
                 acc = bank("a", [P, width])
                 for a in range(2):
@@ -177,12 +178,12 @@ def tile_list_bridge_order_forces_kernel(
                         out=acc[:],
                         lhsT=w1_c[a, b][:, P * t : P * (t + 1)].bitcast(FP8X4),
                         lhsT_scale=w1_s[a, b][:, P * t : P * (t + 1)],
-                        rhs=v_w[a, h][:, local].bitcast(FP8X4),
-                        rhs_scale=v_s[4 * a : P, cols],
+                        rhs=v_w[a, h][:, in_half].bitcast(FP8X4),
+                        rhs_scale=v_s[4 * a : P, in_list],
                         start=(a == 0),
                         stop=(a == 1),
                     )
-                nc.scalar.activation(out=tile[:, t, :], in_=acc[:], func=IDENT, bias=bias[:, t, b : b + 1])
+                nc.scalar.activation(out=a_tile[:, t, :], in_=acc[:], func=IDENT, bias=bias[:, t, b : b + 1])
 
         h_bf = {}
         b_acc = {}
@@ -190,43 +191,46 @@ def tile_list_bridge_order_forces_kernel(
         def product_b(b, h, c):
             acc = bank("b", [P, 4, CHUNK])
             b_acc[b, h, c] = acc
-            local = slice(CHUNK * c, CHUNK * (c + 1))
-            cols = slice(HALF * h + CHUNK * c, HALF * h + CHUNK * (c + 1))
+            in_half = slice(CHUNK * c, CHUNK * (c + 1))
+            in_list = slice(HALF * h + CHUNK * c, HALF * h + CHUNK * (c + 1))
             for t in range(4):
                 for a in range(2):
                     nc.tensor.matmul_mx(
                         out=acc[:, t, :],
-                        lhsT=w4_c[b][:, a, 256 * t : 256 * (t + 1)].bitcast(FP4X4),
+                        lhsT=w4_c[b][:, a, 2 * P * t : 2 * P * (t + 1)].bitcast(FP4X4),
                         lhsT_scale=w4_s[:, a, PASS * b + P * t : PASS * b + P * (t + 1)],
-                        rhs=v_w[a, h][:, local].bitcast(FP8X4),
-                        rhs_scale=(v_s, v_s1)[a][:, cols],
+                        rhs=v_w[a, h][:, in_half].bitcast(FP8X4),
+                        rhs_scale=(v_s, v_s1)[a][:, in_list],
                         start=(a == 0),
                         stop=(a == 1),
                     )
 
+        chunks = (
+            [(0, 0, c) for c in range(4)]
+            + [(0, 1, c) for c in range(2)]
+            + [(1, 0, c) for c in range(4)]
+            + [(0, 1, c) for c in range(2, 4)]
+            + [(1, 1, c) for c in range(4)]
+        )
+
         def product_h(b, h, c):
             nc.vector.tensor_tensor(
-                out=h_bf[b, h][:, 4 * CHUNK * c : 4 * CHUNK * (c + 1)].rearrange("p (c i t) -> p c t i", i=4, t=4),
-                in0=b_acc[b, h, c][:].rearrange("p t (c i) -> p c t i", i=4),
-                in1=a_sb[b, h, c].rearrange("p t (c i) -> p c t i", i=4),
+                out=h_bf[b, h][:, 4 * CHUNK * c : 4 * CHUNK * (c + 1)].rearrange("p (e i t) -> p e t i", i=4, t=4),
+                in0=b_acc[b, h, c][:].rearrange("p t (e i) -> p e t i", i=4),
+                in1=a_sb[b, h, c].rearrange("p t (e i) -> p e t i", i=4),
                 op=MULT,
             )
-
-        chunks = [(0, 0, 0), (0, 0, 1), (0, 0, 2), (0, 0, 3), (0, 1, 0), (0, 1, 1), (1, 0, 0), (1, 0, 1), (1, 0, 2), (1, 0, 3), (0, 1, 2), (0, 1, 3), (1, 1, 0), (1, 1, 1), (1, 1, 2), (1, 1, 3)]
-
-        def step(b, h, c):
-            product_h(b, h, c)
-            nxt = chunks.index((b, h, c)) + 4
-            if nxt < 16:
-                product_b(*chunks[nxt])
+            ahead = chunks.index((b, h, c)) + BANKS["b"]
+            if ahead < len(chunks):
+                product_b(*chunks[ahead])
 
         h_c = {}
         h_s = {}
 
         def quant_h(b, h, c0, c1):
             if (b, h) not in h_c:
-                h_c[b, h] = held([P, HALF], U32, "h_c%d%d" % (b, h))
-                h_s[b, h] = held([P, HALF], U8, "h_s%d%d" % (b, h))
+                h_c[b, h] = sbuf([P, HALF], U32, "h_c%d%d" % (b, h))
+                h_s[b, h] = sbuf([P, HALF], U8, "h_s%d%d" % (b, h))
             nc.vector.quantize_mx(
                 out=h_c[b, h][:, CHUNK * c0 : CHUNK * c1].bitcast(FP8X4),
                 scales=h_s[b, h][:, CHUNK * c0 : CHUNK * c1],
@@ -237,181 +241,187 @@ def tile_list_bridge_order_forces_kernel(
         w3_c = {}
         w3_s = {}
 
-        def cast_w3(copy, n, tag):
-            w3_bf[n] = slot([P, 2 * 4 * P], BF16, tag)
+        def cast_w3(n, buffer):
+            w3_bf[n] = sbuf([P, 2 * 4 * P], BF16, buffer)
             for b in range(2):
-                copy(
-                    out=w3_bf[n][:, 4 * P * b : 4 * P * (b + 1)].rearrange("p (c i t) -> p c t i", i=4, t=4),
-                    in_=w3_raw[b][:, :, P * n : P * (n + 1)].rearrange("p t (c i) -> p c t i", i=4),
+                nc.scalar.copy(
+                    out=w3_bf[n][:, 4 * P * b : 4 * P * (b + 1)].rearrange("p (e i t) -> p e t i", i=4, t=4),
+                    in_=w3_raw[b][:, :, P * n : P * (n + 1)].rearrange("p t (e i) -> p e t i", i=4),
                 )
 
         def quant_w3(n):
-            w3_c[n] = held([P, 2 * P], U32, "w3_c%d" % n)
-            w3_s[n] = held([P, 2 * P], U8, "w3_s%d" % n)
+            w3_c[n] = sbuf([P, 2 * P], U32, "w3_c%d" % n)
+            w3_s[n] = sbuf([P, 2 * P], U8, "w3_s%d" % n)
             nc.vector.quantize_mx(out=w3_c[n][:].bitcast(FP8X4), scales=w3_s[n][:], in_=w3_bf[n][:])
 
         y_sb = {}
 
-        def product_y(n, h, c0, c1, tag):
-            local = slice(CHUNK * c0, CHUNK * c1)
-            acc = psum.tile([P, CHUNK * (c1 - c0)], F32, name="acc_y", bufs=1)
+        def product_y(n, h, c0, c1, kind):
+            in_half = slice(CHUNK * c0, CHUNK * c1)
+            acc = bank(kind, [P, CHUNK * (c1 - c0)])
             for b in range(2):
                 nc.tensor.matmul_mx(
                     out=acc[:],
                     lhsT=w3_c[n][:, P * b : P * (b + 1)].bitcast(FP8X4),
                     lhsT_scale=w3_s[n][:, P * b : P * (b + 1)],
-                    rhs=h_c[b, h][:, local].bitcast(FP8X4),
-                    rhs_scale=h_s[b, h][:, local],
+                    rhs=h_c[b, h][:, in_half].bitcast(FP8X4),
+                    rhs_scale=h_s[b, h][:, in_half],
                     start=(b == 0),
                     stop=(b == 1),
                 )
-            y_sb[n, h, c0] = slot([P, CHUNK * (c1 - c0)], F32, tag)
+            y_sb[n, h, c0] = sbuf([P, CHUNK * (c1 - c0)], F32, "y%d%d%d" % (n, h, c0))
             nc.scalar.activation(out=y_sb[n, h, c0][:], in_=acc[:], func=COPY, scale=gain[:, n : n + 1])
 
         page = {}
 
         def scatter(n, h, c0, c1):
-            if n not in page:
-                page[n] = slot([P, S], F32, ("page0", "h_bf1", "y_3")[n])
+            first, last = HALF * h + CHUNK * c0, HALF * h + CHUNK * c1
             nc.vector.tensor_tensor(
-                page[n][:].indirect(idx2[:, 32 * h + 8 * c0 : 32 * h + 8 * c1]),
+                page[n][:].indirect(idx2[:, first // PER_COLUMN : last // PER_COLUMN]),
                 y_sb[n, h, c0][:],
-                wgo_sb[:, HALF * h + CHUNK * c0 : HALF * h + CHUNK * c1],
+                wgo_sb[:, first:last],
                 MULT,
             )
 
-        def finish(n, pieces):
-            width = S // pieces
-            for k in range(pieces):
+        def finish_on_tensor(n):
+            turned_sum = {}
+            for k in range(2):
+                acc = bank("b", [P, 4, P])
+                for c in range(4):
+                    cols = slice(HALF * k + P * c, HALF * k + P * (c + 1))
+                    nc.tensor.matmul(acc[:, c, :], x0_sb[n][:, cols], ident[:], start=True, stop=False, is_transpose=True)
+                    nc.tensor.matmul(acc[:, c, :], page[n][:, cols], ident[:], start=False, stop=True, is_transpose=True)
+                turned_sum[k] = ring.tile([P, 4, P], F32, name="turned_sum", align_bytes=64)
+                nc.scalar.copy(out=turned_sum[k][:], in_=acc[:])
+            for k in range(2):
+                acc = bank("a", [P, 4, P])
+                for c in range(4):
+                    nc.tensor.transpose(acc[:, c, :], turned_sum[k][:, c, :], ident[:])
+                result = ring.tile([P, HALF], F32, name="result", bufs=4, align_bytes=64)
+                nc.scalar.copy(out=result[:], in_=acc[:].rearrange("p c m -> p (c m)"))
+                nc.scalar.dma_start(out=out[P * n : P * (n + 1), HALF * k : HALF * (k + 1)], in_=result[:])
+
+        def finish_on_vector(n):
+            width = S // LAST_PIECES
+            for k in range(LAST_PIECES):
                 cols = slice(width * k, width * (k + 1))
                 nc.vector.tensor_tensor(out=x0_sb[n][:, cols], in0=page[n][:, cols], in1=x0_sb[n][:, cols], op=ADD)
                 nc.sync.dma_start(out=out[P * n : P * (n + 1), cols], in_=x0_sb[n][:, cols])
 
-        def finish_on_tensor(n):
-            total_sb = {}
-            for k in range(2):
-                total = bank("b", [P, 4, P])
-                for c in range(4):
-                    cols = slice(HALF * k + P * c, HALF * k + P * (c + 1))
-                    nc.tensor.matmul(total[:, c, :], x0_sb[n][:, cols], ident[:], start=True, stop=False, is_transpose=True)
-                    nc.tensor.matmul(total[:, c, :], page[n][:, cols], ident[:], start=False, stop=True, is_transpose=True)
-                total_sb[k] = ring.tile([P, 4, P], F32, name="total_sb", align_bytes=64)
-                nc.scalar.copy(out=total_sb[k][:], in_=total[:])
-            for k in range(2):
-                back = bank("a", [P, 4, P])
-                for c in range(4):
-                    nc.tensor.transpose(back[:, c, :], total_sb[k][:, c, :], ident[:])
-                back_sb = ring.tile([P, HALF], F32, name="back_sb", bufs=4, align_bytes=64)
-                nc.scalar.copy(out=back_sb[:], in_=back[:].rearrange("p c m -> p (c m)"))
-                nc.scalar.dma_start(out=out[P * n : P * (n + 1), HALF * k : HALF * (k + 1)], in_=back_sb[:])
-
-        v_s1 = held([P, S], U8, "v_s1")
+        v_s1 = sbuf([P, S], U8, "v_s1")
         nc.vector.memset(v_s1[:].bitcast(I32), 0)
         for q in range(4):
             nc.vector.tensor_copy(out=tab_s[32 * q : 32 * q + 8, :].bitcast(I32), in_=tab_s_rows[32 * q : 32 * q + 8, :])
-        v_s = held([P, S], U8, "v_s")
+        v_s = sbuf([P, S], U8, "v_s")
         nc.vector.tensor_copy(v_s[:], tab_s[:].indirect(idx[:]))
         nc.sync.dma_start(out=v_s1[0:100, :].bitcast(I32), in_=v_s[4:104, :].bitcast(I32))
-        load_w1(1, 0, "slot_b")
+        load_w1(1, 0, "tab_s")
 
-        turned = bank("a", [P, 4, P])
+        turned_ba = bank("a", [P, 4, P])
         for t in range(4):
-            nc.tensor.transpose(turned[:, t, :], rows[:, t, :], ident[:])
-        turned_gn = psum.tile([P, 4, P], F32, name="acc_y", bufs=1)
+            nc.tensor.transpose(turned_ba[:, t, :], vectors[:, t, :], ident[:])
+        turned_gn = bank("y", [P, 4, P])
         for n in range(3):
-            nc.tensor.transpose(turned_gn[:, n, :], rows[:, 4 + n, :], ident[:])
-        bias = held([P, 4, 2], F32, "bias")
-        nc.scalar.activation(out=bias[:], in_=turned[:, :, 0:2], func=IDENT)
-        gain = held([P, 3], F32, "gain")
+            nc.tensor.transpose(turned_gn[:, n, :], vectors[:, 4 + n, :], ident[:])
+        bias = sbuf([P, 4, 2], F32, "bias")
+        nc.scalar.activation(out=bias[:], in_=turned_ba[:, :, 0:2], func=IDENT)
+        gain = sbuf([P, 3], F32, "gain")
         nc.scalar.copy(out=gain[:], in_=turned_gn[:, 0:3, 0])
 
         gather_words(0, 0, "v_w00")
         gather_words(0, 1, "v_w01")
-        load_w1(0, 1, "slot_c")
+        load_w1(0, 1, "tab_w0")
         gather_words(1, 0, "v_w10")
         order_w4(0)
-        load_w1(1, 1, "slot_g")
-        w4_s = held([P, 2, H], U8, "w4_s")
+        load_w1(1, 1, "w4_raw0")
+        w4_s = sbuf([P, 2, H], U8, "w4_s")
         nc.vector.tensor_copy(
             out=w4_s[:].bitcast(I32).rearrange("p a (b t g) -> p (a b) g t", b=2, t=4),
-            in_=w4s_raw[:].bitcast(I32).rearrange("p a (b g t) -> p (a b) g t", b=2, t=4),
+            in_=w4_s_raw[:].bitcast(I32).rearrange("p a (b g t) -> p (a b) g t", b=2, t=4),
         )
-        for c in range(4):
-            product_b(0, 0, c)
-        gather_words(1, 1, "slot_h")
-        load_w4(1, "slot_d")
+        for chunk in chunks[: BANKS["b"]]:
+            product_b(*chunk)
+        gather_words(1, 1, "w4_s_raw")
+        load_w4(1, "tab_w1")
+
         cast_w1(nc.scalar.copy, 0, 0, 0, 4)
-        load_w3(0, "slot_e")
+        load_w3(0, "w1_raw00")
         quant_w1(0, 0, 0, 4)
         load_w3(1, "w1_bf00")
-        cast_w1(nc.vector.tensor_copy, 1, 0, 0, 1)
-        cast_w1(nc.vector.tensor_copy, 1, 0, 1, 2)
-        cast_w1(nc.scalar.copy, 1, 0, 2, 3)
-        cast_w1(nc.scalar.copy, 1, 0, 3, 4)
-        wgo_sb = slot([P, S], F32, "slot_b")
+        for t in range(4):
+            cast_w1(nc.vector.tensor_copy if t < 2 else nc.scalar.copy, 1, 0, t, t + 1)
+        wgo_sb = sbuf([P, S], F32, "tab_s")
         nc.sync.dma_start(out=wgo_sb[:], in_=wgo)
         for t in range(4):
             quant_w1(1, 0, t, t + 1)
-        product_a(0, 0, 0, 2, "a_0")
-        product_a(0, 0, 2, 4, "a_1")
+
+        product_a(0, 0, 0, 2, "a_first")
+        product_a(0, 0, 2, 4, "a002")
         cast_w1(nc.vector.tensor_copy, 0, 1, 0, 4)
         order_w4(1)
         quant_w1(0, 1, 0, 4)
-        product_a(0, 1, 0, 2, "a_4")
+        product_a(0, 1, 0, 2, "a010")
         cast_w1(nc.scalar.copy, 1, 1, 2, 4)
-        h_bf[0, 0] = slot([P, 4 * HALF], BF16, "slot_c")
-        step(0, 0, 0)
-        step(0, 0, 1)
+        h_bf[0, 0] = sbuf([P, 4 * HALF], BF16, "tab_w0")
+        product_h(0, 0, 0)
+        product_h(0, 0, 1)
         cast_w1(nc.vector.tensor_copy, 1, 1, 0, 2)
-        step(0, 0, 2)
-        step(0, 0, 3)
-        load_x0(0, "slot_g")
+        product_h(0, 0, 2)
+        product_h(0, 0, 3)
+        load_x0(0, "w4_raw0")
         quant_w1(1, 1, 0, 2)
         quant_w1(1, 1, 2, 4)
-        product_a(1, 0, 0, 2, "a_2")
-        product_a(1, 0, 2, 4, "a_3")
-        h_bf[0, 1] = held([P, 4 * HALF], BF16, "h_bf2")
-        step(0, 1, 0)
+
+        product_a(1, 0, 0, 2, "a100")
+        product_a(1, 0, 2, 4, "a102")
+        h_bf[0, 1] = sbuf([P, 4 * HALF], BF16, "h_bf01")
+        product_h(0, 1, 0)
         quant_h(0, 0, 0, 4)
-        step(0, 1, 1)
-        load_x0(1, "slot_c")
-        cast_w3(nc.scalar.copy, 0, "w3_bf0")
+        product_h(0, 1, 1)
+        load_x0(1, "tab_w0")
+        cast_w3(0, "w3_bf0")
         quant_w3(0)
-        h_bf[1, 0] = held([P, 4 * HALF], BF16, "h_bf1")
-        product_a(0, 1, 2, 4, "a_0")
-        step(1, 0, 0)
-        step(1, 0, 1)
-        step(1, 0, 2)
+        h_bf[1, 0] = sbuf([P, 4 * HALF], BF16, "h_bf1")
+        product_a(0, 1, 2, 4, "a_first")
+        product_h(1, 0, 0)
+        product_h(1, 0, 1)
+        product_h(1, 0, 2)
         quant_h(1, 0, 0, 2)
-        product_y(0, 0, 0, 2, "y_0")
-        product_a(1, 1, 0, 4, "a_5")
-        step(1, 0, 3)
+        product_y(0, 0, 0, 2, "y")
+        product_a(1, 1, 0, 4, "a110")
+        product_h(1, 0, 3)
+        page[0] = sbuf([P, S], F32, "page0")
         scatter(0, 0, 0, 2)
         quant_h(1, 0, 2, 4)
-        product_y(0, 0, 2, 4, "y_6")
-        step(0, 1, 2)
-        step(0, 1, 3)
-        cast_w3(nc.scalar.copy, 1, "a_3")
+        product_y(0, 0, 2, 4, "y")
+
+        product_h(0, 1, 2)
+        product_h(0, 1, 3)
+        cast_w3(1, "a102")
         scatter(0, 0, 2, 4)
         quant_h(0, 1, 0, 4)
         quant_w3(1)
-        product_y(1, 0, 0, 4, "y_1")
-        cast_w3(nc.scalar.copy, 2, "y_6")
-        load_x0(2, "slot_e")
-        h_bf[1, 1] = slot([P, 4 * HALF], BF16, "h_bf1")
+        product_y(1, 0, 0, 4, "y")
+        cast_w3(2, "a_first")
+        load_x0(2, "w1_raw00")
+        h_bf[1, 1] = sbuf([P, 4 * HALF], BF16, "h_bf1")
         for c in range(4):
-            step(1, 1, c)
-        quant_h(1, 1, 0, 4)
+            product_h(1, 1, c)
         quant_w3(2)
-        product_y(2, 0, 0, 4, "y_4")
-        product_y(0, 1, 0, 4, "y_2")
-        product_y(1, 1, 0, 4, "y_3")
-        product_y(2, 1, 0, 4, "y_5")
+        quant_h(1, 1, 0, 4)
+
+        product_y(0, 1, 0, 4, "y")
+        product_y(2, 0, 0, 4, "b")
+        product_y(2, 1, 0, 4, "b")
+        product_y(1, 1, 0, 4, "a")
+        page[1] = sbuf([P, S], F32, "h_bf1")
         scatter(1, 0, 0, 4)
         scatter(0, 1, 0, 4)
+        turn["b"] = turn["b"] + 2
         finish_on_tensor(0)
         scatter(1, 1, 0, 4)
         finish_on_tensor(1)
+        page[2] = sbuf([P, S], F32, "y110")
         scatter(2, 0, 0, 4)
         scatter(2, 1, 0, 4)
-        finish(2, 2)
+        finish_on_vector(2)

@@ -124,6 +124,8 @@ def tile_list_bridge_order_forces_kernel(
                 in_=w4_scales[:, 4 * q : 4 * q + 4, :].rearrange("a r c -> r a c").bitcast(I32),
             )
 
+        load_w1(1, 0, "gn_row")
+
         w1_bf = {}
         w1_c = {}
         w1_s = {}
@@ -150,9 +152,9 @@ def tile_list_bridge_order_forces_kernel(
 
         def order_w4(b):
             w4_c[b] = sbuf([P, 2, 2 * PASS], U8, "w4_c%d" % b)
-            nc.vector.tensor_copy(
-                out=w4_c[b][:].bitcast(I32).rearrange("p a (t g e) -> p a g t e", t=4, e=2),
-                in_=w4_raw[b][:].rearrange("p a (g t e) -> p a g t e", t=4, e=2),
+            nc.gpsimd.tensor_copy(
+                out=w4_c[b][:].bitcast(I32).rearrange("p a (t g e) -> p a t g e", t=4, e=2),
+                in_=w4_raw[b][:].rearrange("p a (g t e) -> p a t g e", t=4, e=2),
             )
 
         v_w = {}
@@ -314,8 +316,8 @@ def tile_list_bridge_order_forces_kernel(
             nc.vector.tensor_copy(out=tab_s[32 * q : 32 * q + 8, :].bitcast(I32), in_=tab_s_rows[32 * q : 32 * q + 8, :])
         v_s = sbuf([P, S], U8, "v_s")
         nc.vector.tensor_copy(v_s[:], tab_s[:].indirect(idx[:]))
-        nc.sync.dma_start(out=v_s1[0:100, :].bitcast(I32), in_=v_s[4:104, :].bitcast(I32))
-        load_w1(1, 0, "tab_s")
+        nc.scalar.dma_start(out=v_s1[0:100, :].bitcast(I32), in_=v_s[4:104, :].bitcast(I32))
+        load_w1(0, 1, "tab_s")
 
         turned_ba = bank("a", [P, 4, P])
         for t in range(4):
@@ -330,19 +332,18 @@ def tile_list_bridge_order_forces_kernel(
 
         gather_words(0, 0, "v_w00")
         gather_words(0, 1, "v_w01")
-        load_w1(0, 1, "tab_w0")
+        load_w1(1, 1, "tab_w0")
         gather_words(1, 0, "v_w10")
         order_w4(0)
-        load_w1(1, 1, "w4_raw0")
         w4_s = sbuf([P, 2, H], U8, "w4_s")
-        nc.vector.tensor_copy(
-            out=w4_s[:].bitcast(I32).rearrange("p a (b t g) -> p (a b) g t", b=2, t=4),
-            in_=w4_s_raw[:].bitcast(I32).rearrange("p a (b g t) -> p (a b) g t", b=2, t=4),
+        nc.gpsimd.tensor_copy(
+            out=w4_s[:].bitcast(I32).rearrange("p a (b t g) -> p (a b) t g", b=2, t=4),
+            in_=w4_s_raw[:].bitcast(I32).rearrange("p a (b g t) -> p (a b) t g", b=2, t=4),
         )
         for chunk in chunks[: BANKS["b"]]:
             product_b(*chunk)
-        gather_words(1, 1, "w4_s_raw")
-        load_w4(1, "tab_w1")
+        gather_words(1, 1, "v_w11")
+        load_w4(1, "w4_s_raw")
 
         cast_w1(nc.scalar.copy, 0, 0, 0, 4)
         load_w3(0, "w1_raw00")
@@ -350,7 +351,7 @@ def tile_list_bridge_order_forces_kernel(
         load_w3(1, "w1_bf00")
         for t in range(4):
             cast_w1(nc.vector.tensor_copy if t < 2 else nc.scalar.copy, 1, 0, t, t + 1)
-        wgo_sb = sbuf([P, S], F32, "tab_s")
+        wgo_sb = sbuf([P, S], F32, "gn_row")
         nc.sync.dma_start(out=wgo_sb[:], in_=wgo)
         for t in range(4):
             quant_w1(1, 0, t, t + 1)
@@ -362,13 +363,13 @@ def tile_list_bridge_order_forces_kernel(
         quant_w1(0, 1, 0, 4)
         product_a(0, 1, 0, 2, "a010")
         cast_w1(nc.scalar.copy, 1, 1, 2, 4)
-        h_bf[0, 0] = sbuf([P, 4 * HALF], BF16, "tab_w0")
+        h_bf[0, 0] = sbuf([P, 4 * HALF], BF16, "tab_s")
         product_h(0, 0, 0)
         product_h(0, 0, 1)
         cast_w1(nc.vector.tensor_copy, 1, 1, 0, 2)
         product_h(0, 0, 2)
         product_h(0, 0, 3)
-        load_x0(0, "w4_raw0")
+        load_x0(0, "tab_w0")
         quant_w1(1, 1, 0, 2)
         quant_w1(1, 1, 2, 4)
 
@@ -378,7 +379,7 @@ def tile_list_bridge_order_forces_kernel(
         product_h(0, 1, 0)
         quant_h(0, 0, 0, 4)
         product_h(0, 1, 1)
-        load_x0(1, "tab_w0")
+        load_x0(1, "tab_s")
         cast_w3(0, "w3_bf0")
         quant_w3(0)
         h_bf[1, 0] = sbuf([P, 4 * HALF], BF16, "h_bf1")

@@ -22,6 +22,7 @@ COPY = mybir.ActivationFunctionType.Copy
 P = 128
 PASS = 512
 HALF = 512
+UNIT = 256
 CHUNK = 128
 PER_COLUMN = 16
 BANKS = {"a": 3, "b": 4, "y": 1}
@@ -34,7 +35,6 @@ def tile_list_bridge_order_forces_kernel(
     nc = tc.nc
     with ExitStack() as ctx:
         keep = ctx.enter_context(tc.tile_pool(name="keep", bufs=1))
-        ring = ctx.enter_context(tc.tile_pool(name="ring", bufs=2))
         psum = ctx.enter_context(tc.psum_pool(name="psum", bufs=1))
 
         def sbuf(shape, dtype, buffer):
@@ -48,7 +48,6 @@ def tile_list_bridge_order_forces_kernel(
 
         idx = keep.tile([P, S // PER_COLUMN], U16, name="idx")
         nc.sync.dma_start(idx[:], offs)
-
         tab_s_rows = sbuf([P, T // 4], I32, "tab_s_rows")
         for q in range(4):
             nc.sync.dma_start(
@@ -59,19 +58,8 @@ def tile_list_bridge_order_forces_kernel(
         nc.vector.memset(tab_s[:].bitcast(I32), 0)
         w4_s_raw = sbuf([P, 2, H], U8, "w4_s_raw")
         nc.vector.memset(w4_s_raw[:].rearrange("p a c -> p (a c)").bitcast(I32), 0)
-        ba_rows = sbuf([2, PASS], F32, "ba_rows")
-        nc.sync.dma_start(out=ba_rows[:], in_=ba.rearrange("(b c) -> b c", b=2))
-        gn_row = sbuf([1, N], F32, "gn_row")
-        nc.sync.dma_start(out=gn_row[:], in_=gn.rearrange("(o n) -> o n", o=1))
-        ident = sbuf([P, P], F32, "ident")
-        make_identity(nc, ident[:])
-        vectors = sbuf([P, 7, P], F32, "vectors")
-        nc.gpsimd.memset(vectors[:], 0.0)
-        nc.scalar.copy(
-            out=vectors[0:2, 0:4, :].rearrange("b t (g i) -> b t g i", i=4),
-            in_=ba_rows[:].rearrange("b (g t i) -> b t g i", t=4, i=4),
-        )
-        nc.scalar.copy(out=vectors[0:1, 4:7, :].rearrange("o n p -> o (n p)"), in_=gn_row[:])
+        v_s1 = sbuf([P, S], U8, "v_s1")
+        nc.vector.memset(v_s1[:].bitcast(I32), 0)
 
         w1_raw = {}
         w4_raw = {}
@@ -113,18 +101,40 @@ def tile_list_bridge_order_forces_kernel(
             nc.sync.dma_start(out=x0_sb[n][:], in_=x0[P * n : P * (n + 1), :])
 
         load_tab(0)
-        load_tab(1)
         load_w4(0, "w4_raw0")
-        load_w1(0, 0, "w1_raw00")
-        idx2 = keep.tile([P, S // PER_COLUMN], U16, name="idx2")
-        nc.sync.dma_start(idx2[:], offs2)
+        load_tab(1)
         for q in range(4):
             nc.sync.dma_start(
                 out=w4_s_raw[32 * q : 32 * q + 4, :, :].bitcast(I32),
                 in_=w4_scales[:, 4 * q : 4 * q + 4, :].rearrange("a r c -> r a c").bitcast(I32),
             )
+        idx2 = keep.tile([P, S // PER_COLUMN], U16, name="idx2")
+        nc.sync.dma_start(idx2[:], offs2)
 
-        load_w1(1, 0, "gn_row")
+        ba_rows = sbuf([2, PASS], F32, "ba_rows")
+        nc.scalar.dma_start(out=ba_rows[:], in_=ba.rearrange("(b c) -> b c", b=2))
+        gn_row = sbuf([1, N], F32, "gn_row")
+        nc.scalar.dma_start(out=gn_row[:], in_=gn.rearrange("(o n) -> o n", o=1))
+
+        ident = sbuf([P, P], F32, "ident")
+        make_identity(nc, ident[:])
+        vectors = sbuf([P, 7, P], F32, "vectors")
+        nc.gpsimd.memset(vectors[:], 0.0)
+        nc.scalar.copy(
+            out=vectors[0:2, 0:4, :].rearrange("b t (g i) -> b t g i", i=4),
+            in_=ba_rows[:].rearrange("b (g t i) -> b t g i", t=4, i=4),
+        )
+        nc.scalar.copy(out=vectors[0:1, 4:7, :].rearrange("o n p -> o (n p)"), in_=gn_row[:])
+        turned_ba = bank("a", [P, 4, P])
+        for t in range(4):
+            nc.tensor.transpose(turned_ba[:, t, :], vectors[:, t, :], ident[:])
+        turned_gn = bank("y", [P, 4, P])
+        for n in range(3):
+            nc.tensor.transpose(turned_gn[:, n, :], vectors[:, 4 + n, :], ident[:])
+        bias = sbuf([P, 4, 2], F32, "bias")
+        nc.scalar.activation(out=bias[:], in_=turned_ba[:, :, 0:2], func=IDENT)
+        gain = sbuf([P, 3], F32, "gain")
+        nc.scalar.copy(out=gain[:], in_=turned_gn[:, 0:3, 0])
 
         w1_bf = {}
         w1_c = {}
@@ -166,85 +176,84 @@ def tile_list_bridge_order_forces_kernel(
 
         a_sb = {}
 
-        def product_a(b, h, c0, c1, buffer):
-            width = CHUNK * (c1 - c0)
-            a_tile = sbuf([P, 4, width], F32, buffer)
-            for c in range(c0, c1):
-                a_sb[b, h, c] = a_tile[:, :, CHUNK * (c - c0) : CHUNK * (c - c0 + 1)]
-            in_half = slice(CHUNK * c0, CHUNK * c1)
-            in_list = slice(HALF * h + CHUNK * c0, HALF * h + CHUNK * c1)
-            for t in range(4):
-                acc = bank("a", [P, width])
-                for a in range(2):
-                    nc.tensor.matmul_mx(
-                        out=acc[:],
-                        lhsT=w1_c[a, b][:, P * t : P * (t + 1)].bitcast(FP8X4),
-                        lhsT_scale=w1_s[a, b][:, P * t : P * (t + 1)],
-                        rhs=v_w[a, h][:, in_half].bitcast(FP8X4),
-                        rhs_scale=v_s[4 * a : P, in_list],
-                        start=(a == 0),
-                        stop=(a == 1),
-                    )
-                nc.scalar.activation(out=a_tile[:, t, :], in_=acc[:], func=IDENT, bias=bias[:, t, b : b + 1])
+        def product_a(b, u, buffer):
+            a_sb[b, u] = sbuf([P, 4, UNIT], F32, buffer)
+            h, first = divmod(UNIT * u, HALF)
+            for pair in range(2):
+                acc = bank("a", [P, 2, UNIT])
+                for e in range(2):
+                    t = 2 * pair + e
+                    for a in range(2):
+                        nc.tensor.matmul_mx(
+                            out=acc[:, e, :],
+                            lhsT=w1_c[a, b][:, P * t : P * (t + 1)].bitcast(FP8X4),
+                            lhsT_scale=w1_s[a, b][:, P * t : P * (t + 1)],
+                            rhs=v_w[a, h][:, first : first + UNIT].bitcast(FP8X4),
+                            rhs_scale=v_s[4 * a : P, UNIT * u : UNIT * (u + 1)],
+                            start=(a == 0),
+                            stop=(a == 1),
+                        )
+                for e in range(2):
+                    t = 2 * pair + e
+                    nc.scalar.activation(out=a_sb[b, u][:, t, :], in_=acc[:, e, :], func=IDENT, bias=bias[:, t, b : b + 1])
 
-        h_bf = {}
         b_acc = {}
 
-        def product_b(b, h, c):
+        def product_b(b, c):
             acc = bank("b", [P, 4, CHUNK])
-            b_acc[b, h, c] = acc
-            in_half = slice(CHUNK * c, CHUNK * (c + 1))
-            in_list = slice(HALF * h + CHUNK * c, HALF * h + CHUNK * (c + 1))
-            for t in range(4):
-                for a in range(2):
+            b_acc[b, c] = acc
+            h, first = divmod(CHUNK * c, HALF)
+            for a in range(2):
+                for t in range(4):
                     nc.tensor.matmul_mx(
                         out=acc[:, t, :],
                         lhsT=w4_c[b][:, a, 2 * P * t : 2 * P * (t + 1)].bitcast(FP4X4),
                         lhsT_scale=w4_s[:, a, PASS * b + P * t : PASS * b + P * (t + 1)],
-                        rhs=v_w[a, h][:, in_half].bitcast(FP8X4),
-                        rhs_scale=(v_s, v_s1)[a][:, in_list],
-                        start=(a == 0),
-                        stop=(a == 1),
+                        rhs=v_w[a, h][:, first : first + CHUNK].bitcast(FP8X4),
+                        rhs_scale=(v_s, v_s1)[a][:, CHUNK * c : CHUNK * (c + 1)],
+                        start=(a == 0 and t == 0),
+                        stop=(a == 1 and t == 3),
                     )
 
-        chunks = (
-            [(0, 0, c) for c in range(4)]
-            + [(0, 1, c) for c in range(2)]
-            + [(1, 0, c) for c in range(4)]
-            + [(0, 1, c) for c in range(2, 4)]
-            + [(1, 1, c) for c in range(4)]
-        )
+        chunks = [(b, c) for b in range(2) for c in range(8)]
+        h_bf = {}
 
-        def product_h(b, h, c):
+        def product_h(b, c):
+            h, first = divmod(CHUNK * c, HALF)
+            if (b, h) not in h_bf:
+                h_bf[b, h] = sbuf([P, 4 * HALF], BF16, "h_bf%d%d" % (b, h))
+            u, in_unit = divmod(CHUNK * c, UNIT)
             nc.vector.tensor_tensor(
-                out=h_bf[b, h][:, 4 * CHUNK * c : 4 * CHUNK * (c + 1)].rearrange("p (e i t) -> p e t i", i=4, t=4),
-                in0=b_acc[b, h, c][:].rearrange("p t (e i) -> p e t i", i=4),
-                in1=a_sb[b, h, c].rearrange("p t (e i) -> p e t i", i=4),
+                out=h_bf[b, h][:, 4 * first : 4 * (first + CHUNK)].rearrange("p (e i t) -> p e t i", i=4, t=4),
+                in0=b_acc[b, c][:].rearrange("p t (e i) -> p e t i", i=4),
+                in1=a_sb[b, u][:, :, in_unit : in_unit + CHUNK].rearrange("p t (e i) -> p e t i", i=4),
                 op=MULT,
             )
-            ahead = chunks.index((b, h, c)) + BANKS["b"]
+            ahead = chunks.index((b, c)) + BANKS["b"]
             if ahead < len(chunks):
                 product_b(*chunks[ahead])
 
         h_c = {}
         h_s = {}
 
-        def quant_h(b, h, c0, c1):
+        def quant_h(b, u0, u1):
+            h, first = divmod(UNIT * u0, HALF)
             if (b, h) not in h_c:
                 h_c[b, h] = sbuf([P, HALF], U32, "h_c%d%d" % (b, h))
                 h_s[b, h] = sbuf([P, HALF], U8, "h_s%d%d" % (b, h))
+            last = first + UNIT * (u1 - u0)
             nc.vector.quantize_mx(
-                out=h_c[b, h][:, CHUNK * c0 : CHUNK * c1].bitcast(FP8X4),
-                scales=h_s[b, h][:, CHUNK * c0 : CHUNK * c1],
-                in_=h_bf[b, h][:, 4 * CHUNK * c0 : 4 * CHUNK * c1],
+                out=h_c[b, h][:, first:last].bitcast(FP8X4),
+                scales=h_s[b, h][:, first:last],
+                in_=h_bf[b, h][:, 4 * first : 4 * last],
             )
 
         w3_bf = {}
         w3_c = {}
         w3_s = {}
 
-        def cast_w3(n, buffer):
-            w3_bf[n] = sbuf([P, 2 * 4 * P], BF16, buffer)
+        def cast_w3(n):
+            w3_bf[n] = sbuf([P, 2 * 4 * P], BF16, "w3_bf%d" % n)
             for b in range(2):
                 nc.scalar.copy(
                     out=w3_bf[n][:, 4 * P * b : 4 * P * (b + 1)].rearrange("p (e i t) -> p e t i", i=4, t=4),
@@ -258,29 +267,30 @@ def tile_list_bridge_order_forces_kernel(
 
         y_sb = {}
 
-        def product_y(n, h, c0, c1, kind):
-            in_half = slice(CHUNK * c0, CHUNK * c1)
-            acc = bank(kind, [P, CHUNK * (c1 - c0)])
+        def product_y(n, u0, u1, kind, buffer):
+            h, first = divmod(UNIT * u0, HALF)
+            width = UNIT * (u1 - u0)
+            acc = bank(kind, [P, width])
             for b in range(2):
                 nc.tensor.matmul_mx(
                     out=acc[:],
                     lhsT=w3_c[n][:, P * b : P * (b + 1)].bitcast(FP8X4),
                     lhsT_scale=w3_s[n][:, P * b : P * (b + 1)],
-                    rhs=h_c[b, h][:, in_half].bitcast(FP8X4),
-                    rhs_scale=h_s[b, h][:, in_half],
+                    rhs=h_c[b, h][:, first : first + width].bitcast(FP8X4),
+                    rhs_scale=h_s[b, h][:, first : first + width],
                     start=(b == 0),
                     stop=(b == 1),
                 )
-            y_sb[n, h, c0] = sbuf([P, CHUNK * (c1 - c0)], F32, "y%d%d%d" % (n, h, c0))
-            nc.scalar.activation(out=y_sb[n, h, c0][:], in_=acc[:], func=COPY, scale=gain[:, n : n + 1])
+            y_sb[n, u0] = sbuf([P, width], F32, buffer)
+            nc.scalar.activation(out=y_sb[n, u0][:], in_=acc[:], func=COPY, scale=gain[:, n : n + 1])
 
         page = {}
 
-        def scatter(n, h, c0, c1):
-            first, last = HALF * h + CHUNK * c0, HALF * h + CHUNK * c1
+        def scatter(n, u0, u1):
+            first, last = UNIT * u0, UNIT * u1
             nc.vector.tensor_tensor(
                 page[n][:].indirect(idx2[:, first // PER_COLUMN : last // PER_COLUMN]),
-                y_sb[n, h, c0][:],
+                y_sb[n, u0][:],
                 wgo_sb[:, first:last],
                 MULT,
             )
@@ -293,13 +303,13 @@ def tile_list_bridge_order_forces_kernel(
                     cols = slice(HALF * k + P * c, HALF * k + P * (c + 1))
                     nc.tensor.matmul(acc[:, c, :], x0_sb[n][:, cols], ident[:], start=True, stop=False, is_transpose=True)
                     nc.tensor.matmul(acc[:, c, :], page[n][:, cols], ident[:], start=False, stop=True, is_transpose=True)
-                turned_sum[k] = ring.tile([P, 4, P], F32, name="turned_sum", align_bytes=64)
+                turned_sum[k] = sbuf([P, 4, P], F32, "turned%d" % k)
                 nc.scalar.copy(out=turned_sum[k][:], in_=acc[:])
             for k in range(2):
                 acc = bank("a", [P, 4, P])
                 for c in range(4):
                     nc.tensor.transpose(acc[:, c, :], turned_sum[k][:, c, :], ident[:])
-                result = ring.tile([P, HALF], F32, name="result", bufs=4, align_bytes=64)
+                result = sbuf([P, HALF], F32, "result%d%d" % (n, k))
                 nc.scalar.copy(out=result[:], in_=acc[:].rearrange("p c m -> p (c m)"))
                 nc.scalar.dma_start(out=out[P * n : P * (n + 1), HALF * k : HALF * (k + 1)], in_=result[:])
 
@@ -310,119 +320,107 @@ def tile_list_bridge_order_forces_kernel(
                 nc.vector.tensor_tensor(out=x0_sb[n][:, cols], in0=page[n][:, cols], in1=x0_sb[n][:, cols], op=ADD)
                 nc.sync.dma_start(out=out[P * n : P * (n + 1), cols], in_=x0_sb[n][:, cols])
 
-        v_s1 = sbuf([P, S], U8, "v_s1")
-        nc.vector.memset(v_s1[:].bitcast(I32), 0)
         for q in range(4):
             nc.vector.tensor_copy(out=tab_s[32 * q : 32 * q + 8, :].bitcast(I32), in_=tab_s_rows[32 * q : 32 * q + 8, :])
+        load_w1(0, 0, "tab_s_rows")
         v_s = sbuf([P, S], U8, "v_s")
         nc.vector.tensor_copy(v_s[:], tab_s[:].indirect(idx[:]))
-        nc.scalar.dma_start(out=v_s1[0:100, :].bitcast(I32), in_=v_s[4:104, :].bitcast(I32))
-        load_w1(0, 1, "tab_s")
+        nc.sync.dma_start(out=v_s1[0:100, :].bitcast(I32), in_=v_s[4:104, :].bitcast(I32))
+        load_w1(1, 0, "tab_s")
 
-        turned_ba = bank("a", [P, 4, P])
-        for t in range(4):
-            nc.tensor.transpose(turned_ba[:, t, :], vectors[:, t, :], ident[:])
-        turned_gn = bank("y", [P, 4, P])
-        for n in range(3):
-            nc.tensor.transpose(turned_gn[:, n, :], vectors[:, 4 + n, :], ident[:])
-        bias = sbuf([P, 4, 2], F32, "bias")
-        nc.scalar.activation(out=bias[:], in_=turned_ba[:, :, 0:2], func=IDENT)
-        gain = sbuf([P, 3], F32, "gain")
-        nc.scalar.copy(out=gain[:], in_=turned_gn[:, 0:3, 0])
-
-        gather_words(0, 0, "v_w00")
-        gather_words(0, 1, "v_w01")
-        load_w1(1, 1, "tab_w0")
-        gather_words(1, 0, "v_w10")
         order_w4(0)
         w4_s = sbuf([P, 2, H], U8, "w4_s")
         nc.gpsimd.tensor_copy(
             out=w4_s[:].bitcast(I32).rearrange("p a (b t g) -> p (a b) t g", b=2, t=4),
             in_=w4_s_raw[:].bitcast(I32).rearrange("p a (b g t) -> p (a b) t g", b=2, t=4),
         )
+        gather_words(0, 0, "v_w00")
+        gather_words(1, 0, "v_w10")
+        gather_words(0, 1, "w4_s_raw")
+        load_w1(0, 1, "tab_w0")
+        gather_words(1, 1, "v_w11")
+        load_w1(1, 1, "tab_w1")
         for chunk in chunks[: BANKS["b"]]:
             product_b(*chunk)
-        gather_words(1, 1, "v_w11")
-        load_w4(1, "w4_s_raw")
 
-        cast_w1(nc.scalar.copy, 0, 0, 0, 4)
-        load_w3(0, "w1_raw00")
-        quant_w1(0, 0, 0, 4)
-        load_w3(1, "w1_bf00")
-        for t in range(4):
-            cast_w1(nc.vector.tensor_copy if t < 2 else nc.scalar.copy, 1, 0, t, t + 1)
-        wgo_sb = sbuf([P, S], F32, "gn_row")
+        cast_w1(nc.scalar.copy, 0, 0, 0, 2)
+        cast_w1(nc.scalar.copy, 0, 0, 2, 3)
+        cast_w1(nc.vector.tensor_copy, 0, 0, 3, 4)
+        load_w4(1, "tab_s_rows")
+        quant_w1(0, 0, 0, 2)
+        quant_w1(0, 0, 2, 4)
+        load_w3(0, "w1_bf00")
+        cast_w1(nc.vector.tensor_copy, 1, 0, 0, 2)
+        cast_w1(nc.scalar.copy, 1, 0, 3, 4)
+        cast_w1(nc.vector.tensor_copy, 1, 0, 2, 3)
+        load_w3(1, "tab_s")
+        quant_w1(1, 0, 0, 2)
+        quant_w1(1, 0, 2, 4)
+        wgo_sb = sbuf([P, S], F32, "w1_bf10")
         nc.sync.dma_start(out=wgo_sb[:], in_=wgo)
-        for t in range(4):
-            quant_w1(1, 0, t, t + 1)
 
-        product_a(0, 0, 0, 2, "a_first")
-        product_a(0, 0, 2, 4, "a002")
-        cast_w1(nc.vector.tensor_copy, 0, 1, 0, 4)
-        order_w4(1)
-        quant_w1(0, 1, 0, 4)
-        product_a(0, 1, 0, 2, "a010")
-        cast_w1(nc.scalar.copy, 1, 1, 2, 4)
-        h_bf[0, 0] = sbuf([P, 4 * HALF], BF16, "tab_s")
-        product_h(0, 0, 0)
-        product_h(0, 0, 1)
-        cast_w1(nc.vector.tensor_copy, 1, 1, 0, 2)
-        product_h(0, 0, 2)
-        product_h(0, 0, 3)
+        product_a(0, 0, "a0")
+        product_a(0, 1, "a1")
+        product_h(0, 0)
+        product_h(0, 1)
+        cast_w1(nc.vector.tensor_copy, 0, 1, 0, 2)
+        cast_w1(nc.scalar.copy, 0, 1, 2, 4)
+        product_a(0, 2, "a2")
+        product_h(0, 2)
+        product_h(0, 3)
         load_x0(0, "tab_w0")
-        quant_w1(1, 1, 0, 2)
-        quant_w1(1, 1, 2, 4)
-
-        product_a(1, 0, 0, 2, "a100")
-        product_a(1, 0, 2, 4, "a102")
-        h_bf[0, 1] = sbuf([P, 4 * HALF], BF16, "h_bf01")
-        product_h(0, 1, 0)
-        quant_h(0, 0, 0, 4)
-        product_h(0, 1, 1)
-        load_x0(1, "tab_s")
-        cast_w3(0, "w3_bf0")
+        quant_w1(0, 1, 0, 4)
+        load_x0(1, "w1_bf01")
+        product_a(0, 3, "a3")
+        order_w4(1)
+        product_h(0, 4)
+        quant_h(0, 0, 2)
+        cast_w1(nc.vector.tensor_copy, 1, 1, 0, 2)
+        cast_w1(nc.scalar.copy, 1, 1, 2, 4)
+        product_h(0, 5)
+        load_x0(2, "tab_w1")
+        quant_w1(1, 1, 0, 4)
+        product_a(1, 0, "a4")
+        product_h(0, 6)
+        product_h(0, 7)
+        cast_w3(0)
+        product_a(1, 1, "a0")
+        product_h(1, 0)
+        quant_h(0, 2, 4)
+        product_h(1, 1)
         quant_w3(0)
-        h_bf[1, 0] = sbuf([P, 4 * HALF], BF16, "h_bf1")
-        product_a(0, 1, 2, 4, "a_first")
-        product_h(1, 0, 0)
-        product_h(1, 0, 1)
-        product_h(1, 0, 2)
-        quant_h(1, 0, 0, 2)
-        product_y(0, 0, 0, 2, "y")
-        product_a(1, 1, 0, 4, "a110")
-        product_h(1, 0, 3)
+        product_h(1, 2)
+        quant_h(1, 0, 1)
+        product_y(0, 0, 1, "y", "y0")
+        product_h(1, 3)
+        cast_w3(1)
         page[0] = sbuf([P, S], F32, "page0")
-        scatter(0, 0, 0, 2)
-        quant_h(1, 0, 2, 4)
-        product_y(0, 0, 2, 4, "y")
-
-        product_h(0, 1, 2)
-        product_h(0, 1, 3)
-        cast_w3(1, "a102")
-        scatter(0, 0, 2, 4)
-        quant_h(0, 1, 0, 4)
+        scatter(0, 0, 1)
+        quant_h(1, 1, 2)
+        product_y(0, 1, 2, "y", "y1")
+        product_a(1, 2, "a1")
         quant_w3(1)
-        product_y(1, 0, 0, 4, "y")
-        cast_w3(2, "a_first")
-        load_x0(2, "w1_raw00")
-        h_bf[1, 1] = sbuf([P, 4 * HALF], BF16, "h_bf1")
-        for c in range(4):
-            product_h(1, 1, c)
+        scatter(0, 1, 2)
+        product_y(1, 0, 2, "y", "y2")
+        product_a(1, 3, "a2")
+        cast_w3(2)
+        page[1] = sbuf([P, S], F32, "page1")
+        scatter(1, 0, 2)
         quant_w3(2)
-        quant_h(1, 1, 0, 4)
-
-        product_y(0, 1, 0, 4, "y")
-        product_y(2, 0, 0, 4, "b")
-        product_y(2, 1, 0, 4, "b")
-        product_y(1, 1, 0, 4, "a")
-        page[1] = sbuf([P, S], F32, "h_bf1")
-        scatter(1, 0, 0, 4)
-        scatter(0, 1, 0, 4)
-        turn["b"] = turn["b"] + 2
+        product_y(2, 0, 1, "y", "y3")
+        for c in range(4, 8):
+            product_h(1, c)
+        quant_h(1, 2, 4)
+        product_y(0, 2, 4, "a", "y4")
+        product_y(1, 2, 4, "a", "y5")
+        page[2] = sbuf([P, S], F32, "a2")
+        scatter(2, 0, 1)
+        scatter(0, 2, 4)
+        product_y(2, 1, 2, "y", "y4")
+        product_y(2, 2, 4, "a", "y6")
         finish_on_tensor(0)
-        scatter(1, 1, 0, 4)
+        scatter(1, 2, 4)
         finish_on_tensor(1)
-        page[2] = sbuf([P, S], F32, "y110")
-        scatter(2, 0, 0, 4)
-        scatter(2, 1, 0, 4)
+        scatter(2, 1, 2)
+        scatter(2, 2, 4)
         finish_on_vector(2)

@@ -48,18 +48,16 @@ def tile_list_bridge_order_forces_kernel(
 
         idx = keep.tile([P, S // PER_COLUMN], U16, name="idx")
         nc.sync.dma_start(idx[:], offs)
-        tab_s_rows = sbuf([P, T // 4], I32, "tab_s_rows")
-        for q in range(4):
-            nc.sync.dma_start(
-                out=tab_s_rows[32 * q : 32 * q + 8, :],
-                in_=tab_scales[:, 4 * q : 4 * q + 4, :].bitcast(I32),
-            )
         tab_s = sbuf([P, T], U8, "tab_s")
-        nc.vector.memset(tab_s[:].bitcast(I32), 0)
-        w4_s_raw = sbuf([P, 2, H], U8, "w4_s_raw")
-        nc.vector.memset(w4_s_raw[:].rearrange("p a c -> p (a c)").bitcast(I32), 0)
-        v_s1 = sbuf([P, S], U8, "v_s1")
-        nc.vector.memset(v_s1[:].bitcast(I32), 0)
+        nc.sync.dma_start(out=tab_s[0:32, :].bitcast(I32), in_=tab_scales.rearrange("a r c -> r a c").bitcast(I32))
+        w4_s_rows = sbuf([32, H // 4], I32, "w4_s_rows")
+        nc.sync.dma_start(out=w4_s_rows[:], in_=w4_scales.rearrange("a r c -> r a c").bitcast(I32))
+        nc.vector.memset(tab_s[32:64, :].bitcast(I32), 0)
+        nc.vector.memset(tab_s[64:128, :].bitcast(I32), 0)
+        planes = sbuf([P, 2, S + H], U8, "planes")
+        nc.vector.memset(planes[:].rearrange("p a c -> p (a c)").bitcast(I32), 0)
+        v_s = planes[:, :, 0:S]
+        w4_s = planes[:, :, S : S + H]
 
         w1_raw = {}
         w4_raw = {}
@@ -101,20 +99,14 @@ def tile_list_bridge_order_forces_kernel(
             nc.sync.dma_start(out=x0_sb[n][:], in_=x0[P * n : P * (n + 1), :])
 
         load_tab(0)
-        load_w4(0, "w4_raw0")
-        load_tab(1)
-        for q in range(4):
-            nc.sync.dma_start(
-                out=w4_s_raw[32 * q : 32 * q + 4, :, :].bitcast(I32),
-                in_=w4_scales[:, 4 * q : 4 * q + 4, :].rearrange("a r c -> r a c").bitcast(I32),
-            )
+        ba_rows = sbuf([2, PASS], F32, "ba_rows")
+        nc.sync.dma_start(out=ba_rows[:], in_=ba.rearrange("(b c) -> b c", b=2))
+        gn_row = sbuf([1, N], F32, "gn_row")
+        nc.sync.dma_start(out=gn_row[:], in_=gn.rearrange("(o n) -> o n", o=1))
         idx2 = keep.tile([P, S // PER_COLUMN], U16, name="idx2")
         nc.sync.dma_start(idx2[:], offs2)
-
-        ba_rows = sbuf([2, PASS], F32, "ba_rows")
-        nc.scalar.dma_start(out=ba_rows[:], in_=ba.rearrange("(b c) -> b c", b=2))
-        gn_row = sbuf([1, N], F32, "gn_row")
-        nc.scalar.dma_start(out=gn_row[:], in_=gn.rearrange("(o n) -> o n", o=1))
+        load_tab(1)
+        load_w4(0, "w4_raw0")
 
         ident = sbuf([P, P], F32, "ident")
         make_identity(nc, ident[:])
@@ -189,7 +181,7 @@ def tile_list_bridge_order_forces_kernel(
                             lhsT=w1_c[a, b][:, P * t : P * (t + 1)].bitcast(FP8X4),
                             lhsT_scale=w1_s[a, b][:, P * t : P * (t + 1)],
                             rhs=v_w[a, h][:, first : first + UNIT].bitcast(FP8X4),
-                            rhs_scale=v_s[4 * a : P, UNIT * u : UNIT * (u + 1)],
+                            rhs_scale=v_s[:, a, UNIT * u : UNIT * (u + 1)],
                             start=(a == 0),
                             stop=(a == 1),
                         )
@@ -197,6 +189,22 @@ def tile_list_bridge_order_forces_kernel(
                     t = 2 * pair + e
                     nc.scalar.activation(out=a_sb[b, u][:, t, :], in_=acc[:, e, :], func=IDENT, bias=bias[:, t, b : b + 1])
 
+        def first_a(a, t):
+            if a == 0:
+                first_acc[t] = bank("a" if t < 3 else "y", [P, UNIT])
+            nc.tensor.matmul_mx(
+                out=first_acc[t][:],
+                lhsT=w1_c[a, 0][:, P * t : P * (t + 1)].bitcast(FP8X4),
+                lhsT_scale=w1_s[a, 0][:, P * t : P * (t + 1)],
+                rhs=v_w[a, 0][:, 0:UNIT].bitcast(FP8X4),
+                rhs_scale=v_s[:, a, 0:UNIT],
+                start=(a == 0),
+                stop=(a == 1),
+            )
+            if a == 1:
+                nc.scalar.activation(out=a_sb[0, 0][:, t, :], in_=first_acc[t][:], func=IDENT, bias=bias[:, t, 0:1])
+
+        first_acc = {}
         b_acc = {}
 
         def product_b(b, c):
@@ -210,12 +218,12 @@ def tile_list_bridge_order_forces_kernel(
                         lhsT=w4_c[b][:, a, 2 * P * t : 2 * P * (t + 1)].bitcast(FP4X4),
                         lhsT_scale=w4_s[:, a, PASS * b + P * t : PASS * b + P * (t + 1)],
                         rhs=v_w[a, h][:, first : first + CHUNK].bitcast(FP8X4),
-                        rhs_scale=(v_s, v_s1)[a][:, CHUNK * c : CHUNK * (c + 1)],
+                        rhs_scale=v_s[:, a, CHUNK * c : CHUNK * (c + 1)],
                         start=(a == 0 and t == 0),
                         stop=(a == 1 and t == 3),
                     )
 
-        chunks = [(b, c) for b in range(2) for c in range(8)]
+        chunks = [(0, c) for c in range(6)] + [(1, c) for c in range(4)] + [(0, 6), (0, 7)] + [(1, c) for c in range(4, 8)]
         h_bf = {}
 
         def product_h(b, c):
@@ -320,78 +328,80 @@ def tile_list_bridge_order_forces_kernel(
                 nc.vector.tensor_tensor(out=x0_sb[n][:, cols], in0=page[n][:, cols], in1=x0_sb[n][:, cols], op=ADD)
                 nc.sync.dma_start(out=out[P * n : P * (n + 1), cols], in_=x0_sb[n][:, cols])
 
-        for q in range(4):
-            nc.vector.tensor_copy(out=tab_s[32 * q : 32 * q + 8, :].bitcast(I32), in_=tab_s_rows[32 * q : 32 * q + 8, :])
-        load_w1(0, 0, "tab_s_rows")
-        v_s = sbuf([P, S], U8, "v_s")
-        nc.vector.tensor_copy(v_s[:], tab_s[:].indirect(idx[:]))
-        nc.sync.dma_start(out=v_s1[0:100, :].bitcast(I32), in_=v_s[4:104, :].bitcast(I32))
-        load_w1(1, 0, "tab_s")
-
-        order_w4(0)
-        w4_s = sbuf([P, 2, H], U8, "w4_s")
-        nc.gpsimd.tensor_copy(
-            out=w4_s[:].bitcast(I32).rearrange("p a (b t g) -> p (a b) t g", b=2, t=4),
-            in_=w4_s_raw[:].bitcast(I32).rearrange("p a (b g t) -> p (a b) t g", b=2, t=4),
+        rows = sbuf([32, (S + H) // 4], I32, "rows")
+        nc.vector.tensor_copy(
+            out=rows[:, S // 4 :].rearrange("p (b t g) -> p b t g", b=2, t=4),
+            in_=w4_s_rows[:].rearrange("p (b g t) -> p b t g", b=2, t=4),
         )
+        v_rows = sbuf([P, S], U8, "v_rows")
+        nc.vector.tensor_copy(v_rows[:], tab_s[:].indirect(idx[:]))
+        nc.vector.tensor_copy(out=rows[:, 0 : S // 4], in_=v_rows[0:32, :].bitcast(I32))
+        for q in range(4):
+            nc.sync.dma_start(out=planes[32 * q : 32 * q + 4, :, :].bitcast(I32), in_=rows[8 * q : 8 * q + 8, :])
+        load_w1(0, 0, "v_rows")
+        order_w4(0)
         gather_words(0, 0, "v_w00")
+        gather_words(0, 1, "v_w01")
+        load_w1(1, 0, "tab_w0")
+        load_w4(1, "rows")
+        load_w1(0, 1, "w4_raw0")
         gather_words(1, 0, "v_w10")
-        gather_words(0, 1, "w4_s_raw")
-        load_w1(0, 1, "tab_w0")
         gather_words(1, 1, "v_w11")
         load_w1(1, 1, "tab_w1")
         for chunk in chunks[: BANKS["b"]]:
             product_b(*chunk)
 
-        cast_w1(nc.scalar.copy, 0, 0, 0, 2)
-        cast_w1(nc.scalar.copy, 0, 0, 2, 3)
-        cast_w1(nc.vector.tensor_copy, 0, 0, 3, 4)
-        load_w4(1, "tab_s_rows")
+        cast_w1(nc.scalar.copy, 0, 0, 2, 4)
+        cast_w1(nc.vector.tensor_copy, 0, 0, 0, 2)
+        load_w3(0, "v_rows")
         quant_w1(0, 0, 0, 2)
         quant_w1(0, 0, 2, 4)
-        load_w3(0, "w1_bf00")
-        cast_w1(nc.vector.tensor_copy, 1, 0, 0, 2)
+        load_w3(1, "w1_bf00")
+        for t in range(4):
+            first_a(0, t)
+        cast_w1(nc.vector.tensor_copy, 1, 0, 0, 1)
         cast_w1(nc.scalar.copy, 1, 0, 3, 4)
+        cast_w1(nc.vector.tensor_copy, 1, 0, 1, 2)
+        quant_w1(1, 0, 0, 1)
         cast_w1(nc.vector.tensor_copy, 1, 0, 2, 3)
-        load_w3(1, "tab_s")
-        quant_w1(1, 0, 0, 2)
-        quant_w1(1, 0, 2, 4)
-        wgo_sb = sbuf([P, S], F32, "w1_bf10")
+        wgo_sb = sbuf([P, S], F32, "tab_w0")
         nc.sync.dma_start(out=wgo_sb[:], in_=wgo)
+        a_sb[0, 0] = sbuf([P, 4, UNIT], F32, "a0")
+        first_a(1, 0)
+        for t in range(1, 4):
+            quant_w1(1, 0, t, t + 1)
+            first_a(1, t)
+        load_x0(0, "w1_bf10")
 
-        product_a(0, 0, "a0")
         product_a(0, 1, "a1")
         product_h(0, 0)
         product_h(0, 1)
         cast_w1(nc.vector.tensor_copy, 0, 1, 0, 2)
         cast_w1(nc.scalar.copy, 0, 1, 2, 4)
+        load_x0(1, "w4_raw0")
+        order_w4(1)
         product_a(0, 2, "a2")
         product_h(0, 2)
         product_h(0, 3)
-        load_x0(0, "tab_w0")
         quant_w1(0, 1, 0, 4)
-        load_x0(1, "w1_bf01")
-        product_a(0, 3, "a3")
-        order_w4(1)
-        product_h(0, 4)
-        quant_h(0, 0, 2)
-        cast_w1(nc.vector.tensor_copy, 1, 1, 0, 2)
         cast_w1(nc.scalar.copy, 1, 1, 2, 4)
-        product_h(0, 5)
+        cast_w1(nc.vector.tensor_copy, 1, 1, 0, 2)
         load_x0(2, "tab_w1")
-        quant_w1(1, 1, 0, 4)
-        product_a(1, 0, "a4")
-        product_h(0, 6)
-        product_h(0, 7)
+        product_h(0, 4)
+        quant_w1(1, 1, 0, 2)
+        quant_w1(1, 1, 2, 4)
+        product_a(1, 0, "a3")
+        quant_h(0, 0, 2)
+        product_h(0, 5)
+        product_a(1, 1, "a4")
         cast_w3(0)
-        product_a(1, 1, "a0")
         product_h(1, 0)
-        quant_h(0, 2, 4)
         product_h(1, 1)
-        quant_w3(0)
         product_h(1, 2)
         quant_h(1, 0, 1)
+        quant_w3(0)
         product_y(0, 0, 1, "y", "y0")
+        product_a(0, 3, "w3_bf0")
         product_h(1, 3)
         cast_w3(1)
         page[0] = sbuf([P, S], F32, "page0")
@@ -400,10 +410,13 @@ def tile_list_bridge_order_forces_kernel(
         product_y(0, 1, 2, "y", "y1")
         product_a(1, 2, "a1")
         quant_w3(1)
+        product_h(0, 6)
+        product_h(0, 7)
         scatter(0, 1, 2)
         product_y(1, 0, 2, "y", "y2")
         product_a(1, 3, "a2")
         cast_w3(2)
+        quant_h(0, 2, 4)
         page[1] = sbuf([P, S], F32, "page1")
         scatter(1, 0, 2)
         quant_w3(2)

@@ -24,6 +24,7 @@ PASS = 512
 HALF = 512
 UNIT = 256
 CHUNK = 128
+GN_ROW = 32
 PER_COLUMN = 16
 BANKS = {"a": 3, "b": 4, "y": 1}
 LAST_PIECES = 4
@@ -99,44 +100,44 @@ def tile_list_bridge_order_forces_kernel(
             nc.sync.dma_start(out=x0_sb[n][:], in_=x0[P * n : P * (n + 1), :])
 
         load_tab(0)
+        load_w4(0, "w4_raw0")
         ba_rows = sbuf([2, PASS], F32, "ba_rows")
         nc.sync.dma_start(out=ba_rows[:], in_=ba.rearrange("(b c) -> b c", b=2))
-        gn_row = sbuf([1, N], F32, "gn_row")
-        nc.sync.dma_start(out=gn_row[:], in_=gn.rearrange("(o n) -> o n", o=1))
+        gn_row = sbuf([GN_ROW + 1, N], F32, "gn_row")
+        nc.sync.dma_start(out=gn_row[GN_ROW : GN_ROW + 1, :], in_=gn.rearrange("(o n) -> o n", o=1))
         idx2 = keep.tile([P, S // PER_COLUMN], U16, name="idx2")
         nc.sync.dma_start(idx2[:], offs2)
         load_tab(1)
-        load_w4(0, "w4_raw0")
 
         ident = sbuf([P, P], F32, "ident")
         make_identity(nc, ident[:])
-        vectors = sbuf([P, 7, P], F32, "vectors")
-        nc.gpsimd.memset(vectors[:], 0.0)
+        vectors = sbuf([P, 4, P], F32, "vectors")
+        nc.vector.memset(vectors[:], 0.0)
         nc.scalar.copy(
-            out=vectors[0:2, 0:4, :].rearrange("b t (g i) -> b t g i", i=4),
+            out=vectors[0:2].rearrange("b t (g i) -> b t g i", i=4),
             in_=ba_rows[:].rearrange("b (g t i) -> b t g i", t=4, i=4),
         )
-        nc.scalar.copy(out=vectors[0:1, 4:7, :].rearrange("o n p -> o (n p)"), in_=gn_row[:])
-        turned_ba = bank("a", [P, 4, P])
+        nc.scalar.copy(
+            out=vectors[GN_ROW : GN_ROW + 1, 0:3, :].rearrange("o n p -> o (n p)"), in_=gn_row[GN_ROW : GN_ROW + 1, :]
+        )
+        turned = bank("a", [P, 4, P])
         for t in range(4):
-            nc.tensor.transpose(turned_ba[:, t, :], vectors[:, t, :], ident[:])
-        turned_gn = bank("y", [P, 4, P])
-        for n in range(3):
-            nc.tensor.transpose(turned_gn[:, n, :], vectors[:, 4 + n, :], ident[:])
+            nc.tensor.transpose(turned[:, t, :], vectors[:, t, :], ident[:])
         bias = sbuf([P, 4, 2], F32, "bias")
-        nc.scalar.activation(out=bias[:], in_=turned_ba[:, :, 0:2], func=IDENT)
+        nc.scalar.activation(out=bias[:], in_=turned[:, :, 0:2], func=IDENT)
         gain = sbuf([P, 3], F32, "gain")
-        nc.scalar.copy(out=gain[:], in_=turned_gn[:, 0:3, 0])
+        nc.scalar.copy(out=gain[:], in_=turned[:, 0:3, GN_ROW])
 
         w1_bf = {}
         w1_c = {}
         w1_s = {}
 
         def cast_w1(copy, a, b, t0, t1):
-            if (a, b) not in w1_bf:
-                w1_bf[a, b] = sbuf([P, 4 * PASS], BF16, "w1_bf%d%d" % (a, b))
+            half, first = divmod(t0, 2)
+            if (a, b, half) not in w1_bf:
+                w1_bf[a, b, half] = sbuf([P, 2 * PASS], BF16, "w1_bf%d%d%d" % (a, b, half))
             copy(
-                out=w1_bf[a, b][:, PASS * t0 : PASS * t1].rearrange("p (t g i j) -> p t g j i", t=t1 - t0, i=4, j=4),
+                out=w1_bf[a, b, half][:, PASS * first : PASS * (first + t1 - t0)].rearrange("p (t g i j) -> p t g j i", t=t1 - t0, i=4, j=4),
                 in_=w1_raw[a, b][:].rearrange("p j (g t i) -> p t g j i", t=4, i=4)[:, t0:t1],
             )
 
@@ -147,14 +148,14 @@ def tile_list_bridge_order_forces_kernel(
             nc.vector.quantize_mx(
                 out=w1_c[a, b][:, P * t0 : P * t1].bitcast(FP8X4),
                 scales=w1_s[a, b][:, P * t0 : P * t1],
-                in_=w1_bf[a, b][:, PASS * t0 : PASS * t1],
+                in_=w1_bf[a, b, t0 // 2][:, PASS * (t0 % 2) : PASS * (t0 % 2 + t1 - t0)],
             )
 
         w4_c = {}
 
-        def order_w4(b):
-            w4_c[b] = sbuf([P, 2, 2 * PASS], U8, "w4_c%d" % b)
-            nc.gpsimd.tensor_copy(
+        def order_w4(engine, b, buffer):
+            w4_c[b] = sbuf([P, 2, 2 * PASS], U8, buffer)
+            engine.tensor_copy(
                 out=w4_c[b][:].bitcast(I32).rearrange("p a (t g e) -> p a t g e", t=4, e=2),
                 in_=w4_raw[b][:].rearrange("p a (g t e) -> p a t g e", t=4, e=2),
             )
@@ -244,10 +245,10 @@ def tile_list_bridge_order_forces_kernel(
         h_c = {}
         h_s = {}
 
-        def quant_h(b, u0, u1):
+        def quant_h(b, u0, u1, buffer=None):
             h, first = divmod(UNIT * u0, HALF)
             if (b, h) not in h_c:
-                h_c[b, h] = sbuf([P, HALF], U32, "h_c%d%d" % (b, h))
+                h_c[b, h] = sbuf([P, HALF], U32, buffer or "h_c%d%d" % (b, h))
                 h_s[b, h] = sbuf([P, HALF], U8, "h_s%d%d" % (b, h))
             last = first + UNIT * (u1 - u0)
             nc.vector.quantize_mx(
@@ -339,10 +340,10 @@ def tile_list_bridge_order_forces_kernel(
         for q in range(4):
             nc.sync.dma_start(out=planes[32 * q : 32 * q + 4, :, :].bitcast(I32), in_=rows[8 * q : 8 * q + 8, :])
         load_w1(0, 0, "v_rows")
-        order_w4(0)
         gather_words(0, 0, "v_w00")
         gather_words(0, 1, "v_w01")
         load_w1(1, 0, "tab_w0")
+        order_w4(nc.vector, 0, "w4_c0")
         load_w4(1, "rows")
         load_w1(0, 1, "w4_raw0")
         gather_words(1, 0, "v_w10")
@@ -356,7 +357,7 @@ def tile_list_bridge_order_forces_kernel(
         load_w3(0, "v_rows")
         quant_w1(0, 0, 0, 2)
         quant_w1(0, 0, 2, 4)
-        load_w3(1, "w1_bf00")
+        load_w3(1, "w1_bf001")
         for t in range(4):
             first_a(0, t)
         cast_w1(nc.vector.tensor_copy, 1, 0, 0, 1)
@@ -371,28 +372,30 @@ def tile_list_bridge_order_forces_kernel(
         for t in range(1, 4):
             quant_w1(1, 0, t, t + 1)
             first_a(1, t)
-        load_x0(0, "w1_bf10")
+        load_x0(0, "w1_bf100")
 
         product_a(0, 1, "a1")
+        order_w4(nc.gpsimd, 1, "w1_bf101")
         product_h(0, 0)
         product_h(0, 1)
         cast_w1(nc.vector.tensor_copy, 0, 1, 0, 2)
         cast_w1(nc.scalar.copy, 0, 1, 2, 4)
         load_x0(1, "w4_raw0")
-        order_w4(1)
-        product_a(0, 2, "a2")
         product_h(0, 2)
         product_h(0, 3)
-        quant_w1(0, 1, 0, 4)
         cast_w1(nc.scalar.copy, 1, 1, 2, 4)
         cast_w1(nc.vector.tensor_copy, 1, 1, 0, 2)
-        load_x0(2, "tab_w1")
-        product_h(0, 4)
+        product_a(0, 2, "tab_w1")
+        quant_w1(0, 1, 0, 2)
+        quant_w1(0, 1, 2, 4)
+        load_x0(2, "w1_bf011")
         quant_w1(1, 1, 0, 2)
         quant_w1(1, 1, 2, 4)
         product_a(1, 0, "a3")
-        quant_h(0, 0, 2)
+        h_bf[0, 1] = sbuf([P, 4 * HALF], BF16, "w1_bf110")
+        product_h(0, 4)
         product_h(0, 5)
+        quant_h(0, 0, 2, "w1_bf111")
         product_a(1, 1, "a4")
         cast_w3(0)
         product_h(1, 0)

@@ -50,15 +50,15 @@ def tile_list_bridge_order_forces_kernel(
         idx = keep.tile([P, S // PER_COLUMN], U16, name="idx")
         nc.sync.dma_start(idx[:], offs)
         tab_s = sbuf([P, T], U8, "tab_s")
-        nc.sync.dma_start(out=tab_s[0:32, :].bitcast(I32), in_=tab_scales.rearrange("a r c -> r a c").bitcast(I32))
+        nc.scalar.dma_start(out=tab_s[0:32, :].bitcast(I32), in_=tab_scales.rearrange("a r c -> r a c").bitcast(I32))
         w4_s_rows = sbuf([32, H // 4], I32, "w4_s_rows")
-        nc.sync.dma_start(out=w4_s_rows[:], in_=w4_scales.rearrange("a r c -> r a c").bitcast(I32))
+        nc.scalar.dma_start(out=w4_s_rows[:], in_=w4_scales.rearrange("a r c -> r a c").bitcast(I32))
         nc.vector.memset(tab_s[32:64, :].bitcast(I32), 0)
         nc.vector.memset(tab_s[64:128, :].bitcast(I32), 0)
-        planes = sbuf([P, 2, S + H], U8, "planes")
-        nc.vector.memset(planes[:].rearrange("p a c -> p (a c)").bitcast(I32), 0)
-        v_s = planes[:, :, 0:S]
-        w4_s = planes[:, :, S : S + H]
+        planes = {}
+        for s in range(2):
+            planes[s] = sbuf([P, 2, HALF + PASS], U8, "planes%d" % s)
+            nc.vector.memset(planes[s][:].rearrange("p a c -> p (a c)").bitcast(I32), 0)
 
         w1_raw = {}
         w4_raw = {}
@@ -102,11 +102,9 @@ def tile_list_bridge_order_forces_kernel(
         load_tab(0)
         load_w4(0, "w4_raw0")
         ba_rows = sbuf([2, PASS], F32, "ba_rows")
-        nc.sync.dma_start(out=ba_rows[:], in_=ba.rearrange("(b c) -> b c", b=2))
+        nc.scalar.dma_start(out=ba_rows[:], in_=ba.rearrange("(b c) -> b c", b=2))
         gn_row = sbuf([GN_ROW + 1, N], F32, "gn_row")
-        nc.sync.dma_start(out=gn_row[GN_ROW : GN_ROW + 1, :], in_=gn.rearrange("(o n) -> o n", o=1))
-        idx2 = keep.tile([P, S // PER_COLUMN], U16, name="idx2")
-        nc.sync.dma_start(idx2[:], offs2)
+        nc.scalar.dma_start(out=gn_row[GN_ROW : GN_ROW + 1, :], in_=gn.rearrange("(o n) -> o n", o=1))
         load_tab(1)
 
         ident = sbuf([P, P], F32, "ident")
@@ -182,7 +180,7 @@ def tile_list_bridge_order_forces_kernel(
                             lhsT=w1_c[a, b][:, P * t : P * (t + 1)].bitcast(FP8X4),
                             lhsT_scale=w1_s[a, b][:, P * t : P * (t + 1)],
                             rhs=v_w[a, h][:, first : first + UNIT].bitcast(FP8X4),
-                            rhs_scale=v_s[:, a, UNIT * u : UNIT * (u + 1)],
+                            rhs_scale=planes[h][:, a, first : first + UNIT],
                             start=(a == 0),
                             stop=(a == 1),
                         )
@@ -198,7 +196,7 @@ def tile_list_bridge_order_forces_kernel(
                 lhsT=w1_c[a, 0][:, P * t : P * (t + 1)].bitcast(FP8X4),
                 lhsT_scale=w1_s[a, 0][:, P * t : P * (t + 1)],
                 rhs=v_w[a, 0][:, 0:UNIT].bitcast(FP8X4),
-                rhs_scale=v_s[:, a, 0:UNIT],
+                rhs_scale=planes[0][:, a, 0:UNIT],
                 start=(a == 0),
                 stop=(a == 1),
             )
@@ -217,9 +215,9 @@ def tile_list_bridge_order_forces_kernel(
                     nc.tensor.matmul_mx(
                         out=acc[:, t, :],
                         lhsT=w4_c[b][:, a, 2 * P * t : 2 * P * (t + 1)].bitcast(FP4X4),
-                        lhsT_scale=w4_s[:, a, PASS * b + P * t : PASS * b + P * (t + 1)],
+                        lhsT_scale=planes[b][:, a, HALF + P * t : HALF + P * (t + 1)],
                         rhs=v_w[a, h][:, first : first + CHUNK].bitcast(FP8X4),
-                        rhs_scale=v_s[:, a, CHUNK * c : CHUNK * (c + 1)],
+                        rhs_scale=planes[h][:, a, first : first + CHUNK],
                         start=(a == 0 and t == 0),
                         stop=(a == 1 and t == 3),
                     )
@@ -329,23 +327,36 @@ def tile_list_bridge_order_forces_kernel(
                 nc.vector.tensor_tensor(out=x0_sb[n][:, cols], in0=page[n][:, cols], in1=x0_sb[n][:, cols], op=ADD)
                 nc.sync.dma_start(out=out[P * n : P * (n + 1), cols], in_=x0_sb[n][:, cols])
 
-        rows = sbuf([32, (S + H) // 4], I32, "rows")
-        nc.vector.tensor_copy(
-            out=rows[:, S // 4 :].rearrange("p (b t g) -> p b t g", b=2, t=4),
-            in_=w4_s_rows[:].rearrange("p (b g t) -> p b t g", b=2, t=4),
-        )
-        v_rows = sbuf([P, S], U8, "v_rows")
-        nc.vector.tensor_copy(v_rows[:], tab_s[:].indirect(idx[:]))
-        nc.vector.tensor_copy(out=rows[:, 0 : S // 4], in_=v_rows[0:32, :].bitcast(I32))
-        for q in range(4):
-            nc.sync.dma_start(out=planes[32 * q : 32 * q + 4, :, :].bitcast(I32), in_=rows[8 * q : 8 * q + 8, :])
-        load_w1(0, 0, "v_rows")
+        v_rows = {}
+
+        def gather_scales(s):
+            v_rows[s] = sbuf([P, HALF], U8, "v_rows%d" % s)
+            entries = slice(HALF * s // PER_COLUMN, HALF * (s + 1) // PER_COLUMN)
+            nc.vector.tensor_copy(v_rows[s][:], tab_s[:].indirect(idx[:, entries]))
+
+        def deal_scales(s, buffer):
+            rows = sbuf([32, (HALF + PASS) // 4], I32, buffer)
+            nc.vector.tensor_copy(
+                out=rows[:, HALF // 4 :].rearrange("p (t g) -> p t g", t=4),
+                in_=w4_s_rows[:, P * s : P * (s + 1)].rearrange("p (g t) -> p t g", t=4),
+            )
+            nc.vector.tensor_copy(out=rows[:, 0 : HALF // 4], in_=v_rows[s][0:32, :].bitcast(I32))
+            for q in range(4):
+                nc.sync.dma_start(out=planes[s][32 * q : 32 * q + 4, :, :].bitcast(I32), in_=rows[8 * q : 8 * q + 8, :])
+
+        gather_scales(0)
+        deal_scales(0, "rows0")
+        load_w1(0, 0, "v_rows0")
+        gather_scales(1)
         gather_words(0, 0, "v_w00")
         gather_words(0, 1, "v_w01")
         load_w1(1, 0, "tab_w0")
         order_w4(nc.vector, 0, "w4_c0")
-        load_w4(1, "rows")
-        load_w1(0, 1, "w4_raw0")
+        idx2 = keep.tile([P, S // PER_COLUMN], U16, name="idx2")
+        nc.sync.dma_start(idx2[:], offs2)
+        load_w4(1, "rows0")
+        deal_scales(1, "w4_raw0")
+        load_w1(0, 1, "v_rows1")
         gather_words(1, 0, "v_w10")
         gather_words(1, 1, "v_w11")
         load_w1(1, 1, "tab_w1")
@@ -354,7 +365,7 @@ def tile_list_bridge_order_forces_kernel(
 
         cast_w1(nc.scalar.copy, 0, 0, 2, 4)
         cast_w1(nc.vector.tensor_copy, 0, 0, 0, 2)
-        load_w3(0, "v_rows")
+        load_w3(0, "v_rows0")
         quant_w1(0, 0, 0, 2)
         quant_w1(0, 0, 2, 4)
         load_w3(1, "w1_bf001")
@@ -380,7 +391,7 @@ def tile_list_bridge_order_forces_kernel(
         product_h(0, 1)
         cast_w1(nc.vector.tensor_copy, 0, 1, 0, 2)
         cast_w1(nc.scalar.copy, 0, 1, 2, 4)
-        load_x0(1, "w4_raw0")
+        load_x0(1, "v_rows1")
         product_h(0, 2)
         product_h(0, 3)
         cast_w1(nc.scalar.copy, 1, 1, 2, 4)

@@ -139,6 +139,15 @@ def tile_list_bridge_order_forces_kernel(
                 in_=w1_raw[a, b][:].rearrange("p j (g t i) -> p t g j i", t=4, i=4)[:, t0:t1],
             )
 
+        def cast_w1_gpsimd(a, b, t):
+            half, first = divmod(t, 2)
+            if (a, b, half) not in w1_bf:
+                w1_bf[a, b, half] = sbuf([P, 2 * PASS], BF16, "w1_bf%d%d%d" % (a, b, half))
+            nc.gpsimd.tensor_copy(
+                out=w1_bf[a, b, half][:, PASS * first : PASS * (first + 1)].rearrange("p (g i j) -> p g i j", i=4, j=4),
+                in_=w1_raw[a, b][:].rearrange("p j (g t i) -> p t g i j", t=4, i=4)[:, t],
+            )
+
         def quant_w1(a, b, t0, t1):
             if (a, b) not in w1_c:
                 w1_c[a, b] = sbuf([P, PASS], U32, "w1_c%d%d" % (a, b))
@@ -259,6 +268,14 @@ def tile_list_bridge_order_forces_kernel(
         w3_c = {}
         w3_s = {}
 
+        def cast_w3_gpsimd(n, buffer):
+            w3_bf[n] = sbuf([P, 2 * 4 * P], BF16, buffer)
+            for b in range(2):
+                nc.gpsimd.tensor_copy(
+                    out=w3_bf[n][:, 4 * P * b : 4 * P * (b + 1)].rearrange("p (c t) -> p c t", t=4),
+                    in_=w3_raw[b][:, :, P * n : P * (n + 1)].rearrange("p t c -> p c t"),
+                )
+
         def cast_w3(n):
             w3_bf[n] = sbuf([P, 2 * 4 * P], BF16, "w3_bf%d" % n)
             for b in range(2):
@@ -350,7 +367,7 @@ def tile_list_bridge_order_forces_kernel(
         gather_scales(1)
         gather_words(0, 0, "v_w00")
         gather_words(0, 1, "v_w01")
-        load_w1(1, 0, "tab_w0")
+        load_w1(1, 0, "tab_s")
         order_w4(nc.vector, 0, "w4_c0")
         idx2 = keep.tile([P, S // PER_COLUMN], U16, name="idx2")
         nc.sync.dma_start(idx2[:], offs2)
@@ -376,7 +393,7 @@ def tile_list_bridge_order_forces_kernel(
         cast_w1(nc.vector.tensor_copy, 1, 0, 1, 2)
         quant_w1(1, 0, 0, 1)
         cast_w1(nc.vector.tensor_copy, 1, 0, 2, 3)
-        wgo_sb = sbuf([P, S], F32, "tab_w0")
+        wgo_sb = sbuf([P, S], F32, "tab_s")
         nc.sync.dma_start(out=wgo_sb[:], in_=wgo)
         a_sb[0, 0] = sbuf([P, 4, UNIT], F32, "a0")
         first_a(1, 0)
@@ -389,8 +406,9 @@ def tile_list_bridge_order_forces_kernel(
         order_w4(nc.gpsimd, 1, "w1_bf101")
         product_h(0, 0)
         product_h(0, 1)
-        cast_w1(nc.vector.tensor_copy, 0, 1, 0, 2)
-        cast_w1(nc.scalar.copy, 0, 1, 2, 4)
+        cast_w1(nc.scalar.copy, 0, 1, 0, 2)
+        cast_w1_gpsimd(0, 1, 2)
+        cast_w1_gpsimd(0, 1, 3)
         load_x0(1, "v_rows1")
         product_h(0, 2)
         product_h(0, 3)
@@ -408,14 +426,14 @@ def tile_list_bridge_order_forces_kernel(
         product_h(0, 5)
         quant_h(0, 0, 2, "w1_bf111")
         product_a(1, 1, "a4")
-        cast_w3(0)
+        cast_w3_gpsimd(0, "h_bf00")
         product_h(1, 0)
         product_h(1, 1)
         product_h(1, 2)
         quant_h(1, 0, 1)
         quant_w3(0)
         product_y(0, 0, 1, "y", "y0")
-        product_a(0, 3, "w3_bf0")
+        product_a(0, 3, "h_bf00")
         product_h(1, 3)
         cast_w3(1)
         page[0] = sbuf([P, S], F32, "page0")

@@ -24,6 +24,7 @@ PASS = 512
 HALF = 512
 UNIT = 256
 CHUNK = 128
+SCALE_ROWS = 32
 GN_ROW = 32
 PER_COLUMN = 16
 BANKS = {"a": 3, "b": 4, "y": 1}
@@ -50,15 +51,17 @@ def tile_list_bridge_order_forces_kernel(
         idx = keep.tile([P, S // PER_COLUMN], U16, name="idx")
         nc.sync.dma_start(idx[:], offs)
         tab_s = sbuf([P, T], U8, "tab_s")
-        nc.scalar.dma_start(out=tab_s[0:32, :].bitcast(I32), in_=tab_scales.rearrange("a r c -> r a c").bitcast(I32))
-        w4_s_rows = sbuf([32, H // 4], I32, "w4_s_rows")
-        nc.scalar.dma_start(out=w4_s_rows[:], in_=w4_scales.rearrange("a r c -> r a c").bitcast(I32))
+        nc.scalar.dma_start(
+            out=tab_s[0:SCALE_ROWS, :].bitcast(I32), in_=tab_scales.rearrange("a s c -> s a c").bitcast(I32)
+        )
+        w4_s_rows = sbuf([SCALE_ROWS, H // 4], I32, "w4_s_rows")
+        nc.scalar.dma_start(out=w4_s_rows[:], in_=w4_scales.rearrange("a s c -> s a c").bitcast(I32))
         nc.vector.memset(tab_s[32:64, :].bitcast(I32), 0)
         nc.vector.memset(tab_s[64:128, :].bitcast(I32), 0)
         planes = {}
-        for s in range(2):
-            planes[s] = sbuf([P, 2, HALF + PASS], U8, "planes%d" % s)
-            nc.vector.memset(planes[s][:].rearrange("p a c -> p (a c)").bitcast(I32), 0)
+        for x in range(2):
+            planes[x] = sbuf([P, 2, HALF + PASS], U8, "planes%d" % x)
+            nc.vector.memset(planes[x][:].rearrange("p a c -> p (a c)").bitcast(I32), 0)
 
         w1_raw = {}
         w4_raw = {}
@@ -130,21 +133,21 @@ def tile_list_bridge_order_forces_kernel(
         w1_c = {}
         w1_s = {}
 
+        def rounded_w1(a, b, t0, t1):
+            pair, first = divmod(t0, 2)
+            if (a, b, pair) not in w1_bf:
+                w1_bf[a, b, pair] = sbuf([P, 2 * PASS], BF16, "w1_bf%d%d%d" % (a, b, pair))
+            return w1_bf[a, b, pair][:, PASS * first : PASS * (first + t1 - t0)]
+
         def cast_w1(copy, a, b, t0, t1):
-            half, first = divmod(t0, 2)
-            if (a, b, half) not in w1_bf:
-                w1_bf[a, b, half] = sbuf([P, 2 * PASS], BF16, "w1_bf%d%d%d" % (a, b, half))
             copy(
-                out=w1_bf[a, b, half][:, PASS * first : PASS * (first + t1 - t0)].rearrange("p (t g i j) -> p t g j i", t=t1 - t0, i=4, j=4),
+                out=rounded_w1(a, b, t0, t1).rearrange("p (t g i j) -> p t g j i", t=t1 - t0, i=4, j=4),
                 in_=w1_raw[a, b][:].rearrange("p j (g t i) -> p t g j i", t=4, i=4)[:, t0:t1],
             )
 
         def cast_w1_gpsimd(a, b, t):
-            half, first = divmod(t, 2)
-            if (a, b, half) not in w1_bf:
-                w1_bf[a, b, half] = sbuf([P, 2 * PASS], BF16, "w1_bf%d%d%d" % (a, b, half))
             nc.gpsimd.tensor_copy(
-                out=w1_bf[a, b, half][:, PASS * first : PASS * (first + 1)].rearrange("p (g i j) -> p g i j", i=4, j=4),
+                out=rounded_w1(a, b, t, t + 1).rearrange("p (g i j) -> p g i j", i=4, j=4),
                 in_=w1_raw[a, b][:].rearrange("p j (g t i) -> p t g i j", t=4, i=4)[:, t],
             )
 
@@ -155,7 +158,7 @@ def tile_list_bridge_order_forces_kernel(
             nc.vector.quantize_mx(
                 out=w1_c[a, b][:, P * t0 : P * t1].bitcast(FP8X4),
                 scales=w1_s[a, b][:, P * t0 : P * t1],
-                in_=w1_bf[a, b, t0 // 2][:, PASS * (t0 % 2) : PASS * (t0 % 2 + t1 - t0)],
+                in_=rounded_w1(a, b, t0, t1),
             )
 
         w4_c = {}
@@ -197,6 +200,8 @@ def tile_list_bridge_order_forces_kernel(
                     t = 2 * pair + e
                     nc.scalar.activation(out=a_sb[b, u][:, t, :], in_=acc[:, e, :], func=IDENT, bias=bias[:, t, b : b + 1])
 
+        first_acc = {}
+
         def first_a(a, t):
             if a == 0:
                 first_acc[t] = bank("a" if t < 3 else "y", [P, UNIT])
@@ -209,10 +214,11 @@ def tile_list_bridge_order_forces_kernel(
                 start=(a == 0),
                 stop=(a == 1),
             )
-            if a == 1:
+            if a == 1 and t < 3:
                 nc.scalar.activation(out=a_sb[0, 0][:, t, :], in_=first_acc[t][:], func=IDENT, bias=bias[:, t, 0:1])
+            if a == 1 and t == 3:
+                nc.vector.tensor_scalar_add(out=a_sb[0, 0][:, t, :], in0=first_acc[t][:], scalar1=bias[:, t, 0:1])
 
-        first_acc = {}
         b_acc = {}
 
         def product_b(b, c):
@@ -231,7 +237,12 @@ def tile_list_bridge_order_forces_kernel(
                         stop=(a == 1 and t == 3),
                     )
 
-        chunks = [(0, c) for c in range(6)] + [(1, c) for c in range(4)] + [(0, 6), (0, 7)] + [(1, c) for c in range(4, 8)]
+        chunks = (
+            [(0, c) for c in range(6)]
+            + [(1, c) for c in range(4)]
+            + [(0, c) for c in range(6, 8)]
+            + [(1, c) for c in range(4, 8)]
+        )
         h_bf = {}
 
         def product_h(b, c):
@@ -346,20 +357,20 @@ def tile_list_bridge_order_forces_kernel(
 
         v_rows = {}
 
-        def gather_scales(s):
-            v_rows[s] = sbuf([P, HALF], U8, "v_rows%d" % s)
-            entries = slice(HALF * s // PER_COLUMN, HALF * (s + 1) // PER_COLUMN)
-            nc.vector.tensor_copy(v_rows[s][:], tab_s[:].indirect(idx[:, entries]))
+        def gather_scales(h):
+            v_rows[h] = sbuf([P, HALF], U8, "v_rows%d" % h)
+            entries = slice(HALF * h // PER_COLUMN, HALF * (h + 1) // PER_COLUMN)
+            nc.vector.tensor_copy(v_rows[h][:], tab_s[:].indirect(idx[:, entries]))
 
-        def deal_scales(s, buffer):
-            rows = sbuf([32, (HALF + PASS) // 4], I32, buffer)
+        def deal_scales(x, buffer):
+            rows = sbuf([SCALE_ROWS, (HALF + PASS) // 4], I32, buffer)
             nc.vector.tensor_copy(
                 out=rows[:, HALF // 4 :].rearrange("p (t g) -> p t g", t=4),
-                in_=w4_s_rows[:, P * s : P * (s + 1)].rearrange("p (g t) -> p t g", t=4),
+                in_=w4_s_rows[:, P * x : P * (x + 1)].rearrange("p (g t) -> p t g", t=4),
             )
-            nc.vector.tensor_copy(out=rows[:, 0 : HALF // 4], in_=v_rows[s][0:32, :].bitcast(I32))
+            nc.vector.tensor_copy(out=rows[:, 0 : HALF // 4], in_=v_rows[x][0:SCALE_ROWS, :].bitcast(I32))
             for q in range(4):
-                nc.sync.dma_start(out=planes[s][32 * q : 32 * q + 4, :, :].bitcast(I32), in_=rows[8 * q : 8 * q + 8, :])
+                nc.sync.dma_start(out=planes[x][32 * q : 32 * q + 4, :, :].bitcast(I32), in_=rows[8 * q : 8 * q + 8, :])
 
         gather_scales(0)
         deal_scales(0, "rows0")
@@ -389,10 +400,10 @@ def tile_list_bridge_order_forces_kernel(
         for t in range(4):
             first_a(0, t)
         cast_w1(nc.vector.tensor_copy, 1, 0, 0, 1)
-        cast_w1(nc.scalar.copy, 1, 0, 3, 4)
+        cast_w1(nc.scalar.copy, 1, 0, 2, 3)
         cast_w1(nc.vector.tensor_copy, 1, 0, 1, 2)
+        cast_w1(nc.scalar.copy, 1, 0, 3, 4)
         quant_w1(1, 0, 0, 1)
-        cast_w1(nc.vector.tensor_copy, 1, 0, 2, 3)
         wgo_sb = sbuf([P, S], F32, "tab_s")
         nc.sync.dma_start(out=wgo_sb[:], in_=wgo)
         a_sb[0, 0] = sbuf([P, 4, UNIT], F32, "a0")
@@ -412,6 +423,7 @@ def tile_list_bridge_order_forces_kernel(
         load_x0(1, "v_rows1")
         product_h(0, 2)
         product_h(0, 3)
+
         cast_w1(nc.scalar.copy, 1, 1, 2, 4)
         cast_w1(nc.vector.tensor_copy, 1, 1, 0, 2)
         product_a(0, 2, "tab_w1")
@@ -421,12 +433,13 @@ def tile_list_bridge_order_forces_kernel(
         quant_w1(1, 1, 0, 2)
         quant_w1(1, 1, 2, 4)
         product_a(1, 0, "a3")
+        product_a(1, 1, "a4")
         h_bf[0, 1] = sbuf([P, 4 * HALF], BF16, "w1_bf110")
         product_h(0, 4)
         product_h(0, 5)
         quant_h(0, 0, 2, "w1_bf111")
-        product_a(1, 1, "a4")
         cast_w3_gpsimd(0, "h_bf00")
+
         product_h(1, 0)
         product_h(1, 1)
         product_h(1, 2)
@@ -440,6 +453,7 @@ def tile_list_bridge_order_forces_kernel(
         scatter(0, 0, 1)
         quant_h(1, 1, 2)
         product_y(0, 1, 2, "y", "y1")
+
         product_a(1, 2, "a1")
         quant_w3(1)
         product_h(0, 6)
@@ -456,6 +470,7 @@ def tile_list_bridge_order_forces_kernel(
         for c in range(4, 8):
             product_h(1, c)
         quant_h(1, 2, 4)
+
         product_y(0, 2, 4, "a", "y4")
         product_y(1, 2, 4, "a", "y5")
         page[2] = sbuf([P, S], F32, "a2")

@@ -38,6 +38,7 @@ def tile_list_bridge_order_forces_kernel(
     with ExitStack() as ctx:
         keep = ctx.enter_context(tc.tile_pool(name="keep", bufs=1))
         psum = ctx.enter_context(tc.psum_pool(name="psum", bufs=1))
+        laid = ctx.enter_context(tc.tile_pool(name="laid", bufs=1))
 
         def sbuf(shape, dtype, buffer):
             return keep.tile(shape, dtype, name=buffer, align_bytes=64)
@@ -241,7 +242,6 @@ def tile_list_bridge_order_forces_kernel(
             [(0, c) for c in range(6)]
             + [(1, c) for c in range(4)]
             + [(0, c) for c in range(6, 8)]
-            + [(1, c) for c in range(4, 8)]
         )
         h_bf = {}
 
@@ -259,6 +259,36 @@ def tile_list_bridge_order_forces_kernel(
             ahead = chunks.index((b, c)) + BANKS["b"]
             if ahead < len(chunks):
                 product_b(*chunks[ahead])
+
+        b_sb = {}
+
+        def product_b_out(b, u, buffer):
+            b_sb[b, u] = sbuf([P, 4, UNIT], F32, buffer)
+            h, first = divmod(UNIT * u, HALF)
+            for pair in range(2):
+                acc = bank("a", [P, 2, UNIT])
+                for e in range(2):
+                    t = 2 * pair + e
+                    for a in range(2):
+                        nc.tensor.matmul_mx(
+                            out=acc[:, e, :],
+                            lhsT=w4_c[b][:, a, 2 * P * t : 2 * P * (t + 1)].bitcast(FP4X4),
+                            lhsT_scale=planes[b][:, a, HALF + P * t : HALF + P * (t + 1)],
+                            rhs=v_w[a, h][:, first : first + UNIT].bitcast(FP8X4),
+                            rhs_scale=planes[h][:, a, first : first + UNIT],
+                            start=(a == 0),
+                            stop=(a == 1),
+                        )
+                nc.scalar.copy(out=b_sb[b, u][:, 2 * pair : 2 * pair + 2, :], in_=acc[:])
+
+        def product_h_gpsimd(b, u):
+            h, first = divmod(UNIT * u, HALF)
+            nc.gpsimd.tensor_tensor(
+                out=h_bf[b, h][:, 4 * first : 4 * (first + UNIT)].rearrange("p (e i t) -> p e t i", i=2, t=4),
+                in0=b_sb[b, u][:].rearrange("p t (e i) -> p e t i", i=2),
+                in1=a_sb[b, u][:].rearrange("p t (e i) -> p e t i", i=2),
+                op=MULT,
+            )
 
         h_c = {}
         h_s = {}
@@ -295,14 +325,14 @@ def tile_list_bridge_order_forces_kernel(
                     in_=w3_raw[b][:, :, P * n : P * (n + 1)].rearrange("p t (e i) -> p e t i", i=4),
                 )
 
-        def quant_w3(n):
-            w3_c[n] = sbuf([P, 2 * P], U32, "w3_c%d" % n)
+        def quant_w3(n, codes=None):
+            w3_c[n] = codes or sbuf([P, 2 * P], U32, "w3_c%d" % n)
             w3_s[n] = sbuf([P, 2 * P], U8, "w3_s%d" % n)
             nc.vector.quantize_mx(out=w3_c[n][:].bitcast(FP8X4), scales=w3_s[n][:], in_=w3_bf[n][:])
 
         y_sb = {}
 
-        def product_y(n, u0, u1, kind, buffer):
+        def product_y(n, u0, u1, kind, buffer, weighted=None):
             h, first = divmod(UNIT * u0, HALF)
             width = UNIT * (u1 - u0)
             acc = bank(kind, [P, width])
@@ -316,8 +346,19 @@ def tile_list_bridge_order_forces_kernel(
                     start=(b == 0),
                     stop=(b == 1),
                 )
-            y_sb[n, u0] = sbuf([P, width], F32, buffer)
-            nc.scalar.activation(out=y_sb[n, u0][:], in_=acc[:], func=COPY, scale=gain[:, n : n + 1])
+            if weighted is None:
+                y_sb[n, u0] = sbuf([P, width], F32, buffer)
+                nc.scalar.activation(out=y_sb[n, u0][:], in_=acc[:], func=COPY, scale=gain[:, n : n + 1])
+            else:
+                y_sb[n, u0] = weighted
+                nc.vector.scalar_tensor_tensor(
+                    out=weighted[:],
+                    in0=acc[:],
+                    scalar=gain[:, n : n + 1],
+                    in1=wgo_sb[:, UNIT * u0 : UNIT * u1],
+                    op0=MULT,
+                    op1=MULT,
+                )
 
         page = {}
 
@@ -329,6 +370,10 @@ def tile_list_bridge_order_forces_kernel(
                 wgo_sb[:, first:last],
                 MULT,
             )
+
+        def scatter_copy(n, u0, u1):
+            first, last = UNIT * u0, UNIT * u1
+            nc.vector.tensor_copy(page[n][:].indirect(idx2[:, first // PER_COLUMN : last // PER_COLUMN]), y_sb[n, u0][:])
 
         def finish_on_tensor(n):
             turned_sum = {}
@@ -452,23 +497,28 @@ def tile_list_bridge_order_forces_kernel(
         page[0] = sbuf([P, S], F32, "page0")
         scatter(0, 0, 1)
         quant_h(1, 1, 2)
-        product_y(0, 1, 2, "y", "y1")
 
         product_a(1, 2, "a1")
+        product_b_out(1, 2, "b0")
         quant_w3(1)
         product_h(0, 6)
         product_h(0, 7)
-        scatter(0, 1, 2)
-        product_y(1, 0, 2, "y", "y2")
+        product_y(0, 1, 2, "y", None, sbuf([P, UNIT], F32, "y1"))
+        h_bf[1, 1] = sbuf([P, 4 * HALF], BF16, "w3_bf1")
+        product_h_gpsimd(1, 2)
+        scatter_copy(0, 1, 2)
         product_a(1, 3, "a2")
+        product_b_out(1, 3, "b1")
+        product_h_gpsimd(1, 3)
         cast_w3(2)
-        quant_h(0, 2, 4)
+        product_y(1, 0, 2, "y", None, laid.tile([P, HALF], F32, name="y2", offset=0, align_bytes=64))
         page[1] = sbuf([P, S], F32, "page1")
-        scatter(1, 0, 2)
-        quant_w3(2)
+        scatter_copy(1, 0, 2)
+        quant_w3(2, laid.tile([P, 2 * P], U32, name="w3_c2", offset=0, align_bytes=64))
         product_y(2, 0, 1, "y", "y3")
-        for c in range(4, 8):
-            product_h(1, c)
+        h_c[0, 1] = laid.tile([P, HALF], U32, name="h_c01", offset=1024, align_bytes=64)
+        h_s[0, 1] = sbuf([P, HALF], U8, "h_s01")
+        quant_h(0, 2, 4)
         quant_h(1, 2, 4)
 
         product_y(0, 2, 4, "a", "y4")

@@ -43,6 +43,9 @@ def tile_list_bridge_order_forces_kernel(
         def sbuf(shape, dtype, buffer):
             return keep.tile(shape, dtype, name=buffer, align_bytes=64)
 
+        def over(shape, dtype, label, offset):
+            return laid.tile(shape, dtype, name=label, offset=offset, align_bytes=64)
+
         turn = {kind: 0 for kind in BANKS}
 
         def bank(kind, shape):
@@ -181,7 +184,7 @@ def tile_list_bridge_order_forces_kernel(
         a_sb = {}
 
         def product_a(b, u, buffer):
-            a_sb[b, u] = sbuf([P, 4, UNIT], F32, buffer)
+            a_sb[b, u] = sbuf([P, 4, UNIT], F32, buffer) if isinstance(buffer, str) else buffer
             h, first = divmod(UNIT * u, HALF)
             for pair in range(2):
                 acc = bank("a", [P, 2, UNIT])
@@ -241,7 +244,6 @@ def tile_list_bridge_order_forces_kernel(
         chunks = (
             [(0, c) for c in range(6)]
             + [(1, c) for c in range(4)]
-            + [(0, c) for c in range(6, 8)]
         )
         h_bf = {}
 
@@ -262,11 +264,11 @@ def tile_list_bridge_order_forces_kernel(
 
         b_sb = {}
 
-        def product_b_out(b, u, buffer):
-            b_sb[b, u] = sbuf([P, 4, UNIT], F32, buffer)
+        def product_b_out(b, u, buffer, kinds="aa"):
+            b_sb[b, u] = sbuf([P, 4, UNIT], F32, buffer) if isinstance(buffer, str) else buffer
             h, first = divmod(UNIT * u, HALF)
             for pair in range(2):
-                acc = bank("a", [P, 2, UNIT])
+                acc = bank(kinds[pair], [P, 2, UNIT])
                 for e in range(2):
                     t = 2 * pair + e
                     for a in range(2):
@@ -284,9 +286,9 @@ def tile_list_bridge_order_forces_kernel(
         def product_h_gpsimd(b, u):
             h, first = divmod(UNIT * u, HALF)
             nc.gpsimd.tensor_tensor(
-                out=h_bf[b, h][:, 4 * first : 4 * (first + UNIT)].rearrange("p (e i t) -> p e t i", i=2, t=4),
-                in0=b_sb[b, u][:].rearrange("p t (e i) -> p e t i", i=2),
-                in1=a_sb[b, u][:].rearrange("p t (e i) -> p e t i", i=2),
+                out=h_bf[b, h][:, 4 * first : 4 * (first + UNIT)].rearrange("p (e t) -> p e t", t=4),
+                in0=b_sb[b, u][:].rearrange("p t e -> p e t"),
+                in1=a_sb[b, u][:].rearrange("p t e -> p e t"),
                 op=MULT,
             )
 
@@ -309,21 +311,17 @@ def tile_list_bridge_order_forces_kernel(
         w3_c = {}
         w3_s = {}
 
-        def cast_w3_gpsimd(n, buffer):
-            w3_bf[n] = sbuf([P, 2 * 4 * P], BF16, buffer)
-            for b in range(2):
-                nc.gpsimd.tensor_copy(
-                    out=w3_bf[n][:, 4 * P * b : 4 * P * (b + 1)].rearrange("p (c t) -> p c t", t=4),
-                    in_=w3_raw[b][:, :, P * n : P * (n + 1)].rearrange("p t c -> p c t"),
-                )
+        def cast_w3_gpsimd(n, b):
+            nc.gpsimd.tensor_copy(
+                out=w3_bf[n][:, 4 * P * b : 4 * P * (b + 1)].rearrange("p (c t) -> p c t", t=4),
+                in_=w3_raw[b][:, :, P * n : P * (n + 1)].rearrange("p t c -> p c t"),
+            )
 
-        def cast_w3(n):
-            w3_bf[n] = sbuf([P, 2 * 4 * P], BF16, "w3_bf%d" % n)
-            for b in range(2):
-                nc.scalar.copy(
-                    out=w3_bf[n][:, 4 * P * b : 4 * P * (b + 1)].rearrange("p (e i t) -> p e t i", i=4, t=4),
-                    in_=w3_raw[b][:, :, P * n : P * (n + 1)].rearrange("p t (e i) -> p e t i", i=4),
-                )
+        def cast_w3(n, b):
+            nc.scalar.copy(
+                out=w3_bf[n][:, 4 * P * b : 4 * P * (b + 1)].rearrange("p (e i t) -> p e t i", i=4, t=4),
+                in_=w3_raw[b][:, :, P * n : P * (n + 1)].rearrange("p t (e i) -> p e t i", i=4),
+            )
 
         def quant_w3(n, codes=None):
             w3_c[n] = codes or sbuf([P, 2 * P], U32, "w3_c%d" % n)
@@ -332,7 +330,7 @@ def tile_list_bridge_order_forces_kernel(
 
         y_sb = {}
 
-        def product_y(n, u0, u1, kind, buffer, weighted=None):
+        def product_y(n, u0, u1, kind, plain=None, weighted=None):
             h, first = divmod(UNIT * u0, HALF)
             width = UNIT * (u1 - u0)
             acc = bank(kind, [P, width])
@@ -347,7 +345,7 @@ def tile_list_bridge_order_forces_kernel(
                     stop=(b == 1),
                 )
             if weighted is None:
-                y_sb[n, u0] = sbuf([P, width], F32, buffer)
+                y_sb[n, u0] = plain
                 nc.scalar.activation(out=y_sb[n, u0][:], in_=acc[:], func=COPY, scale=gain[:, n : n + 1])
             else:
                 y_sb[n, u0] = weighted
@@ -381,8 +379,10 @@ def tile_list_bridge_order_forces_kernel(
                 acc = bank("b", [P, 4, P])
                 for c in range(4):
                     cols = slice(HALF * k + P * c, HALF * k + P * (c + 1))
-                    nc.tensor.matmul(acc[:, c, :], x0_sb[n][:, cols], ident[:], start=True, stop=False, is_transpose=True)
-                    nc.tensor.matmul(acc[:, c, :], page[n][:, cols], ident[:], start=False, stop=True, is_transpose=True)
+                    nc.tensor.matmul(acc[:, c, :], x0_sb[n][:, cols], ident[:], start=(c == 0), stop=False, is_transpose=True)
+                for c in range(4):
+                    cols = slice(HALF * k + P * c, HALF * k + P * (c + 1))
+                    nc.tensor.matmul(acc[:, c, :], page[n][:, cols], ident[:], start=False, stop=(c == 3), is_transpose=True)
                 turned_sum[k] = sbuf([P, 4, P], F32, "turned%d" % k)
                 nc.scalar.copy(out=turned_sum[k][:], in_=acc[:])
             for k in range(2):
@@ -456,16 +456,16 @@ def tile_list_bridge_order_forces_kernel(
         for t in range(1, 4):
             quant_w1(1, 0, t, t + 1)
             first_a(1, t)
-        load_x0(0, "w1_bf100")
 
         product_a(0, 1, "a1")
         order_w4(nc.gpsimd, 1, "w1_bf101")
+        h_bf[0, 0] = over([P, 4 * HALF], BF16, "h_bf00", 2048)
         product_h(0, 0)
         product_h(0, 1)
-        cast_w1(nc.scalar.copy, 0, 1, 0, 2)
+        cast_w1(nc.scalar.copy, 0, 1, 0, 1)
+        cast_w1_gpsimd(0, 1, 1)
         cast_w1_gpsimd(0, 1, 2)
         cast_w1_gpsimd(0, 1, 3)
-        load_x0(1, "v_rows1")
         product_h(0, 2)
         product_h(0, 3)
 
@@ -479,58 +479,59 @@ def tile_list_bridge_order_forces_kernel(
         quant_w1(1, 1, 2, 4)
         product_a(1, 0, "a3")
         product_a(1, 1, "a4")
-        h_bf[0, 1] = sbuf([P, 4 * HALF], BF16, "w1_bf110")
+        quant_h(0, 0, 2, "w1_bf111")
+        h_bf[0, 1] = over([P, 4 * HALF], BF16, "h_bf01", 5632)
         product_h(0, 4)
         product_h(0, 5)
-        quant_h(0, 0, 2, "w1_bf111")
-        cast_w3_gpsimd(0, "h_bf00")
+        w3_bf[0] = over([P, 2 * PASS], BF16, "w3_bf0", 512)
+        w3_bf[2] = over([P, 2 * PASS], BF16, "w3_bf2", 3072)
+        w3_bf[1] = over([P, 2 * PASS], BF16, "w3_bf1", 13312)
+        for b in range(2):
+            cast_w3_gpsimd(0, b)
+            cast_w3_gpsimd(2, b)
+        cast_w3(1, 0)
+        cast_w3(1, 1)
 
-        product_h(1, 0)
-        product_h(1, 1)
-        product_h(1, 2)
-        quant_h(1, 0, 1)
+        for c in range(4):
+            product_h(1, c)
         quant_w3(0)
-        product_y(0, 0, 1, "y", "y0")
-        product_a(0, 3, "h_bf00")
-        product_h(1, 3)
-        cast_w3(1)
-        page[0] = sbuf([P, S], F32, "page0")
-        scatter(0, 0, 1)
-        quant_h(1, 1, 2)
+        quant_h(1, 0, 2)
+        quant_w3(2)
+        quant_w3(1, over([P, 2 * P], U32, "w3_c1", 3072))
 
-        product_a(1, 2, "a1")
-        product_b_out(1, 2, "b0")
-        quant_w3(1)
-        product_h(0, 6)
-        product_h(0, 7)
-        product_y(0, 1, 2, "y", None, sbuf([P, UNIT], F32, "y1"))
-        h_bf[1, 1] = sbuf([P, 4 * HALF], BF16, "w3_bf1")
+        for n in range(3):
+            page[n] = sbuf([P, S], F32, "page%d" % n)
+        product_y(0, 0, 2, "b", weighted=over([P, HALF], F32, "z0", 13312 - 1536))
+        scatter_copy(0, 0, 2)
+        product_y(1, 0, 2, "b", weighted=sbuf([P, HALF], F32, "z1"))
+        scatter_copy(1, 0, 2)
+        product_y(2, 0, 1, "b", weighted=over([P, UNIT], F32, "z2", 13312 + 512))
+        scatter_copy(2, 0, 1)
+        h_bf[1, 1] = over([P, 4 * HALF], BF16, "h_bf11", 13312 + 1536)
+        both = sbuf([P, 8, UNIT], F32, "w1_bf001")
+        product_a(1, 2, both[:, 0:4])
+        product_b_out(1, 2, both[:, 4:8], "ay")
         product_h_gpsimd(1, 2)
-        scatter_copy(0, 1, 2)
-        product_a(1, 3, "a2")
+        product_a(1, 3, "a1")
         product_b_out(1, 3, "b1")
         product_h_gpsimd(1, 3)
-        cast_w3(2)
-        product_y(1, 0, 2, "y", None, laid.tile([P, HALF], F32, name="y2", offset=0, align_bytes=64))
-        page[1] = sbuf([P, S], F32, "page1")
-        scatter_copy(1, 0, 2)
-        quant_w3(2, laid.tile([P, 2 * P], U32, name="w3_c2", offset=0, align_bytes=64))
-        product_y(2, 0, 1, "y", "y3")
-        h_c[0, 1] = laid.tile([P, HALF], U32, name="h_c01", offset=1024, align_bytes=64)
-        h_s[0, 1] = sbuf([P, HALF], U8, "h_s01")
+        load_x0(0, "b1")
+        load_x0(1, "a1")
+        product_a(0, 3, "a2")
+        product_b_out(0, 3, "w1_bf001")
+        product_h_gpsimd(0, 3)
         quant_h(0, 2, 4)
+        h_c[1, 1] = over([P, HALF], U32, "h_c11", 5632)
+        h_s[1, 1] = sbuf([P, HALF], U8, "h_s11")
         quant_h(1, 2, 4)
-
-        product_y(0, 2, 4, "a", "y4")
-        product_y(1, 2, 4, "a", "y5")
-        page[2] = sbuf([P, S], F32, "a2")
-        scatter(2, 0, 1)
+        product_y(2, 1, 2, "a", plain=over([P, UNIT], F32, "y21", 5632 + 2048))
+        scatter(2, 1, 2)
+        product_y(0, 2, 4, "y", plain=sbuf([P, HALF], F32, "y4"))
+        product_y(1, 2, 4, "a", plain=sbuf([P, HALF], F32, "y5"))
+        product_y(2, 2, 4, "a", plain=sbuf([P, HALF], F32, "y6"))
         scatter(0, 2, 4)
-        product_y(2, 1, 2, "y", "y4")
-        product_y(2, 2, 4, "a", "y6")
         finish_on_tensor(0)
         scatter(1, 2, 4)
         finish_on_tensor(1)
-        scatter(2, 1, 2)
         scatter(2, 2, 4)
         finish_on_vector(2)

@@ -49,6 +49,8 @@ def tile_list_bridge_order_forces_kernel(
         turn = {kind: 0 for kind in BANKS}
 
         def bank(kind, shape):
+            if kind not in BANKS:
+                return psum.tile(shape, F32, name="bank_" + kind)
             turn[kind] = turn[kind] + 1
             return psum.tile(shape, F32, name="bank_%s%d" % (kind, turn[kind] % BANKS[kind]))
 
@@ -183,11 +185,14 @@ def tile_list_bridge_order_forces_kernel(
 
         a_sb = {}
 
-        def product_a(b, u, buffer):
+        def by_lines(tile):
+            return tile[:].rearrange("p x y -> p (x y)").rearrange("p (e t i) -> p e t i", t=4, i=4)
+
+        def product_a(b, u, buffer, kinds="aa", lines=False):
             a_sb[b, u] = sbuf([P, 4, UNIT], F32, buffer) if isinstance(buffer, str) else buffer
             h, first = divmod(UNIT * u, HALF)
             for pair in range(2):
-                acc = bank("a", [P, 2, UNIT])
+                acc = bank(kinds[pair], [P, 2, UNIT])
                 for e in range(2):
                     t = 2 * pair + e
                     for a in range(2):
@@ -202,7 +207,15 @@ def tile_list_bridge_order_forces_kernel(
                         )
                 for e in range(2):
                     t = 2 * pair + e
-                    nc.scalar.activation(out=a_sb[b, u][:, t, :], in_=acc[:, e, :], func=IDENT, bias=bias[:, t, b : b + 1])
+                    if lines:
+                        nc.scalar.activation(
+                            out=by_lines(a_sb[b, u])[:, :, t, :],
+                            in_=acc[:, e, :].rearrange("p (e i) -> p e i", i=4),
+                            func=IDENT,
+                            bias=bias[:, t, b : b + 1],
+                        )
+                    else:
+                        nc.scalar.activation(out=a_sb[b, u][:, t, :], in_=acc[:, e, :], func=IDENT, bias=bias[:, t, b : b + 1])
 
         first_acc = {}
 
@@ -225,8 +238,8 @@ def tile_list_bridge_order_forces_kernel(
 
         b_acc = {}
 
-        def product_b(b, c):
-            acc = bank("b", [P, 4, CHUNK])
+        def product_b(b, c, kind="b"):
+            acc = bank(kind, [P, 4, CHUNK])
             b_acc[b, c] = acc
             h, first = divmod(CHUNK * c, HALF)
             for a in range(2):
@@ -258,9 +271,8 @@ def tile_list_bridge_order_forces_kernel(
                 in1=a_sb[b, u][:, :, in_unit : in_unit + CHUNK].rearrange("p t (e i) -> p e t i", i=4),
                 op=MULT,
             )
-            ahead = chunks.index((b, c)) + BANKS["b"]
-            if ahead < len(chunks):
-                product_b(*chunks[ahead])
+            if (b, c) in chunks[: -BANKS["b"]]:
+                product_b(*chunks[chunks.index((b, c)) + BANKS["b"]])
 
         b_sb = {}
 
@@ -281,14 +293,17 @@ def tile_list_bridge_order_forces_kernel(
                             start=(a == 0),
                             stop=(a == 1),
                         )
-                nc.scalar.copy(out=b_sb[b, u][:, 2 * pair : 2 * pair + 2, :], in_=acc[:])
+                nc.scalar.copy(
+                    out=by_lines(b_sb[b, u])[:, :, 2 * pair : 2 * pair + 2, :],
+                    in_=acc[:].rearrange("p t (e i) -> p e t i", i=4),
+                )
 
         def product_h_gpsimd(b, u):
             h, first = divmod(UNIT * u, HALF)
             nc.gpsimd.tensor_tensor(
-                out=h_bf[b, h][:, 4 * first : 4 * (first + UNIT)].rearrange("p (e t) -> p e t", t=4),
-                in0=b_sb[b, u][:].rearrange("p t e -> p e t"),
-                in1=a_sb[b, u][:].rearrange("p t e -> p e t"),
+                out=h_bf[b, h][:, 4 * first : 4 * (first + UNIT)].rearrange("p (e i t) -> p e t i", i=4, t=4),
+                in0=by_lines(b_sb[b, u]),
+                in1=by_lines(a_sb[b, u]),
                 op=MULT,
             )
 
@@ -334,15 +349,15 @@ def tile_list_bridge_order_forces_kernel(
             h, first = divmod(UNIT * u0, HALF)
             width = UNIT * (u1 - u0)
             acc = bank(kind, [P, width])
-            for b in range(2):
+            for b in (0, 1) if h == 0 else (1, 0):
                 nc.tensor.matmul_mx(
                     out=acc[:],
                     lhsT=w3_c[n][:, P * b : P * (b + 1)].bitcast(FP8X4),
                     lhsT_scale=w3_s[n][:, P * b : P * (b + 1)],
                     rhs=h_c[b, h][:, first : first + width].bitcast(FP8X4),
                     rhs_scale=h_s[b, h][:, first : first + width],
-                    start=(b == 0),
-                    stop=(b == 1),
+                    start=(b == h),
+                    stop=(b != h),
                 )
             if weighted is None:
                 y_sb[n, u0] = plain
@@ -373,20 +388,28 @@ def tile_list_bridge_order_forces_kernel(
             first, last = UNIT * u0, UNIT * u1
             nc.vector.tensor_copy(page[n][:].indirect(idx2[:, first // PER_COLUMN : last // PER_COLUMN]), y_sb[n, u0][:])
 
+        sums = {}
+
+        def open_sum(n):
+            for k in range(2):
+                sums[n, k] = psum.tile([P, 4, P], F32, name="bank_a%d" % k)
+                for c in range(4):
+                    cols = slice(HALF * k + P * c, HALF * k + P * (c + 1))
+                    nc.tensor.matmul(
+                        sums[n, k][:, c, :], x0_sb[n][:, cols], ident[:], start=(c == 0), stop=False, is_transpose=True
+                    )
+
         def finish_on_tensor(n):
             turned_sum = {}
             for k in range(2):
-                acc = bank("b", [P, 4, P])
-                for c in range(4):
-                    cols = slice(HALF * k + P * c, HALF * k + P * (c + 1))
-                    nc.tensor.matmul(acc[:, c, :], x0_sb[n][:, cols], ident[:], start=(c == 0), stop=False, is_transpose=True)
+                acc = sums[n, k]
                 for c in range(4):
                     cols = slice(HALF * k + P * c, HALF * k + P * (c + 1))
                     nc.tensor.matmul(acc[:, c, :], page[n][:, cols], ident[:], start=False, stop=(c == 3), is_transpose=True)
                 turned_sum[k] = sbuf([P, 4, P], F32, "turned%d" % k)
                 nc.scalar.copy(out=turned_sum[k][:], in_=acc[:])
             for k in range(2):
-                acc = bank("a", [P, 4, P])
+                acc = bank("b%d" % (2 * k + 1 - n), [P, 4, P])
                 for c in range(4):
                     nc.tensor.transpose(acc[:, c, :], turned_sum[k][:, c, :], ident[:])
                 result = sbuf([P, HALF], F32, "result%d%d" % (n, k))
@@ -456,16 +479,18 @@ def tile_list_bridge_order_forces_kernel(
         for t in range(1, 4):
             quant_w1(1, 0, t, t + 1)
             first_a(1, t)
+        load_x0(0, "w1_bf100")
 
         product_a(0, 1, "a1")
         order_w4(nc.gpsimd, 1, "w1_bf101")
-        h_bf[0, 0] = over([P, 4 * HALF], BF16, "h_bf00", 2048)
+        h_bf[0, 0] = over([P, 4 * HALF], BF16, "h_bf00", 5120)
         product_h(0, 0)
         product_h(0, 1)
         cast_w1(nc.scalar.copy, 0, 1, 0, 1)
         cast_w1_gpsimd(0, 1, 1)
         cast_w1_gpsimd(0, 1, 2)
         cast_w1_gpsimd(0, 1, 3)
+        load_x0(1, "v_rows1")
         product_h(0, 2)
         product_h(0, 3)
 
@@ -480,58 +505,63 @@ def tile_list_bridge_order_forces_kernel(
         product_a(1, 0, "a3")
         product_a(1, 1, "a4")
         quant_h(0, 0, 2, "w1_bf111")
-        h_bf[0, 1] = over([P, 4 * HALF], BF16, "h_bf01", 5632)
+        h_bf[0, 1] = over([P, 4 * HALF], BF16, "h_bf01", 8704)
         product_h(0, 4)
         product_h(0, 5)
-        w3_bf[0] = over([P, 2 * PASS], BF16, "w3_bf0", 512)
-        w3_bf[2] = over([P, 2 * PASS], BF16, "w3_bf2", 3072)
-        w3_bf[1] = over([P, 2 * PASS], BF16, "w3_bf1", 13312)
+        w3_two = over([P, 2, 2 * PASS], BF16, "w3_two", 2048)
+        w3_bf[0] = w3_two[:, 0]
+        w3_bf[1] = w3_two[:, 1]
         for b in range(2):
-            cast_w3_gpsimd(0, b)
-            cast_w3_gpsimd(2, b)
-        cast_w3(1, 0)
-        cast_w3(1, 1)
+            nc.gpsimd.tensor_copy(
+                out=w3_two[:, :, PASS * b : PASS * (b + 1)].rearrange("p n (c t) -> p n c t", t=4),
+                in_=w3_raw[b][:, :, 0 : 2 * P].rearrange("p t (n c) -> p n c t", n=2),
+            )
 
         for c in range(4):
             product_h(1, c)
+        product_a(1, 2, "a5", lines=True)
+        product_b_out(1, 2, "b0", ("a", "b3"))
         quant_w3(0)
         quant_h(1, 0, 2)
-        quant_w3(2)
-        quant_w3(1, over([P, 2 * P], U32, "w3_c1", 3072))
+        quant_w3(1)
 
-        for n in range(3):
+        for n in range(2):
             page[n] = sbuf([P, S], F32, "page%d" % n)
-        product_y(0, 0, 2, "b", weighted=over([P, HALF], F32, "z0", 13312 - 1536))
+        product_y(0, 0, 2, "y0", weighted=sbuf([P, HALF], F32, "z0"))
+        product_y(1, 0, 2, "b0", weighted=sbuf([P, HALF], F32, "z1"))
         scatter_copy(0, 0, 2)
-        product_y(1, 0, 2, "b", weighted=sbuf([P, HALF], F32, "z1"))
         scatter_copy(1, 0, 2)
-        product_y(2, 0, 1, "b", weighted=over([P, UNIT], F32, "z2", 13312 + 512))
-        scatter_copy(2, 0, 1)
-        h_bf[1, 1] = over([P, 4 * HALF], BF16, "h_bf11", 13312 + 1536)
-        both = sbuf([P, 8, UNIT], F32, "w1_bf001")
-        product_a(1, 2, both[:, 0:4])
-        product_b_out(1, 2, both[:, 4:8], "ay")
+        h_bf[1, 1] = over([P, 4 * HALF], BF16, "h_bf11", 4608)
         product_h_gpsimd(1, 2)
-        product_a(1, 3, "a1")
+        w3_bf[2] = sbuf([P, 2 * PASS], BF16, "b0")
+        for b in range(2):
+            cast_w3_gpsimd(2, b)
+        product_a(1, 3, over([P, 4, UNIT], F32, "a13", 16384), lines=True)
+        product_a(0, 3, "a2")
+        product_b(0, 6, "y0")
+        product_b(0, 7, "b0")
         product_b_out(1, 3, "b1")
         product_h_gpsimd(1, 3)
-        load_x0(0, "b1")
-        load_x0(1, "a1")
-        product_a(0, 3, "a2")
-        product_b_out(0, 3, "w1_bf001")
-        product_h_gpsimd(0, 3)
-        quant_h(0, 2, 4)
-        h_c[1, 1] = over([P, HALF], U32, "h_c11", 5632)
-        h_s[1, 1] = sbuf([P, HALF], U8, "h_s11")
+        product_h(0, 6)
+        product_h(0, 7)
+        open_sum(0)
+        quant_w3(2, over([P, 2 * P], U32, "w3_c2", 16384))
+        h_c[0, 1] = over([P, HALF], U32, "h_c01", 16384 + 1024)
+        h_s[0, 1] = sbuf([P, HALF], U8, "h_s01")
         quant_h(1, 2, 4)
-        product_y(2, 1, 2, "a", plain=over([P, UNIT], F32, "y21", 5632 + 2048))
-        scatter(2, 1, 2)
-        product_y(0, 2, 4, "y", plain=sbuf([P, HALF], F32, "y4"))
-        product_y(1, 2, 4, "a", plain=sbuf([P, HALF], F32, "y5"))
-        product_y(2, 2, 4, "a", plain=sbuf([P, HALF], F32, "y6"))
+        quant_h(0, 2, 4)
+        product_y(2, 0, 1, "b0", plain=sbuf([P, UNIT], F32, "y20"))
+        page[2] = sbuf([P, S], F32, "page2")
+        scatter(2, 0, 1)
+        product_y(0, 2, 4, "b3", plain=sbuf([P, HALF], F32, "y02"))
+        product_y(1, 2, 4, "b3", plain=sbuf([P, HALF], F32, "y12"))
+        product_y(2, 2, 4, "b3", plain=sbuf([P, HALF], F32, "y6"))
         scatter(0, 2, 4)
+        product_y(2, 1, 2, "y0", plain=sbuf([P, UNIT], F32, "y02"))
         finish_on_tensor(0)
+        open_sum(1)
         scatter(1, 2, 4)
         finish_on_tensor(1)
+        scatter(2, 1, 2)
         scatter(2, 2, 4)
         finish_on_vector(2)

@@ -533,25 +533,23 @@ def tile_list_bridge_order_forces_kernel(
         scatter_copy(1, 0, 2)
         h_bf[1, 1] = over([P, 4 * HALF], BF16, "h_bf11", 4608)
         product_h_gpsimd(1, 2)
-        w3_bf[2] = sbuf([P, 2 * PASS], BF16, "b0")
+        product_a(1, 3, "a6", lines=True)
+        product_b_out(1, 3, "b1")
+        w3_bf[2] = sbuf([P, 2 * PASS], BF16, "w1_bf101")
         for b in range(2):
-            cast_w3_gpsimd(2, b)
-        product_a(1, 3, over([P, 4, UNIT], F32, "a13", 16384), lines=True)
+            cast_w3(2, b)
         product_a(0, 3, "a2")
         product_b(0, 6, "y0")
         product_b(0, 7, "b0")
-        product_b_out(1, 3, "b1")
         product_h_gpsimd(1, 3)
+        quant_w3(2, sbuf([P, 2 * P], U32, "z0"))
         product_h(0, 6)
         product_h(0, 7)
         open_sum(0)
-        quant_w3(2, over([P, 2 * P], U32, "w3_c2", 16384))
-        h_c[0, 1] = over([P, HALF], U32, "h_c01", 16384 + 1024)
-        h_s[0, 1] = sbuf([P, HALF], U8, "h_s01")
         quant_h(1, 2, 4)
         quant_h(0, 2, 4)
-        product_y(2, 0, 1, "b0", plain=sbuf([P, UNIT], F32, "y20"))
-        page[2] = sbuf([P, S], F32, "page2")
+        product_y(2, 0, 1, "a2", plain=sbuf([P, UNIT], F32, "y20"))
+        page[2] = sbuf([P, S], F32, "a2")
         scatter(2, 0, 1)
         product_y(0, 2, 4, "b3", plain=sbuf([P, HALF], F32, "y02"))
         product_y(1, 2, 4, "b3", plain=sbuf([P, HALF], F32, "y12"))

@@ -151,10 +151,10 @@ def tile_list_bridge_order_forces_kernel(
                 in_=w1_raw[a, b][:].rearrange("p j (g t i) -> p t g j i", t=4, i=4)[:, t0:t1],
             )
 
-        def cast_w1_gpsimd(a, b, t):
+        def cast_w1_gpsimd(a, b, t0, t1):
             nc.gpsimd.tensor_copy(
-                out=rounded_w1(a, b, t, t + 1).rearrange("p (g i j) -> p g i j", i=4, j=4),
-                in_=w1_raw[a, b][:].rearrange("p j (g t i) -> p t g i j", t=4, i=4)[:, t],
+                out=rounded_w1(a, b, t0, t1).rearrange("p (t g i j) -> p t g i j", t=t1 - t0, i=4, j=4),
+                in_=w1_raw[a, b][:].rearrange("p j (g t i) -> p t g i j", t=4, i=4)[:, t0:t1],
             )
 
         def quant_w1(a, b, t0, t1):
@@ -392,7 +392,7 @@ def tile_list_bridge_order_forces_kernel(
 
         def open_sum(n):
             for k in range(2):
-                sums[n, k] = psum.tile([P, 4, P], F32, name="bank_a%d" % k)
+                sums[n, k] = psum.tile([P, 4, P], F32, name="bank_b%d" % (k + 1))
                 for c in range(4):
                     cols = slice(HALF * k + P * c, HALF * k + P * (c + 1))
                     nc.tensor.matmul(
@@ -409,7 +409,7 @@ def tile_list_bridge_order_forces_kernel(
                 turned_sum[k] = sbuf([P, 4, P], F32, "turned%d" % k)
                 nc.scalar.copy(out=turned_sum[k][:], in_=acc[:])
             for k in range(2):
-                acc = bank("b%d" % (2 * k + 1 - n), [P, 4, P])
+                acc = bank((("a0", "a1"), ("b0", "b3"))[n][k], [P, 4, P])
                 for c in range(4):
                     nc.tensor.transpose(acc[:, c, :], turned_sum[k][:, c, :], ident[:])
                 result = sbuf([P, HALF], F32, "result%d%d" % (n, k))
@@ -486,10 +486,8 @@ def tile_list_bridge_order_forces_kernel(
         h_bf[0, 0] = over([P, 4 * HALF], BF16, "h_bf00", 5120)
         product_h(0, 0)
         product_h(0, 1)
-        cast_w1(nc.scalar.copy, 0, 1, 0, 1)
-        cast_w1_gpsimd(0, 1, 1)
-        cast_w1_gpsimd(0, 1, 2)
-        cast_w1_gpsimd(0, 1, 3)
+        cast_w1(nc.scalar.copy, 0, 1, 0, 2)
+        cast_w1_gpsimd(0, 1, 2, 4)
         load_x0(1, "v_rows1")
         product_h(0, 2)
         product_h(0, 3)
@@ -498,9 +496,9 @@ def tile_list_bridge_order_forces_kernel(
         cast_w1(nc.vector.tensor_copy, 1, 1, 0, 2)
         product_a(0, 2, "tab_w1")
         quant_w1(0, 1, 0, 2)
+        quant_w1(1, 1, 0, 2)
         quant_w1(0, 1, 2, 4)
         load_x0(2, "w1_bf011")
-        quant_w1(1, 1, 0, 2)
         quant_w1(1, 1, 2, 4)
         product_a(1, 0, "a3")
         product_a(1, 1, "a4")
@@ -519,8 +517,8 @@ def tile_list_bridge_order_forces_kernel(
 
         for c in range(4):
             product_h(1, c)
-        product_a(1, 2, "a5", lines=True)
-        product_b_out(1, 2, "b0", ("a", "b3"))
+        product_a(1, 2, "a5", ("b3", "b0"), lines=True)
+        product_b_out(1, 2, "b0", ("b1", "b2"))
         quant_w3(0)
         quant_h(1, 0, 2)
         quant_w3(1)
@@ -528,19 +526,19 @@ def tile_list_bridge_order_forces_kernel(
         for n in range(2):
             page[n] = sbuf([P, S], F32, "page%d" % n)
         product_y(0, 0, 2, "y0", weighted=sbuf([P, HALF], F32, "z0"))
-        product_y(1, 0, 2, "b0", weighted=sbuf([P, HALF], F32, "z1"))
+        product_y(1, 0, 2, "a1", weighted=sbuf([P, HALF], F32, "z1"))
         scatter_copy(0, 0, 2)
         scatter_copy(1, 0, 2)
         h_bf[1, 1] = over([P, 4 * HALF], BF16, "h_bf11", 4608)
         product_h_gpsimd(1, 2)
-        product_a(1, 3, "a6", lines=True)
-        product_b_out(1, 3, "b1")
+        product_a(1, 3, "a6", ("b3", "b0"), lines=True)
+        product_b_out(1, 3, "b1", ("b1", "b2"))
         w3_bf[2] = sbuf([P, 2 * PASS], BF16, "w1_bf101")
         for b in range(2):
             cast_w3(2, b)
-        product_a(0, 3, "a2")
+        product_a(0, 3, "a2", ("b3", "b0"))
         product_b(0, 6, "y0")
-        product_b(0, 7, "b0")
+        product_b(0, 7, "a1")
         product_h_gpsimd(1, 3)
         quant_w3(2, sbuf([P, 2 * P], U32, "z0"))
         product_h(0, 6)
@@ -548,12 +546,12 @@ def tile_list_bridge_order_forces_kernel(
         open_sum(0)
         quant_h(1, 2, 4)
         quant_h(0, 2, 4)
-        product_y(2, 0, 1, "a2", plain=sbuf([P, UNIT], F32, "y20"))
+        product_y(2, 0, 1, "b3", plain=sbuf([P, UNIT], F32, "y20"))
         page[2] = sbuf([P, S], F32, "a2")
         scatter(2, 0, 1)
-        product_y(0, 2, 4, "b3", plain=sbuf([P, HALF], F32, "y02"))
-        product_y(1, 2, 4, "b3", plain=sbuf([P, HALF], F32, "y12"))
-        product_y(2, 2, 4, "b3", plain=sbuf([P, HALF], F32, "y6"))
+        product_y(0, 2, 4, "a2", plain=sbuf([P, HALF], F32, "y02"))
+        product_y(1, 2, 4, "a2", plain=sbuf([P, HALF], F32, "y12"))
+        product_y(2, 2, 4, "a2", plain=sbuf([P, HALF], F32, "y6"))
         scatter(0, 2, 4)
         product_y(2, 1, 2, "y0", plain=sbuf([P, UNIT], F32, "y02"))
         finish_on_tensor(0)

@@ -392,7 +392,7 @@ def tile_list_bridge_order_forces_kernel(
 
         def open_sum(n):
             for k in range(2):
-                sums[n, k] = psum.tile([P, 4, P], F32, name="bank_b%d" % (k + 1))
+                sums[n, k] = bank((("b1", "b2"), ("b0", "b3"))[n][k], [P, 4, P])
                 for c in range(4):
                     cols = slice(HALF * k + P * c, HALF * k + P * (c + 1))
                     nc.tensor.matmul(
@@ -409,7 +409,7 @@ def tile_list_bridge_order_forces_kernel(
                 turned_sum[k] = sbuf([P, 4, P], F32, "turned%d" % k)
                 nc.scalar.copy(out=turned_sum[k][:], in_=acc[:])
             for k in range(2):
-                acc = bank((("a0", "a1"), ("b0", "b3"))[n][k], [P, 4, P])
+                acc = bank((("a0", "a1"), ("b1", "b2"))[n][k], [P, 4, P])
                 for c in range(4):
                     nc.tensor.transpose(acc[:, c, :], turned_sum[k][:, c, :], ident[:])
                 result = sbuf([P, HALF], F32, "result%d%d" % (n, k))
@@ -552,10 +552,10 @@ def tile_list_bridge_order_forces_kernel(
         product_y(0, 2, 4, "a2", plain=sbuf([P, HALF], F32, "y02"))
         product_y(1, 2, 4, "a2", plain=sbuf([P, HALF], F32, "y12"))
         product_y(2, 2, 4, "a2", plain=sbuf([P, HALF], F32, "y6"))
+        open_sum(1)
         scatter(0, 2, 4)
         product_y(2, 1, 2, "y0", plain=sbuf([P, UNIT], F32, "y02"))
         finish_on_tensor(0)
-        open_sum(1)
         scatter(1, 2, 4)
         finish_on_tensor(1)
         scatter(2, 1, 2)

@@ -260,15 +260,21 @@ def tile_list_bridge_order_forces_kernel(
         )
         h_bf = {}
 
-        def product_h(b, c):
-            h, first = divmod(CHUNK * c, HALF)
-            if (b, h) not in h_bf:
-                h_bf[b, h] = sbuf([P, 4 * HALF], BF16, "h_bf%d%d" % (b, h))
+        def rounded_h(b, entry, count):
+            u = max(key[1] for key in h_bf if key[0] == b and UNIT * key[1] <= entry)
+            first = entry - UNIT * u
+            return h_bf[b, u][:, 4 * first : 4 * (first + count)]
+
+        def product_h(b, c, lines=False):
             u, in_unit = divmod(CHUNK * c, UNIT)
+            if lines:
+                a_part = by_lines(a_sb[b, u])[:, in_unit // 4 : (in_unit + CHUNK) // 4]
+            else:
+                a_part = a_sb[b, u][:, :, in_unit : in_unit + CHUNK].rearrange("p t (e i) -> p e t i", i=4)
             nc.vector.tensor_tensor(
-                out=h_bf[b, h][:, 4 * first : 4 * (first + CHUNK)].rearrange("p (e i t) -> p e t i", i=4, t=4),
+                out=rounded_h(b, CHUNK * c, CHUNK).rearrange("p (e i t) -> p e t i", i=4, t=4),
                 in0=b_acc[b, c][:].rearrange("p t (e i) -> p e t i", i=4),
-                in1=a_sb[b, u][:, :, in_unit : in_unit + CHUNK].rearrange("p t (e i) -> p e t i", i=4),
+                in1=a_part,
                 op=MULT,
             )
             if (b, c) in chunks[: -BANKS["b"]]:
@@ -298,12 +304,12 @@ def tile_list_bridge_order_forces_kernel(
                     in_=acc[:].rearrange("p t (e i) -> p e t i", i=4),
                 )
 
-        def product_h_gpsimd(b, u):
-            h, first = divmod(UNIT * u, HALF)
+        def product_h_gpsimd(b, entry, count, b_lines):
+            u, in_unit = divmod(entry, UNIT)
             nc.gpsimd.tensor_tensor(
-                out=h_bf[b, h][:, 4 * first : 4 * (first + UNIT)].rearrange("p (e i t) -> p e t i", i=4, t=4),
-                in0=by_lines(b_sb[b, u]),
-                in1=by_lines(a_sb[b, u]),
+                out=rounded_h(b, entry, count).rearrange("p (e i t) -> p e t i", i=4, t=4),
+                in0=b_lines,
+                in1=by_lines(a_sb[b, u])[:, in_unit // 4 : (in_unit + count) // 4],
                 op=MULT,
             )
 
@@ -319,7 +325,7 @@ def tile_list_bridge_order_forces_kernel(
             nc.vector.quantize_mx(
                 out=h_c[b, h][:, first:last].bitcast(FP8X4),
                 scales=h_s[b, h][:, first:last],
-                in_=h_bf[b, h][:, 4 * first : 4 * last],
+                in_=rounded_h(b, UNIT * u0, UNIT * (u1 - u0)),
             )
 
         w3_bf = {}
@@ -503,7 +509,7 @@ def tile_list_bridge_order_forces_kernel(
         product_a(1, 0, "a3")
         product_a(1, 1, "a4")
         quant_h(0, 0, 2, "w1_bf111")
-        h_bf[0, 1] = over([P, 4 * HALF], BF16, "h_bf01", 8704)
+        h_bf[0, 2] = over([P, 4 * UNIT], BF16, "h_bf02", 8704)
         product_h(0, 4)
         product_h(0, 5)
         w3_two = over([P, 2, 2 * PASS], BF16, "w3_two", 2048)
@@ -515,12 +521,14 @@ def tile_list_bridge_order_forces_kernel(
                 in_=w3_raw[b][:, :, 0 : 2 * P].rearrange("p t (n c) -> p n c t", n=2),
             )
 
+        h_bf[1, 0] = sbuf([P, 4 * HALF], BF16, "h_bf10")
         for c in range(4):
             product_h(1, c)
         product_a(1, 2, "a5", ("b3", "b0"), lines=True)
         product_b_out(1, 2, "b0", ("b1", "b2"))
         quant_w3(0)
         quant_h(1, 0, 2)
+        quant_h(0, 2, 3, "h_bf10")
         quant_w3(1)
 
         for n in range(2):
@@ -529,8 +537,8 @@ def tile_list_bridge_order_forces_kernel(
         product_y(1, 0, 2, "a1", weighted=sbuf([P, HALF], F32, "z1"))
         scatter_copy(0, 0, 2)
         scatter_copy(1, 0, 2)
-        h_bf[1, 1] = over([P, 4 * HALF], BF16, "h_bf11", 4608)
-        product_h_gpsimd(1, 2)
+        h_bf[1, 2] = over([P, 4 * HALF], BF16, "h_bf12", 4672)
+        product_h_gpsimd(1, 2 * UNIT, UNIT, by_lines(b_sb[1, 2]))
         product_a(1, 3, "a6", ("b3", "b0"), lines=True)
         product_b_out(1, 3, "b1", ("b1", "b2"))
         w3_bf[2] = sbuf([P, 2 * PASS], BF16, "w1_bf101")
@@ -539,13 +547,14 @@ def tile_list_bridge_order_forces_kernel(
         product_a(0, 3, "a2", ("b3", "b0"))
         product_b(0, 6, "y0")
         product_b(0, 7, "a1")
-        product_h_gpsimd(1, 3)
+        product_h_gpsimd(1, 3 * UNIT, UNIT, by_lines(b_sb[1, 3]))
         quant_w3(2, sbuf([P, 2 * P], U32, "z0"))
+        h_bf[0, 3] = sbuf([P, 4 * UNIT], BF16, "h_bf03")
         product_h(0, 6)
         product_h(0, 7)
         open_sum(0)
         quant_h(1, 2, 4)
-        quant_h(0, 2, 4)
+        quant_h(0, 3, 4)
         product_y(2, 0, 1, "b3", plain=sbuf([P, UNIT], F32, "y20"))
         page[2] = sbuf([P, S], F32, "a2")
         scatter(2, 0, 1)

@@ -127,7 +127,7 @@ def tile_list_bridge_order_forces_kernel(
         nc.scalar.copy(
             out=vectors[GN_ROW : GN_ROW + 1, 0:3, :].rearrange("o n p -> o (n p)"), in_=gn_row[GN_ROW : GN_ROW + 1, :]
         )
-        turned = bank("a", [P, 4, P])
+        turned = bank("a1", [P, 4, P])
         for t in range(4):
             nc.tensor.transpose(turned[:, t, :], vectors[:, t, :], ident[:])
         bias = sbuf([P, 4, 2], F32, "bias")
@@ -188,53 +188,64 @@ def tile_list_bridge_order_forces_kernel(
         def by_lines(tile):
             return tile[:].rearrange("p x y -> p (x y)").rearrange("p (e t i) -> p e t i", t=4, i=4)
 
-        def product_a(b, u, buffer, kinds="aa", lines=False):
-            a_sb[b, u] = sbuf([P, 4, UNIT], F32, buffer) if isinstance(buffer, str) else buffer
+        a_acc = {}
+
+        def sums_a(b, u, pair, kind):
             h, first = divmod(UNIT * u, HALF)
+            acc = bank(kind, [P, 2, UNIT])
+            a_acc[b, u, pair] = acc
+            for e in range(2):
+                t = 2 * pair + e
+                for a in range(2):
+                    nc.tensor.matmul_mx(
+                        out=acc[:, e, :],
+                        lhsT=w1_c[a, b][:, P * t : P * (t + 1)].bitcast(FP8X4),
+                        lhsT_scale=w1_s[a, b][:, P * t : P * (t + 1)],
+                        rhs=v_w[a, h][:, first : first + UNIT].bitcast(FP8X4),
+                        rhs_scale=planes[h][:, a, first : first + UNIT],
+                        start=(a == 0),
+                        stop=(a == 1),
+                    )
+
+        def empty_a(b, u, pair, lines=False):
+            for e in range(2):
+                t = 2 * pair + e
+                if lines:
+                    nc.scalar.activation(
+                        out=by_lines(a_sb[b, u])[:, :, t, :],
+                        in_=a_acc[b, u, pair][:, e, :].rearrange("p (e i) -> p e i", i=4),
+                        func=IDENT,
+                        bias=bias[:, t, b : b + 1],
+                    )
+                else:
+                    nc.scalar.activation(
+                        out=a_sb[b, u][:, t, :], in_=a_acc[b, u, pair][:, e, :], func=IDENT, bias=bias[:, t, b : b + 1]
+                    )
+
+        def product_a(b, u, buffer, kinds, lines=False):
+            a_sb[b, u] = sbuf([P, 4, UNIT], F32, buffer)
             for pair in range(2):
-                acc = bank(kinds[pair], [P, 2, UNIT])
-                for e in range(2):
-                    t = 2 * pair + e
-                    for a in range(2):
-                        nc.tensor.matmul_mx(
-                            out=acc[:, e, :],
-                            lhsT=w1_c[a, b][:, P * t : P * (t + 1)].bitcast(FP8X4),
-                            lhsT_scale=w1_s[a, b][:, P * t : P * (t + 1)],
-                            rhs=v_w[a, h][:, first : first + UNIT].bitcast(FP8X4),
-                            rhs_scale=planes[h][:, a, first : first + UNIT],
-                            start=(a == 0),
-                            stop=(a == 1),
-                        )
-                for e in range(2):
-                    t = 2 * pair + e
-                    if lines:
-                        nc.scalar.activation(
-                            out=by_lines(a_sb[b, u])[:, :, t, :],
-                            in_=acc[:, e, :].rearrange("p (e i) -> p e i", i=4),
-                            func=IDENT,
-                            bias=bias[:, t, b : b + 1],
-                        )
-                    else:
-                        nc.scalar.activation(out=a_sb[b, u][:, t, :], in_=acc[:, e, :], func=IDENT, bias=bias[:, t, b : b + 1])
+                sums_a(b, u, pair, kinds[pair])
+                empty_a(b, u, pair, lines)
 
         first_acc = {}
 
         def first_a(a, t):
             if a == 0:
-                first_acc[t] = bank("a" if t < 3 else "y", [P, UNIT])
+                first_acc[t] = bank(("a2", "a0", "a1", "y0")[t], [P, HALF])
             nc.tensor.matmul_mx(
                 out=first_acc[t][:],
                 lhsT=w1_c[a, 0][:, P * t : P * (t + 1)].bitcast(FP8X4),
                 lhsT_scale=w1_s[a, 0][:, P * t : P * (t + 1)],
-                rhs=v_w[a, 0][:, 0:UNIT].bitcast(FP8X4),
-                rhs_scale=planes[0][:, a, 0:UNIT],
+                rhs=v_w[a, 0][:].bitcast(FP8X4),
+                rhs_scale=planes[0][:, a, 0:HALF],
                 start=(a == 0),
                 stop=(a == 1),
             )
-            if a == 1 and t < 3:
-                nc.scalar.activation(out=a_sb[0, 0][:, t, :], in_=first_acc[t][:], func=IDENT, bias=bias[:, t, 0:1])
-            if a == 1 and t == 3:
-                nc.vector.tensor_scalar_add(out=a_sb[0, 0][:, t, :], in0=first_acc[t][:], scalar1=bias[:, t, 0:1])
+            if a == 1 and t < 2:
+                nc.scalar.activation(out=a_sb[0, 0][:, t, :], in_=first_acc[t][:, 0:UNIT], func=IDENT, bias=bias[:, t, 0:1])
+            if a == 1 and t >= 2:
+                nc.vector.tensor_scalar_add(out=a_sb[0, 0][:, t, :], in0=first_acc[t][:, 0:UNIT], scalar1=bias[:, t, 0:1])
 
         b_acc = {}
 
@@ -487,7 +498,11 @@ def tile_list_bridge_order_forces_kernel(
             first_a(1, t)
         load_x0(0, "w1_bf100")
 
-        product_a(0, 1, "a1")
+        a_sb[0, 1] = sbuf([P, 4, UNIT], F32, "a1")
+        for t in range(4):
+            nc.scalar.activation(out=a_sb[0, 1][:, t, :], in_=first_acc[t][:, UNIT:HALF], func=IDENT, bias=bias[:, t, 0:1])
+        sums_a(0, 2, 0, "a2")
+        sums_a(0, 2, 1, "a0")
         order_w4(nc.gpsimd, 1, "w1_bf101")
         h_bf[0, 0] = over([P, 4 * HALF], BF16, "h_bf00", 5120)
         product_h(0, 0)
@@ -500,14 +515,16 @@ def tile_list_bridge_order_forces_kernel(
 
         cast_w1(nc.scalar.copy, 1, 1, 2, 4)
         cast_w1(nc.vector.tensor_copy, 1, 1, 0, 2)
-        product_a(0, 2, "tab_w1")
+        a_sb[0, 2] = sbuf([P, 4, UNIT], F32, "tab_w1")
+        for pair in range(2):
+            empty_a(0, 2, pair)
         quant_w1(0, 1, 0, 2)
         quant_w1(1, 1, 0, 2)
         quant_w1(0, 1, 2, 4)
         load_x0(2, "w1_bf011")
         quant_w1(1, 1, 2, 4)
-        product_a(1, 0, "a3")
-        product_a(1, 1, "a4")
+        product_a(1, 0, "a3", ("a1", "y0"))
+        product_a(1, 1, "a4", ("a2", "a0"))
         quant_h(0, 0, 2, "w1_bf111")
         h_bf[0, 2] = over([P, 4 * UNIT], BF16, "h_bf02", 8704)
         product_h(0, 4)

from contextlib import ExitStack

import concourse.mybir as mybir
from concourse.masks import make_identity

K, H, N, T, S = 1024, 1024, 384, 2048, 1024
FLOPS = 2 * K * H * S * 2 + 2 * H * N * S

F32 = mybir.dt.float32
BF16 = mybir.dt.bfloat16
I32 = mybir.dt.int32
U32 = mybir.dt.uint32
U16 = mybir.dt.uint16
U8 = mybir.dt.uint8
FP8X4 = mybir.dt.float8_e4m3fn_x4
FP4X4 = mybir.dt.float4_e2m1fn_x4
MULT = mybir.AluOpType.mult
ADD = mybir.AluOpType.add
IDENT = mybir.ActivationFunctionType.Identity
COPY = mybir.ActivationFunctionType.Copy

P = 128
PASS = 512
HALF = 512
UNIT = 256
CHUNK = 128
SCALE_ROWS = 32
GN_ROW = 32
PER_COLUMN = 16
BANKS = {"a": 3, "b": 4, "y": 1}
LAST_PIECES = 4


def tile_list_bridge_order_forces_kernel(
    tc, tab_words, tab_scales, offs, w1, ba, w4_words, w4_scales, w3, offs2, wgo, gn, x0, out
):
    nc = tc.nc
    with ExitStack() as ctx:
        keep = ctx.enter_context(tc.tile_pool(name="keep", bufs=1))
        psum = ctx.enter_context(tc.psum_pool(name="psum", bufs=1))
        laid = ctx.enter_context(tc.tile_pool(name="laid", bufs=1))

        def sbuf(shape, dtype, buffer):
            return keep.tile(shape, dtype, name=buffer, align_bytes=64)

        def over(shape, dtype, label, offset):
            return laid.tile(shape, dtype, name=label, offset=offset, align_bytes=64)

        turn = {kind: 0 for kind in BANKS}

        def bank(kind, shape):
            if kind not in BANKS:
                return psum.tile(shape, F32, name="bank_" + kind)
            turn[kind] = turn[kind] + 1
            return psum.tile(shape, F32, name="bank_%s%d" % (kind, turn[kind] % BANKS[kind]))

        idx = keep.tile([P, S // PER_COLUMN], U16, name="idx")
        nc.sync.dma_start(idx[:], offs)
        tab_s = sbuf([P, T], U8, "tab_s")
        nc.scalar.dma_start(
            out=tab_s[0:SCALE_ROWS, :].bitcast(I32), in_=tab_scales.rearrange("a s c -> s a c").bitcast(I32)
        )
        w4_s_rows = sbuf([SCALE_ROWS, H // 4], I32, "w4_s_rows")
        nc.scalar.dma_start(out=w4_s_rows[:], in_=w4_scales.rearrange("a s c -> s a c").bitcast(I32))
        nc.vector.memset(tab_s[32:64, :].bitcast(I32), 0)
        nc.vector.memset(tab_s[64:128, :].bitcast(I32), 0)
        planes = {}
        for x in range(2):
            planes[x] = sbuf([P, 2, HALF + PASS], U8, "planes%d" % x)
            nc.vector.memset(planes[x][:].rearrange("p a c -> p (a c)").bitcast(I32), 0)

        w1_raw = {}
        w4_raw = {}
        tab_w = {}
        w3_raw = {}
        x0_sb = {}

        def load_w1(a, b, buffer):
            w1_raw[a, b] = sbuf([P, 4, PASS], F32, buffer)
            nc.sync.dma_start(
                out=w1_raw[a, b][:],
                in_=w1[PASS * a : PASS * (a + 1), PASS * b : PASS * (b + 1)].rearrange("(p j) c -> p j c", j=4),
            )

        def load_w4(b, buffer):
            w4_raw[b] = sbuf([P, 2, PASS // 2], I32, buffer)
            nc.sync.dma_start(
                out=w4_raw[b][:],
                in_=w4_words[:, :, 2 * PASS * b : 2 * PASS * (b + 1)].rearrange("a p c -> p a c").bitcast(I32),
            )

        def load_tab(a):
            tab_w[a] = sbuf([P, T], U32, "tab_w%d" % a)
            nc.sync.dma_start(
                out=tab_w[a][:].bitcast(I32),
                in_=tab_words[a].rearrange("p t i -> p (t i)").bitcast(I32),
            )

        def load_w3(b, buffer):
            w3_raw[b] = sbuf([P, 4, N], F32, buffer)
            for t in range(4):
                nc.sync.dma_start(
                    out=w3_raw[b][:, t, :],
                    in_=w3[PASS * b : PASS * (b + 1), :].rearrange("(g t i) n -> t g i n", t=4, i=4)[t],
                )

        def load_x0(n, buffer):
            x0_sb[n] = sbuf([P, S], F32, buffer)
            nc.sync.dma_start(out=x0_sb[n][:], in_=x0[P * n : P * (n + 1), :])

        load_tab(0)
        load_w4(0, "w4_raw0")
        ba_rows = sbuf([2, PASS], F32, "ba_rows")
        nc.scalar.dma_start(out=ba_rows[:], in_=ba.rearrange("(b c) -> b c", b=2))
        gn_row = sbuf([GN_ROW + 1, N], F32, "gn_row")
        nc.scalar.dma_start(out=gn_row[GN_ROW : GN_ROW + 1, :], in_=gn.rearrange("(o n) -> o n", o=1))
        load_tab(1)

        ident = sbuf([P, P], F32, "ident")
        make_identity(nc, ident[:])
        vectors = sbuf([P, 4, P], F32, "vectors")
        nc.vector.memset(vectors[:], 0.0)
        nc.scalar.copy(
            out=vectors[0:2].rearrange("b t (g i) -> b t g i", i=4),
            in_=ba_rows[:].rearrange("b (g t i) -> b t g i", t=4, i=4),
        )
        nc.scalar.copy(
            out=vectors[GN_ROW : GN_ROW + 1, 0:3, :].rearrange("o n p -> o (n p)"), in_=gn_row[GN_ROW : GN_ROW + 1, :]
        )
        turned = bank("a1", [P, 4, P])
        for t in range(4):
            nc.tensor.transpose(turned[:, t, :], vectors[:, t, :], ident[:])
        bias = sbuf([P, 4, 2], F32, "bias")
        nc.scalar.activation(out=bias[:], in_=turned[:, :, 0:2], func=IDENT)
        gain = sbuf([P, 3], F32, "gain")
        nc.scalar.copy(out=gain[:], in_=turned[:, 0:3, GN_ROW])

        w1_bf = {}
        w1_c = {}
        w1_s = {}

        def rounded_w1(a, b, t0, t1):
            pair, first = divmod(t0, 2)
            if (a, b, pair) not in w1_bf:
                w1_bf[a, b, pair] = sbuf([P, 2 * PASS], BF16, "w1_bf%d%d%d" % (a, b, pair))
            return w1_bf[a, b, pair][:, PASS * first : PASS * (first + t1 - t0)]

        def cast_w1(copy, a, b, t0, t1):
            copy(
                out=rounded_w1(a, b, t0, t1).rearrange("p (t g i j) -> p t g j i", t=t1 - t0, i=4, j=4),
                in_=w1_raw[a, b][:].rearrange("p j (g t i) -> p t g j i", t=4, i=4)[:, t0:t1],
            )

        def cast_w1_gpsimd(a, b, t0, t1):
            nc.gpsimd.tensor_copy(
                out=rounded_w1(a, b, t0, t1).rearrange("p (t g i j) -> p t g i j", t=t1 - t0, i=4, j=4),
                in_=w1_raw[a, b][:].rearrange("p j (g t i) -> p t g i j", t=4, i=4)[:, t0:t1],
            )

        def quant_w1(a, b, t0, t1):
            if (a, b) not in w1_c:
                w1_c[a, b] = sbuf([P, PASS], U32, "w1_c%d%d" % (a, b))
                w1_s[a, b] = sbuf([P, PASS], U8, "w1_s%d%d" % (a, b))
            nc.vector.quantize_mx(
                out=w1_c[a, b][:, P * t0 : P * t1].bitcast(FP8X4),
                scales=w1_s[a, b][:, P * t0 : P * t1],
                in_=rounded_w1(a, b, t0, t1),
            )

        w4_c = {}

        def order_w4(engine, b, buffer):
            w4_c[b] = sbuf([P, 2, 2 * PASS], U8, buffer)
            engine.tensor_copy(
                out=w4_c[b][:].bitcast(I32).rearrange("p a (t g e) -> p a t g e", t=4, e=2),
                in_=w4_raw[b][:].rearrange("p a (g t e) -> p a t g e", t=4, e=2),
            )

        v_w = {}

        def gather_words(a, h, buffer):
            v_w[a, h] = sbuf([P, HALF], U32, buffer)
            entries = slice(HALF * h // PER_COLUMN, HALF * (h + 1) // PER_COLUMN)
            nc.vector.tensor_copy(v_w[a, h][:], tab_w[a][:].indirect(idx[:, entries]))

        a_sb = {}

        def by_lines(tile):
            return tile[:].rearrange("p x y -> p (x y)").rearrange("p (e t i) -> p e t i", t=4, i=4)

        a_acc = {}

        def sums_a(b, u, pair, kind):
            h, first = divmod(UNIT * u, HALF)
            acc = bank(kind, [P, 2, UNIT])
            a_acc[b, u, pair] = acc
            for e in range(2):
                t = 2 * pair + e
                for a in range(2):
                    nc.tensor.matmul_mx(
                        out=acc[:, e, :],
                        lhsT=w1_c[a, b][:, P * t : P * (t + 1)].bitcast(FP8X4),
                        lhsT_scale=w1_s[a, b][:, P * t : P * (t + 1)],
                        rhs=v_w[a, h][:, first : first + UNIT].bitcast(FP8X4),
                        rhs_scale=planes[h][:, a, first : first + UNIT],
                        start=(a == 0),
                        stop=(a == 1),
                    )

        def empty_a(b, u, pair, lines=False):
            for e in range(2):
                t = 2 * pair + e
                if lines:
                    nc.scalar.activation(
                        out=by_lines(a_sb[b, u])[:, :, t, :],
                        in_=a_acc[b, u, pair][:, e, :].rearrange("p (e i) -> p e i", i=4),
                        func=IDENT,
                        bias=bias[:, t, b : b + 1],
                    )
                else:
                    nc.scalar.activation(
                        out=a_sb[b, u][:, t, :], in_=a_acc[b, u, pair][:, e, :], func=IDENT, bias=bias[:, t, b : b + 1]
                    )

        def product_a(b, u, buffer, kinds, lines=False):
            a_sb[b, u] = sbuf([P, 4, UNIT], F32, buffer)
            for pair in range(2):
                sums_a(b, u, pair, kinds[pair])
                empty_a(b, u, pair, lines)

        first_acc = {}

        def first_a(a, t):
            if a == 0:
                first_acc[t] = bank(("a2", "a0", "a1", "y0")[t], [P, HALF])
            nc.tensor.matmul_mx(
                out=first_acc[t][:],
                lhsT=w1_c[a, 0][:, P * t : P * (t + 1)].bitcast(FP8X4),
                lhsT_scale=w1_s[a, 0][:, P * t : P * (t + 1)],
                rhs=v_w[a, 0][:].bitcast(FP8X4),
                rhs_scale=planes[0][:, a, 0:HALF],
                start=(a == 0),
                stop=(a == 1),
            )
            if a == 1 and t < 2:
                nc.scalar.activation(out=a_sb[0, 0][:, t, :], in_=first_acc[t][:, 0:UNIT], func=IDENT, bias=bias[:, t, 0:1])
            if a == 1 and t >= 2:
                nc.vector.tensor_scalar_add(out=a_sb[0, 0][:, t, :], in0=first_acc[t][:, 0:UNIT], scalar1=bias[:, t, 0:1])

        b_acc = {}

        def product_b(b, c, kind="b"):
            acc = bank(kind, [P, 4, CHUNK])
            b_acc[b, c] = acc
            h, first = divmod(CHUNK * c, HALF)
            for a in range(2):
                for t in range(4):
                    nc.tensor.matmul_mx(
                        out=acc[:, t, :],
                        lhsT=w4_c[b][:, a, 2 * P * t : 2 * P * (t + 1)].bitcast(FP4X4),
                        lhsT_scale=planes[b][:, a, HALF + P * t : HALF + P * (t + 1)],
                        rhs=v_w[a, h][:, first : first + CHUNK].bitcast(FP8X4),
                        rhs_scale=planes[h][:, a, first : first + CHUNK],
                        start=(a == 0 and t == 0),
                        stop=(a == 1 and t == 3),
                    )

        chunks = (
            [(0, c) for c in range(6)]
            + [(1, c) for c in range(4)]
        )
        h_bf = {}

        def rounded_h(b, entry, count):
            u = max(key[1] for key in h_bf if key[0] == b and UNIT * key[1] <= entry)
            first = entry - UNIT * u
            return h_bf[b, u][:, 4 * first : 4 * (first + count)]

        def product_h(b, c, lines=False):
            u, in_unit = divmod(CHUNK * c, UNIT)
            if lines:
                a_part = by_lines(a_sb[b, u])[:, in_unit // 4 : (in_unit + CHUNK) // 4]
            else:
                a_part = a_sb[b, u][:, :, in_unit : in_unit + CHUNK].rearrange("p t (e i) -> p e t i", i=4)
            nc.vector.tensor_tensor(
                out=rounded_h(b, CHUNK * c, CHUNK).rearrange("p (e i t) -> p e t i", i=4, t=4),
                in0=b_acc[b, c][:].rearrange("p t (e i) -> p e t i", i=4),
                in1=a_part,
                op=MULT,
            )
            if (b, c) in chunks[: -BANKS["b"]]:
                product_b(*chunks[chunks.index((b, c)) + BANKS["b"]])

        b_sb = {}

        def product_b_out(b, u, buffer, kinds="aa"):
            b_sb[b, u] = sbuf([P, 4, UNIT], F32, buffer) if isinstance(buffer, str) else buffer
            h, first = divmod(UNIT * u, HALF)
            for pair in range(2):
                acc = bank(kinds[pair], [P, 2, UNIT])
                for e in range(2):
                    t = 2 * pair + e
                    for a in range(2):
                        nc.tensor.matmul_mx(
                            out=acc[:, e, :],
                            lhsT=w4_c[b][:, a, 2 * P * t : 2 * P * (t + 1)].bitcast(FP4X4),
                            lhsT_scale=planes[b][:, a, HALF + P * t : HALF + P * (t + 1)],
                            rhs=v_w[a, h][:, first : first + UNIT].bitcast(FP8X4),
                            rhs_scale=planes[h][:, a, first : first + UNIT],
                            start=(a == 0),
                            stop=(a == 1),
                        )
                nc.scalar.copy(
                    out=by_lines(b_sb[b, u])[:, :, 2 * pair : 2 * pair + 2, :],
                    in_=acc[:].rearrange("p t (e i) -> p e t i", i=4),
                )

        def product_h_gpsimd(b, entry, count, b_lines):
            u, in_unit = divmod(entry, UNIT)
            nc.gpsimd.tensor_tensor(
                out=rounded_h(b, entry, count).rearrange("p (e i t) -> p e t i", i=4, t=4),
                in0=b_lines,
                in1=by_lines(a_sb[b, u])[:, in_unit // 4 : (in_unit + count) // 4],
                op=MULT,
            )

        h_c = {}
        h_s = {}

        def quant_h(b, u0, u1, buffer=None):
            h, first = divmod(UNIT * u0, HALF)
            if (b, h) not in h_c:
                h_c[b, h] = sbuf([P, HALF], U32, buffer or "h_c%d%d" % (b, h))
                h_s[b, h] = sbuf([P, HALF], U8, "h_s%d%d" % (b, h))
            last = first + UNIT * (u1 - u0)
            nc.vector.quantize_mx(
                out=h_c[b, h][:, first:last].bitcast(FP8X4),
                scales=h_s[b, h][:, first:last],
                in_=rounded_h(b, UNIT * u0, UNIT * (u1 - u0)),
            )

        w3_bf = {}
        w3_c = {}
        w3_s = {}

        def cast_w3_gpsimd(n, b):
            nc.gpsimd.tensor_copy(
                out=w3_bf[n][:, 4 * P * b : 4 * P * (b + 1)].rearrange("p (c t) -> p c t", t=4),
                in_=w3_raw[b][:, :, P * n : P * (n + 1)].rearrange("p t c -> p c t"),
            )

        def cast_w3(n, b):
            nc.scalar.copy(
                out=w3_bf[n][:, 4 * P * b : 4 * P * (b + 1)].rearrange("p (e i t) -> p e t i", i=4, t=4),
                in_=w3_raw[b][:, :, P * n : P * (n + 1)].rearrange("p t (e i) -> p e t i", i=4),
            )

        def quant_w3(n, codes=None):
            w3_c[n] = codes or sbuf([P, 2 * P], U32, "w3_c%d" % n)
            w3_s[n] = sbuf([P, 2 * P], U8, "w3_s%d" % n)
            nc.vector.quantize_mx(out=w3_c[n][:].bitcast(FP8X4), scales=w3_s[n][:], in_=w3_bf[n][:])

        y_sb = {}

        def product_y(n, u0, u1, kind, plain=None, weighted=None):
            h, first = divmod(UNIT * u0, HALF)
            width = UNIT * (u1 - u0)
            acc = bank(kind, [P, width])
            for b in (0, 1) if h == 0 else (1, 0):
                nc.tensor.matmul_mx(
                    out=acc[:],
                    lhsT=w3_c[n][:, P * b : P * (b + 1)].bitcast(FP8X4),
                    lhsT_scale=w3_s[n][:, P * b : P * (b + 1)],
                    rhs=h_c[b, h][:, first : first + width].bitcast(FP8X4),
                    rhs_scale=h_s[b, h][:, first : first + width],
                    start=(b == h),
                    stop=(b != h),
                )
            if weighted is None:
                y_sb[n, u0] = plain
                nc.scalar.activation(out=y_sb[n, u0][:], in_=acc[:], func=COPY, scale=gain[:, n : n + 1])
            else:
                y_sb[n, u0] = weighted
                nc.vector.scalar_tensor_tensor(
                    out=weighted[:],
                    in0=acc[:],
                    scalar=gain[:, n : n + 1],
                    in1=wgo_sb[:, UNIT * u0 : UNIT * u1],
                    op0=MULT,
                    op1=MULT,
                )

        page = {}

        def scatter(n, u0, u1):
            first, last = UNIT * u0, UNIT * u1
            nc.vector.tensor_tensor(
                page[n][:].indirect(idx2[:, first // PER_COLUMN : last // PER_COLUMN]),
                y_sb[n, u0][:],
                wgo_sb[:, first:last],
                MULT,
            )

        def scatter_copy(n, u0, u1):
            first, last = UNIT * u0, UNIT * u1
            nc.vector.tensor_copy(page[n][:].indirect(idx2[:, first // PER_COLUMN : last // PER_COLUMN]), y_sb[n, u0][:])

        sums = {}

        def open_sum(n):
            for k in range(2):
                sums[n, k] = bank((("b1", "b2"), ("b0", "b3"))[n][k], [P, 4, P])
                for c in range(4):
                    cols = slice(HALF * k + P * c, HALF * k + P * (c + 1))
                    nc.tensor.matmul(
                        sums[n, k][:, c, :], x0_sb[n][:, cols], ident[:], start=(c == 0), stop=False, is_transpose=True
                    )

        def finish_on_tensor(n):
            turned_sum = {}
            for k in range(2):
                acc = sums[n, k]
                for c in range(4):
                    cols = slice(HALF * k + P * c, HALF * k + P * (c + 1))
                    nc.tensor.matmul(acc[:, c, :], page[n][:, cols], ident[:], start=False, stop=(c == 3), is_transpose=True)
                turned_sum[k] = sbuf([P, 4, P], F32, "turned%d" % k)
                nc.scalar.copy(out=turned_sum[k][:], in_=acc[:])
            for k in range(2):
                acc = bank((("a0", "a1"), ("b1", "b2"))[n][k], [P, 4, P])
                for c in range(4):
                    nc.tensor.transpose(acc[:, c, :], turned_sum[k][:, c, :], ident[:])
                result = sbuf([P, HALF], F32, "result%d%d" % (n, k))
                nc.scalar.copy(out=result[:], in_=acc[:].rearrange("p c m -> p (c m)"))
                nc.scalar.dma_start(out=out[P * n : P * (n + 1), HALF * k : HALF * (k + 1)], in_=result[:])

        def finish_on_vector(n):
            width = S // LAST_PIECES
            for k in range(LAST_PIECES):
                cols = slice(width * k, width * (k + 1))
                nc.vector.tensor_tensor(out=x0_sb[n][:, cols], in0=page[n][:, cols], in1=x0_sb[n][:, cols], op=ADD)
                nc.sync.dma_start(out=out[P * n : P * (n + 1), cols], in_=x0_sb[n][:, cols])

        v_rows = {}

        def gather_scales(h):
            v_rows[h] = sbuf([P, HALF], U8, "v_rows%d" % h)
            entries = slice(HALF * h // PER_COLUMN, HALF * (h + 1) // PER_COLUMN)
            nc.vector.tensor_copy(v_rows[h][:], tab_s[:].indirect(idx[:, entries]))

        def deal_scales(x, buffer):
            rows = sbuf([SCALE_ROWS, (HALF + PASS) // 4], I32, buffer)
            nc.vector.tensor_copy(
                out=rows[:, HALF // 4 :].rearrange("p (t g) -> p t g", t=4),
                in_=w4_s_rows[:, P * x : P * (x + 1)].rearrange("p (g t) -> p t g", t=4),
            )
            nc.vector.tensor_copy(out=rows[:, 0 : HALF // 4], in_=v_rows[x][0:SCALE_ROWS, :].bitcast(I32))
            for q in range(4):
                nc.sync.dma_start(out=planes[x][32 * q : 32 * q + 4, :, :].bitcast(I32), in_=rows[8 * q : 8 * q + 8, :])

        gather_scales(0)
        deal_scales(0, "rows0")
        load_w1(0, 0, "v_rows0")
        gather_scales(1)
        gather_words(0, 0, "v_w00")
        gather_words(0, 1, "v_w01")
        load_w1(1, 0, "tab_s")
        order_w4(nc.vector, 0, "w4_c0")
        idx2 = keep.tile([P, S // PER_COLUMN], U16, name="idx2")
        nc.sync.dma_start(idx2[:], offs2)
        load_w4(1, "rows0")
        deal_scales(1, "w4_raw0")
        load_w1(0, 1, "v_rows1")
        gather_words(1, 0, "v_w10")
        gather_words(1, 1, "v_w11")
        load_w1(1, 1, "tab_w1")
        for chunk in chunks[: BANKS["b"]]:
            product_b(*chunk)

        cast_w1(nc.scalar.copy, 0, 0, 2, 4)
        cast_w1(nc.vector.tensor_copy, 0, 0, 0, 2)
        load_w3(0, "v_rows0")
        quant_w1(0, 0, 0, 2)
        quant_w1(0, 0, 2, 4)
        load_w3(1, "w1_bf001")
        for t in range(4):
            first_a(0, t)
        cast_w1(nc.vector.tensor_copy, 1, 0, 0, 1)
        cast_w1(nc.scalar.copy, 1, 0, 2, 3)
        cast_w1(nc.vector.tensor_copy, 1, 0, 1, 2)
        cast_w1(nc.scalar.copy, 1, 0, 3, 4)
        quant_w1(1, 0, 0, 1)
        wgo_sb = sbuf([P, S], F32, "tab_s")
        nc.sync.dma_start(out=wgo_sb[:], in_=wgo)
        a_sb[0, 0] = sbuf([P, 4, UNIT], F32, "a0")
        first_a(1, 0)
        for t in range(1, 4):
            quant_w1(1, 0, t, t + 1)
            first_a(1, t)
        load_x0(0, "w1_bf100")

        a_sb[0, 1] = sbuf([P, 4, UNIT], F32, "a1")
        for t in range(4):
            nc.scalar.activation(out=a_sb[0, 1][:, t, :], in_=first_acc[t][:, UNIT:HALF], func=IDENT, bias=bias[:, t, 0:1])
        sums_a(0, 2, 0, "a2")
        sums_a(0, 2, 1, "a0")
        order_w4(nc.gpsimd, 1, "w1_bf101")
        h_bf[0, 0] = over([P, 4 * HALF], BF16, "h_bf00", 5120)
        product_h(0, 0)
        product_h(0, 1)
        cast_w1(nc.scalar.copy, 0, 1, 0, 2)
        cast_w1_gpsimd(0, 1, 2, 4)
        load_x0(1, "v_rows1")
        product_h(0, 2)
        product_h(0, 3)

        cast_w1(nc.scalar.copy, 1, 1, 2, 4)
        cast_w1(nc.vector.tensor_copy, 1, 1, 0, 2)
        a_sb[0, 2] = sbuf([P, 4, UNIT], F32, "tab_w1")
        for pair in range(2):
            empty_a(0, 2, pair)
        quant_w1(0, 1, 0, 2)
        quant_w1(1, 1, 0, 2)
        quant_w1(0, 1, 2, 4)
        load_x0(2, "w1_bf011")
        quant_w1(1, 1, 2, 4)
        product_a(1, 0, "a3", ("a1", "y0"))
        product_a(1, 1, "a4", ("a2", "a0"))
        quant_h(0, 0, 2, "w1_bf111")
        h_bf[0, 2] = over([P, 4 * UNIT], BF16, "h_bf02", 8704)
        product_h(0, 4)
        product_h(0, 5)
        w3_two = over([P, 2, 2 * PASS], BF16, "w3_two", 2048)
        w3_bf[0] = w3_two[:, 0]
        w3_bf[1] = w3_two[:, 1]
        for b in range(2):
            nc.gpsimd.tensor_copy(
                out=w3_two[:, :, PASS * b : PASS * (b + 1)].rearrange("p n (c t) -> p n c t", t=4),
                in_=w3_raw[b][:, :, 0 : 2 * P].rearrange("p t (n c) -> p n c t", n=2),
            )

        h_bf[1, 0] = sbuf([P, 4 * HALF], BF16, "h_bf10")
        for c in range(4):
            product_h(1, c)
        product_a(1, 2, "a5", ("b3", "b0"), lines=True)
        product_b_out(1, 2, "b0", ("b1", "b2"))
        quant_w3(0)
        quant_h(1, 0, 2)
        quant_h(0, 2, 3, "h_bf10")
        quant_w3(1)

        for n in range(2):
            page[n] = sbuf([P, S], F32, "page%d" % n)
        product_y(0, 0, 2, "y0", weighted=sbuf([P, HALF], F32, "z0"))
        product_y(1, 0, 2, "a1", weighted=sbuf([P, HALF], F32, "z1"))
        scatter_copy(0, 0, 2)
        scatter_copy(1, 0, 2)
        h_bf[1, 2] = over([P, 4 * HALF], BF16, "h_bf12", 4672)
        product_h_gpsimd(1, 2 * UNIT, UNIT, by_lines(b_sb[1, 2]))
        product_a(1, 3, "a6", ("b3", "b0"), lines=True)
        product_b_out(1, 3, "b1", ("b1", "b2"))
        w3_bf[2] = sbuf([P, 2 * PASS], BF16, "w1_bf101")
        for b in range(2):
            cast_w3(2, b)
        product_a(0, 3, "a2", ("b3", "b0"))
        product_b(0, 6, "y0")
        product_b(0, 7, "a1")
        product_h_gpsimd(1, 3 * UNIT, UNIT, by_lines(b_sb[1, 3]))
        quant_w3(2, sbuf([P, 2 * P], U32, "z0"))
        h_bf[0, 3] = sbuf([P, 4 * UNIT], BF16, "h_bf03")
        product_h(0, 6)
        product_h(0, 7)
        open_sum(0)
        quant_h(1, 2, 4)
        quant_h(0, 3, 4)
        product_y(2, 0, 1, "b3", plain=sbuf([P, UNIT], F32, "y20"))
        page[2] = sbuf([P, S], F32, "a2")
        scatter(2, 0, 1)
        product_y(0, 2, 4, "a2", plain=sbuf([P, HALF], F32, "y02"))
        product_y(1, 2, 4, "a2", plain=sbuf([P, HALF], F32, "y12"))
        product_y(2, 2, 4, "a2", plain=sbuf([P, HALF], F32, "y6"))
        open_sum(1)
        scatter(0, 2, 4)
        product_y(2, 1, 2, "y0", plain=sbuf([P, UNIT], F32, "y02"))
        finish_on_tensor(0)
        scatter(1, 2, 4)
        finish_on_tensor(1)
        scatter(2, 1, 2)
        scatter(2, 2, 4)
        finish_on_vector(2)
